import numpy as np
import ml_dtypes


def mxq(x, axis, fmt="e4m3"):
    dtype, down = {"e4m3": (ml_dtypes.float8_e4m3fn, 7), "e5m2": (ml_dtypes.float8_e5m2, 14)}[fmt]
    v = np.moveaxis(np.asarray(x, np.float32).astype(ml_dtypes.bfloat16).astype(np.float64), axis, -1)
    blocks = v.reshape(v.shape[:-1] + (-1, 32))
    amax = np.abs(blocks).max(-1, keepdims=True)
    byte = np.maximum(np.where(amax > 0, np.frexp(amax)[1] - 1 + 127, 0) - down, 1)
    scale = np.exp2(byte - 127.0)
    codes = (blocks / scale).astype(np.float32).astype(dtype).astype(np.float64)
    return np.moveaxis((codes * scale).reshape(v.shape), -1, axis)


WIDE = False


def mx_kscale(k):
    if not WIDE:
        return np.ones(k)
    levels = np.array([10, -10, 5, -5, 0])
    if k % 512:
        return np.exp2(np.random.permutation(np.resize(levels, k // 32))).repeat(32)
    a = np.empty((k // 512, 16))
    for p in range(k // 512):
        a[p, :8] = np.random.permutation(np.resize(levels, 8))
        for g in range(8):
            far = levels[np.abs(levels - a[p, g]) >= 10]
            a[p, g + 8] = far[np.random.randint(len(far))]
    return np.exp2(a.ravel()).repeat(32)


def f64(x):
    return np.asarray(x).astype(np.float64)


def striped(idx):
    return np.tile(idx.reshape(-1, 16).T, (8, 1)).astype(np.uint16)


def unstriped(offs):
    return offs[:16].T.reshape(-1).astype(np.int64)


E2M1 = np.array([0.0, 0.5, 1.0, 1.5, 2.0, 3.0, 4.0, 6.0, -0.0, -0.5, -1.0, -1.5, -2.0, -3.0, -4.0, -6.0])


def pack_weight(w, fmt):
    k, n = w.shape
    w = f64(np.asarray(w, np.float32).astype(ml_dtypes.bfloat16)).reshape(k // 32, 32, n)
    amax = np.abs(w).max(1)
    if fmt == "e4m3":
        byte = np.frexp(amax)[1] - 1 + 127 - 7
    else:
        mant, ex = np.frexp(amax / 6.0)
        byte = np.where(mant > 0.5, ex, ex - 1) + 127
    byte = np.clip(np.where(amax > 0, byte, 1), 1, 254)
    scaled = (w * np.exp2(127.0 - byte)[:, None, :]).reshape(k, n).astype(np.float32)
    by_word = np.ascontiguousarray(scaled.reshape(k // 512, 128, 4, n).transpose(0, 1, 3, 2))
    if fmt == "e4m3":
        words = by_word.astype(ml_dtypes.float8_e4m3fn).view(np.uint8)
    else:
        c = by_word.astype(ml_dtypes.float4_e2m1fn).view(np.uint8) & 0xF
        words = (c[..., 0::2] | (c[..., 1::2] << 4)).reshape(k // 512, 128, 2 * n)
    return np.ascontiguousarray(words), np.ascontiguousarray(byte.astype(np.uint8).reshape(k // 512, 16, n))


def unpack_weight(words, scales, fmt):
    g, _, n = scales.shape
    words = np.ascontiguousarray(words).reshape(g, 128, n, -1)
    if fmt == "e4m3":
        vals = words.view(ml_dtypes.float8_e4m3fn).astype(np.float64)
    else:
        nib = np.empty((g, 128, n, 4), np.uint8)
        nib[..., 0::2] = words & 0xF
        nib[..., 1::2] = words >> 4
        vals = E2M1[nib]
    vals = vals * np.repeat(np.exp2(scales.astype(np.float64) - 127.0), 8, axis=1)[..., None]
    return vals.transpose(0, 1, 3, 2).reshape(g * 512, n)


def gelu(v):
    return 0.5 * v * (1.0 + np.tanh(np.sqrt(2.0 / np.pi) * (v + 0.044715 * v**3)))


T, S, K, H, N = 2048, 1024, 1024, 1024, 384

def setup_inputs():
    n = np.random.standard_normal
    s = mx_kscale(K)[:, None]
    u = mx_kscale(H)[:, None]
    tab_words, tab_scales = pack_weight(n((K, T)) * s, "e4m3")
    w1 = (n((K, H)) / np.sqrt(K) / s * u.T).astype(np.float32)
    w4_words, w4_scales = pack_weight(n((K, H)) / np.sqrt(K) / s * u.T, "e2m1")
    b1 = (0.5 * n(H) * u[:, 0]).astype(np.float32)
    b4 = (0.5 * n(H) * u[:, 0]).astype(np.float32)
    w2 = (n((H, N)) / np.sqrt(H) / u).astype(np.float32)
    b2 = (0.5 * n(N)).astype(np.float32)
    gT = n((N, T)).astype(np.float32)
    offs = striped(np.random.permutation(T)[:S])
    return {"tab_words": tab_words, "tab_scales": tab_scales, "offs": offs,
            "w1": w1, "b1": b1, "w4_words": w4_words, "w4_scales": w4_scales,
            "b4": b4, "w2": w2, "b2": b2, "gT": gT}

def reference(tab_words, tab_scales, offs, w1, b1, w4_words, w4_scales, b4, w2, b2, gT):
    v = unpack_weight(tab_words, tab_scales, "e4m3")[:, unstriped(offs)]
    w4 = unpack_weight(w4_words, w4_scales, "e2m1")
    a = (mxq(f64(w1), 0, "e4m3").T @ v) + f64(b1)[:, None]
    b = (w4.T @ v) + f64(b4)[:, None]
    h = np.maximum(a, b)
    y = mxq(f64(w2), 0, "e4m3").T @ mxq(h, 0, "e4m3")
    g = f64(gT)[:, unstriped(offs)]
    new = np.minimum(g, y + f64(b2)[:, None])
    out = f64(gT).copy()
    out[:, unstriped(offs)] = new
    return out

@@ -1,0 +1,279 @@
+from contextlib import ExitStack
+
+import concourse.mybir as mybir
+from concourse.masks import make_identity
+
+T, S, K, H, N = 2048, 1024, 1024, 1024, 384
+FLOPS = 2 * S * (2 * K * H + H * N)
+
+F32 = mybir.dt.float32
+BF16 = mybir.dt.bfloat16
+I32 = mybir.dt.int32
+U32 = mybir.dt.uint32
+U16 = mybir.dt.uint16
+U8 = mybir.dt.uint8
+FP8X4 = mybir.dt.float8_e4m3fn_x4
+FP4X4 = mybir.dt.float4_e2m1fn_x4
+ALU = mybir.AluOpType
+ACT = mybir.ActivationFunctionType
+
+P = 128
+KP = 512
+HALF = 512
+
+
+def tile_list_marathon_split_caps_kernel(tc, tab_words, tab_scales, offs, w1, b1, w4_words, w4_scales, b4, w2, b2, gT, out):
+    nc = tc.nc
+    with ExitStack() as ctx:
+        keep = ctx.enter_context(tc.tile_pool(name="keep", bufs=1))
+        psum = ctx.enter_context(tc.psum_pool(name="psum", bufs=1))
+
+        def sb(name, shape, dtype):
+            return keep.tile(shape, dtype, name=name, align_bytes=64)
+
+        pairs = [(a, g) for g in range(2) for a in range(2)]
+        offsets = keep.tile([P, S // 16], U16, name="offsets")
+        tsc = sb("tsc", [P, T], U8)
+        brows = sb("brows", [P, 2 * P], F32)
+        w4s_raw = sb("w4s_raw", [P, 2 * H], U8)
+        vs = [sb(f"vs{a}", [P, S], U8) for a in range(2)]
+        ident = sb("ident", [P, P], F32)
+        tw = [sb(f"tw{a}", [P, T], U32) for a in range(2)]
+        w1_raw = {(a, g): sb(f"w1_raw{a}{g}", [P, 4, KP], F32) for a, g in pairs}
+        w4_raw = [sb(f"w4_raw{g}", [P, 2 * 2 * KP], U8) for g in range(2)]
+        w2_raw = [sb(f"w2_raw{g}", [P, 4, N], F32) for g in range(2)]
+        page = [sb(f"page{m}", [P, T], F32) for m in range(3)]
+        banks = [psum.tile([P, HALF], F32, name=f"bank{b}") for b in range(8)]
+
+        nc.gpsimd.memset(tsc[:].bitcast(I32), 0)
+        nc.gpsimd.memset(brows[:], 0.0)
+        nc.gpsimd.memset(w4s_raw[:].bitcast(I32), 0)
+        make_identity(nc, ident[:])
+        nc.gpsimd.memset(vs[1][:].bitcast(I32), 0)
+
+        def load_tw(a):
+            nc.sync.dma_start(tw[a][:].bitcast(I32), tab_words[a].rearrange("p t i -> p (t i)").bitcast(I32))
+
+        def load_w1(a, g):
+            nc.sync.dma_start(
+                w1_raw[a, g][:], w1[KP * a : KP * (a + 1), KP * g : KP * (g + 1)].rearrange("(p j) c -> p j c", j=4)
+            )
+
+        def load_w4(g):
+            nc.sync.dma_start(
+                w4_raw[g][:].bitcast(I32).rearrange("p (a c) -> p a c", a=2),
+                w4_words[:, :, 2 * KP * g : 2 * KP * (g + 1)].bitcast(I32).rearrange("a p c -> p a c"),
+            )
+
+        def load_page(m):
+            nc.sync.dma_start(page[m][:], gT[P * m : P * (m + 1), :])
+
+        def load_w2(g):
+            rows = w2[KP * g : KP * (g + 1), :].rearrange("(q t i) n -> t q i n", t=4, i=4)
+            for t in range(4):
+                nc.sync.dma_start(w2_raw[g][:, t, :], rows[t])
+
+        nc.sync.dma_start(offsets[:], offs)
+        load_tw(0)
+        for q in range(4):
+            nc.scalar.dma_start(tsc[32 * q : 32 * q + 8, :].bitcast(I32), tab_scales[:, 4 * q : 4 * q + 4, :].bitcast(I32))
+        for v, vec in enumerate((b1, b4)):
+            nc.scalar.dma_start(brows[4 * v : 4 * v + 4, :], vec.rearrange("(q t i) -> t q i", t=4, i=4))
+        nc.scalar.dma_start(brows[8:11, 0:P], b2.rearrange("(m p) -> m p", p=P))
+        load_w1(0, 0)
+        load_tw(1)
+        for q in range(4):
+            nc.sync.dma_start(
+                w4s_raw[32 * q : 32 * q + 4, :].bitcast(I32).rearrange("r (a c) -> r a c", a=2),
+                w4_scales[:, 4 * q : 4 * q + 4, :].bitcast(I32).rearrange("a r c -> r a c"),
+            )
+        load_w1(1, 0)
+        load_w4(0)
+        load_page(0)
+        load_w1(0, 1)
+        load_w1(1, 1)
+        load_w4(1)
+        load_w2(0)
+        load_w2(1)
+        load_page(1)
+        load_page(2)
+
+        for g in range(2):
+            nc.tensor.transpose(banks[6][:, P * g : P * (g + 1)], brows[:, P * g : P * (g + 1)], ident[:])
+        bias = sb("bias", [P, 2, 16], F32)
+        nc.scalar.copy(bias[:], banks[6][:, 0 : 2 * P].rearrange("p (g c) -> p g c", g=2)[:, :, 0:16])
+
+        nc.vector.tensor_copy(vs[0][:], tsc[:].indirect(offsets[:]))
+        nc.gpsimd.dma_start(vs[1][0:124, :].bitcast(I32), vs[0][4:128, :].bitcast(I32))
+
+        def half_list(s):
+            return offsets[:, 32 * s : 32 * (s + 1)]
+
+        vw = {(a, s): sb(f"vw{a}{s}", [P, HALF], U32) for a in range(2) for s in range(2)}
+        w1_bf = {(a, g): sb(f"w1_bf{a}{g}", [P, 4 * KP], BF16) for a, g in pairs}
+        w1_codes = {(a, g): sb(f"w1_codes{a}{g}", [P, KP], U32) for a, g in pairs}
+        w1_sc = {(a, g): sb(f"w1_sc{a}{g}", [P, KP], U8) for a, g in pairs}
+
+        def gather_words(a, s):
+            nc.vector.tensor_copy(vw[a, s][:], tw[a][:].indirect(half_list(s)))
+
+        def cast_w1(a, g, u, copy):
+            dst = w1_bf[a, g][:].rearrange("p (t q i j) -> p t q j i", t=4, i=4, j=4)
+            src = w1_raw[a, g][:].rearrange("p j (q t i) -> p t q j i", t=4, i=4)
+            copy(dst[:, 2 * u : 2 * u + 2], src[:, 2 * u : 2 * u + 2])
+
+        def quant_w1(a, g, u):
+            cols = slice(256 * u, 256 * (u + 1))
+            nc.vector.quantize_mx(
+                w1_codes[a, g][:, cols].bitcast(FP8X4), w1_sc[a, g][:, cols], w1_bf[a, g][:, 1024 * u : 1024 * (u + 1)]
+            )
+
+        def by_activation(dst, src):
+            for t in range(2):
+                nc.scalar.activation(dst[:, t], src[:, t], ACT.Copy)
+
+        w4c = [sb(f"w4c{g}", [P, 2 * 2 * KP], U8) for g in range(2)]
+        w4s = sb("w4s", [P, 2 * H], U8)
+
+        def order_w4_scales():
+            nc.vector.tensor_copy(
+                w4s[:].bitcast(I32).rearrange("p (u t q) -> p u t q", t=4, q=32),
+                w4s_raw[:].bitcast(I32).rearrange("p (u q t) -> p u t q", t=4, q=32),
+            )
+
+        def order_w4(g):
+            nc.vector.tensor_copy(
+                w4c[g][:].bitcast(I32).rearrange("p (a t q e) -> p a t q e", t=4, q=32, e=2),
+                w4_raw[g][:].bitcast(I32).rearrange("p (a q t e) -> p a t q e", t=4, q=32, e=2),
+            )
+
+        picked = [sb(f"picked{m}", [P, S], F32) for m in range(3)]
+
+        def gather_page(m):
+            nc.vector.tensor_copy(picked[m][:], page[m][:].indirect(offsets[:]))
+
+        gs_pairs = [(0, 0), (1, 0), (0, 1), (1, 1)]
+        h_planes = {(g, s): sb(f"h_planes{g}{s}", [P, 4, HALF], BF16) for g, s in gs_pairs}
+        woven = [sb(f"woven{i}", [P, 4 * HALF], BF16) for i in range(2)]
+        h_bf = {(0, 0): woven[0], (1, 0): woven[1], (0, 1): woven[1], (1, 1): woven[0]}
+        h_codes = {(g, s): sb(f"h_codes{g}{s}", [P, HALF], U32) for g, s in gs_pairs}
+        h_sc = {(g, s): sb(f"h_sc{g}{s}", [P, HALF], U8) for g, s in gs_pairs}
+        a_sb = [sb(f"a_sb{i}", [P, HALF], F32) for i in range(3)]
+        units = []
+
+        def unit(g, s, t):
+            cols = slice(HALF * s, HALF * (s + 1))
+            slot = len(units) % 3
+            units.append((g, s, t))
+            pa, pb = banks[2 * slot], banks[2 * slot + 1]
+            for a in range(2):
+                nc.tensor.matmul_mx(
+                    pa[:], w1_codes[a, g][:, P * t : P * (t + 1)].bitcast(FP8X4), w1_sc[a, g][:, P * t : P * (t + 1)],
+                    vw[a, s][:].bitcast(FP8X4), vs[a][:, cols], start=(a == 0), stop=(a == 1),
+                )
+            for a in range(2):
+                c0 = KP * a + P * t
+                s0 = H * a + KP * g + P * t
+                nc.tensor.matmul_mx(
+                    pb[:], w4c[g][:, 2 * c0 : 2 * (c0 + P)].bitcast(FP4X4), w4s[:, s0 : s0 + P],
+                    vw[a, s][:].bitcast(FP8X4), vs[a][:, cols], start=(a == 0), stop=(a == 1),
+                )
+            nc.scalar.activation(a_sb[slot][:], pa[:], ACT.Identity, bias=bias[:, g, t : t + 1])
+            nc.vector.scalar_tensor_tensor(
+                h_planes[g, s][:, t, :], pb[:], bias[:, g, 4 + t : 5 + t], a_sb[slot][:], ALU.add, ALU.max
+            )
+
+        def weave_h(g, s):
+            nc.scalar.copy(
+                h_bf[g, s][:].rearrange("p (c i t) -> p c t i", i=4, t=4),
+                h_planes[g, s][:].rearrange("p t (c i) -> p c t i", i=4),
+            )
+
+        def quant_h(g, s):
+            nc.vector.quantize_mx(h_codes[g, s][:].bitcast(FP8X4), h_sc[g, s][:], h_bf[g, s][:])
+
+        w2_bf = sb("w2_bf", [P, 2 * 4 * N], BF16)
+        w2_codes = sb("w2_codes", [P, 2 * N], U32)
+        w2_sc = sb("w2_sc", [P, 2 * N], U8)
+
+        def cast_w2(g):
+            nc.scalar.copy(
+                w2_bf[:, 4 * N * g : 4 * N * (g + 1)].rearrange("p (c i t) -> p c t i", i=4, t=4),
+                w2_raw[g][:].rearrange("p t (c i) -> p c t i", i=4),
+            )
+
+        def quant_w2():
+            for lo, hi in ((0, 512), (512, 768)):
+                nc.vector.quantize_mx(w2_codes[:, lo:hi].bitcast(FP8X4), w2_sc[:, lo:hi], w2_bf[:, 4 * lo : 4 * hi])
+
+        capped = {(m, 1): sb(f"capped{m}", [P, HALF], F32)[:] for m in range(3)}
+        capped[0, 0] = capped[2, 1]
+        capped[1, 0] = capped[0, 1]
+        capped[2, 0] = woven[0][:].bitcast(F32)[:, 0:HALF]
+        y_bank = {(0, 0): 7, (1, 0): 6, (2, 0): 7, (0, 1): 2, (1, 1): 3, (2, 1): 4}
+
+        def second_stage(m, s):
+            py = banks[y_bank[m, s]]
+            for g in range(2):
+                c0 = N * g + P * m
+                nc.tensor.matmul_mx(
+                    py[:], w2_codes[:, c0 : c0 + P].bitcast(FP8X4), w2_sc[:, c0 : c0 + P],
+                    h_codes[g, s][:].bitcast(FP8X4), h_sc[g, s][:], start=(g == 0), stop=(g == 1),
+                )
+            nc.vector.scalar_tensor_tensor(
+                capped[m, s], py[:], bias[:, 0, 8 + m : 9 + m], picked[m][:, HALF * s : HALF * (s + 1)], ALU.add, ALU.min
+            )
+
+        def scatter(m, s):
+            nc.vector.tensor_copy(page[m][:].indirect(half_list(s)), capped[m, s])
+
+        gather_words(0, 0)
+        gather_words(0, 1)
+        cast_w1(0, 0, 0, by_activation)
+        cast_w1(0, 0, 1, nc.vector.tensor_copy)
+        quant_w1(0, 0, 0)
+        quant_w1(0, 0, 1)
+        gather_words(1, 0)
+        order_w4_scales()
+        cast_w1(1, 0, 0, nc.scalar.copy)
+        cast_w1(1, 0, 1, nc.vector.tensor_copy)
+        quant_w1(1, 0, 0)
+        order_w4(0)
+        quant_w1(1, 0, 1)
+        gather_words(1, 1)
+        for t in range(4):
+            unit(0, 0, t)
+        for a in range(2):
+            for u in range(2):
+                cast_w1(a, 1, u, nc.scalar.copy)
+                quant_w1(a, 1, u)
+        order_w4(1)
+        gather_page(0)
+        for g, s in ((0, 1), (1, 0)):
+            for t in range(4):
+                unit(g, s, t)
+        weave_h(0, 0)
+        quant_h(0, 0)
+        weave_h(1, 0)
+        quant_h(1, 0)
+        cast_w2(0)
+        cast_w2(1)
+        quant_w2()
+        for t in range(4):
+            unit(1, 1, t)
+        gather_page(1)
+        gather_page(2)
+        for m in range(2):
+            second_stage(m, 0)
+        for m in range(2):
+            scatter(m, 0)
+        for g in range(2):
+            weave_h(g, 1)
+            quant_h(g, 1)
+        second_stage(2, 0)
+        scatter(2, 0)
+        for m in range(3):
+            second_stage(m, 1)
+        for m in range(3):
+            scatter(m, 1)
+            nc.sync.dma_start(out[P * m : P * (m + 1), :], page[m][:])

@@ -36,7 +36,9 @@ def tile_list_marathon_split_caps_kernel(tc, tab_words, tab_scales, offs, w1, b1
         tsc = sb("tsc", [P, T], U8)
         brows = sb("brows", [P, 2 * P], F32)
         w4s_raw = sb("w4s_raw", [P, 2 * H], U8)
-        vs = [sb(f"vs{a}", [P, S], U8) for a in range(2)]
+        vs_both = sb("vs_both", [P, 2 * S], U8)
+        vs = [vs_both[:, S * a : S * (a + 1)] for a in range(2)]
+        vs_raw = sb("vs_raw", [P, S], U8)
         ident = sb("ident", [P, P], F32)
         tw = [sb(f"tw{a}", [P, T], U32) for a in range(2)]
         w1_raw = {(a, g): sb(f"w1_raw{a}{g}", [P, 4, KP], F32) for a, g in pairs}
@@ -45,11 +47,21 @@ def tile_list_marathon_split_caps_kernel(tc, tab_words, tab_scales, offs, w1, b1
         page = [sb(f"page{m}", [P, T], F32) for m in range(3)]
         banks = [psum.tile([P, HALF], F32, name=f"bank{b}") for b in range(8)]
 
-        nc.gpsimd.memset(tsc[:].bitcast(I32), 0)
-        nc.gpsimd.memset(brows[:], 0.0)
+        for q in range(4):
+            nc.vector.memset(tsc[32 * q : 32 * q + 24, :].bitcast(I32), 0)
         nc.gpsimd.memset(w4s_raw[:].bitcast(I32), 0)
+        for q in range(4):
+            nc.gpsimd.dma_start(
+                w4s_raw[32 * q : 32 * q + 4, :].bitcast(I32).rearrange("r (a c) -> r a c", a=2),
+                w4_scales[:, 4 * q : 4 * q + 4, :].bitcast(I32).rearrange("a r c -> r a c"),
+            )
+        nc.gpsimd.memset(vs_both[96:128, :].bitcast(I32), 0)
+        nc.gpsimd.memset(brows[0:96, :], 0.0)
+        nc.gpsimd.memset(brows[96:120, :], 0.0)
         make_identity(nc, ident[:])
-        nc.gpsimd.memset(vs[1][:].bitcast(I32), 0)
+        b2c = sb("b2c", [P, 3], F32)
+        with nc.allow_non_contiguous_dma(reason="one value to a partition"):
+            nc.gpsimd.dma_start(b2c[:], b2.rearrange("(m p) -> p m", p=P))
 
         def load_tw(a):
             nc.sync.dma_start(tw[a][:].bitcast(I32), tab_words[a].rearrange("p t i -> p (t i)").bitcast(I32))
@@ -74,37 +86,34 @@ def tile_list_marathon_split_caps_kernel(tc, tab_words, tab_scales, offs, w1, b1
                 nc.sync.dma_start(w2_raw[g][:, t, :], rows[t])
 
         nc.sync.dma_start(offsets[:], offs)
-        load_tw(0)
-        for q in range(4):
-            nc.scalar.dma_start(tsc[32 * q : 32 * q + 8, :].bitcast(I32), tab_scales[:, 4 * q : 4 * q + 4, :].bitcast(I32))
-        for v, vec in enumerate((b1, b4)):
-            nc.scalar.dma_start(brows[4 * v : 4 * v + 4, :], vec.rearrange("(q t i) -> t q i", t=4, i=4))
-        nc.scalar.dma_start(brows[8:11, 0:P], b2.rearrange("(m p) -> m p", p=P))
-        load_w1(0, 0)
-        load_tw(1)
         for q in range(4):
             nc.sync.dma_start(
-                w4s_raw[32 * q : 32 * q + 4, :].bitcast(I32).rearrange("r (a c) -> r a c", a=2),
-                w4_scales[:, 4 * q : 4 * q + 4, :].bitcast(I32).rearrange("a r c -> r a c"),
+                tsc[32 * q + 24 : 32 * q + 32, :].bitcast(I32), tab_scales[:, 4 * q : 4 * q + 4, :].bitcast(I32)
             )
+        load_tw(0)
+        load_w1(0, 0)
+        load_tw(1)
+        for v, vec in enumerate((b1, b4)):
+            nc.sync.dma_start(brows[120 + 4 * v : 124 + 4 * v, :], vec.rearrange("(q t i) -> t q i", t=4, i=4))
+        nc.vector.tensor_copy(vs_raw[:], tsc[:].indirect(offsets[:]))
+        for a in range(2):
+            nc.sync.dma_start(vs[a][0:100, :].bitcast(I32), vs_raw[24 + 4 * a : 124 + 4 * a, :].bitcast(I32))
         load_w1(1, 0)
         load_w4(0)
-        load_page(0)
         load_w1(0, 1)
+        load_page(0)
         load_w1(1, 1)
         load_w4(1)
+        load_page(1)
         load_w2(0)
         load_w2(1)
-        load_page(1)
         load_page(2)
 
         for g in range(2):
-            nc.tensor.transpose(banks[6][:, P * g : P * (g + 1)], brows[:, P * g : P * (g + 1)], ident[:])
+            nc.tensor.transpose(banks[7][:, P * g : P * (g + 1)], brows[:, P * g : P * (g + 1)], ident[:])
         bias = sb("bias", [P, 2, 16], F32)
-        nc.scalar.copy(bias[:], banks[6][:, 0 : 2 * P].rearrange("p (g c) -> p g c", g=2)[:, :, 0:16])
+        nc.scalar.copy(bias[:], banks[7][:, 0 : 2 * P].rearrange("p (g c) -> p g c", g=2)[:, :, 112:128])
 
-        nc.vector.tensor_copy(vs[0][:], tsc[:].indirect(offsets[:]))
-        nc.gpsimd.dma_start(vs[1][0:124, :].bitcast(I32), vs[0][4:128, :].bitcast(I32))
 
         def half_list(s):
             return offsets[:, 32 * s : 32 * (s + 1)]
@@ -132,11 +141,17 @@ def tile_list_marathon_split_caps_kernel(tc, tab_words, tab_scales, offs, w1, b1
             for t in range(2):
                 nc.scalar.activation(dst[:, t], src[:, t], ACT.Copy)
 
+        def on_gpsimd(dst, src):
+            half = dst.shape[1] // 2
+            for u in range(2):
+                part = slice(half * u, half * (u + 1))
+                nc.gpsimd.tensor_scalar(dst[:, part], src[:, part], 1.0, 0.0, ALU.mult, ALU.add)
+
         w4c = [sb(f"w4c{g}", [P, 2 * 2 * KP], U8) for g in range(2)]
         w4s = sb("w4s", [P, 2 * H], U8)
 
         def order_w4_scales():
-            nc.vector.tensor_copy(
+            nc.gpsimd.tensor_copy(
                 w4s[:].bitcast(I32).rearrange("p (u t q) -> p u t q", t=4, q=32),
                 w4s_raw[:].bitcast(I32).rearrange("p (u q t) -> p u t q", t=4, q=32),
             )
@@ -158,12 +173,12 @@ def tile_list_marathon_split_caps_kernel(tc, tab_words, tab_scales, offs, w1, b1
         h_bf = {(0, 0): woven[0], (1, 0): woven[1], (0, 1): woven[1], (1, 1): woven[0]}
         h_codes = {(g, s): sb(f"h_codes{g}{s}", [P, HALF], U32) for g, s in gs_pairs}
         h_sc = {(g, s): sb(f"h_sc{g}{s}", [P, HALF], U8) for g, s in gs_pairs}
-        a_sb = [sb(f"a_sb{i}", [P, HALF], F32) for i in range(3)]
+        a_sb = [sb(f"a_sb{i}", [P, HALF], F32) for i in range(4)]
         units = []
 
         def unit(g, s, t):
             cols = slice(HALF * s, HALF * (s + 1))
-            slot = len(units) % 3
+            slot = len(units) % 4
             units.append((g, s, t))
             pa, pb = banks[2 * slot], banks[2 * slot + 1]
             for a in range(2):
@@ -178,16 +193,16 @@ def tile_list_marathon_split_caps_kernel(tc, tab_words, tab_scales, offs, w1, b1
                     pb[:], w4c[g][:, 2 * c0 : 2 * (c0 + P)].bitcast(FP4X4), w4s[:, s0 : s0 + P],
                     vw[a, s][:].bitcast(FP8X4), vs[a][:, cols], start=(a == 0), stop=(a == 1),
                 )
-            nc.scalar.activation(a_sb[slot][:], pa[:], ACT.Identity, bias=bias[:, g, t : t + 1])
+            nc.scalar.activation(a_sb[slot][:], pa[:], ACT.Identity, bias=bias[:, g, 8 + t : 9 + t])
             nc.vector.scalar_tensor_tensor(
-                h_planes[g, s][:, t, :], pb[:], bias[:, g, 4 + t : 5 + t], a_sb[slot][:], ALU.add, ALU.max
+                h_planes[g, s][:, t, :], pb[:], bias[:, g, 12 + t : 13 + t], a_sb[slot][:], ALU.add, ALU.max
             )
 
-        def weave_h(g, s):
-            nc.scalar.copy(
-                h_bf[g, s][:].rearrange("p (c i t) -> p c t i", i=4, t=4),
-                h_planes[g, s][:].rearrange("p t (c i) -> p c t i", i=4),
-            )
+        def weave_h(g, s, copy):
+            dst = h_bf[g, s][:].rearrange("p (c i t) -> p c t i", i=4, t=4)
+            src = h_planes[g, s][:].rearrange("p t (c i) -> p c t i", i=4)
+            for u in range(2):
+                copy(dst[:, 64 * u : 64 * (u + 1)], src[:, 64 * u : 64 * (u + 1)])
 
         def quant_h(g, s):
             nc.vector.quantize_mx(h_codes[g, s][:].bitcast(FP8X4), h_sc[g, s][:], h_bf[g, s][:])
@@ -196,8 +211,8 @@ def tile_list_marathon_split_caps_kernel(tc, tab_words, tab_scales, offs, w1, b1
         w2_codes = sb("w2_codes", [P, 2 * N], U32)
         w2_sc = sb("w2_sc", [P, 2 * N], U8)
 
-        def cast_w2(g):
-            nc.scalar.copy(
+        def cast_w2(g, copy):
+            copy(
                 w2_bf[:, 4 * N * g : 4 * N * (g + 1)].rearrange("p (c i t) -> p c t i", i=4, t=4),
                 w2_raw[g][:].rearrange("p t (c i) -> p c t i", i=4),
             )
@@ -207,10 +222,10 @@ def tile_list_marathon_split_caps_kernel(tc, tab_words, tab_scales, offs, w1, b1
                 nc.vector.quantize_mx(w2_codes[:, lo:hi].bitcast(FP8X4), w2_sc[:, lo:hi], w2_bf[:, 4 * lo : 4 * hi])
 
         capped = {(m, 1): sb(f"capped{m}", [P, HALF], F32)[:] for m in range(3)}
-        capped[0, 0] = capped[2, 1]
-        capped[1, 0] = capped[0, 1]
-        capped[2, 0] = woven[0][:].bitcast(F32)[:, 0:HALF]
-        y_bank = {(0, 0): 7, (1, 0): 6, (2, 0): 7, (0, 1): 2, (1, 1): 3, (2, 1): 4}
+        capped[0, 0] = a_sb[3][:]
+        for m in (1, 2):
+            capped[m, 0] = woven[0][:].bitcast(F32)[:, HALF * (m - 1) : HALF * m]
+        y_bank = {(0, 0): 0, (1, 0): 1, (2, 0): 2, (0, 1): 3, (1, 1): 4, (2, 1): 5}
 
         def second_stage(m, s):
             py = banks[y_bank[m, s]]
@@ -221,7 +236,7 @@ def tile_list_marathon_split_caps_kernel(tc, tab_words, tab_scales, offs, w1, b1
                     h_codes[g, s][:].bitcast(FP8X4), h_sc[g, s][:], start=(g == 0), stop=(g == 1),
                 )
             nc.vector.scalar_tensor_tensor(
-                capped[m, s], py[:], bias[:, 0, 8 + m : 9 + m], picked[m][:, HALF * s : HALF * (s + 1)], ALU.add, ALU.min
+                capped[m, s], py[:], b2c[:, m : m + 1], picked[m][:, HALF * s : HALF * (s + 1)], ALU.add, ALU.min
             )
 
         def scatter(m, s):
@@ -243,35 +258,40 @@ def tile_list_marathon_split_caps_kernel(tc, tab_words, tab_scales, offs, w1, b1
         gather_words(1, 1)
         for t in range(4):
             unit(0, 0, t)
-        for a in range(2):
-            for u in range(2):
-                cast_w1(a, 1, u, nc.scalar.copy)
-                quant_w1(a, 1, u)
+        cast_w1(0, 1, 0, nc.scalar.copy)
+        quant_w1(0, 1, 0)
+        cast_w1(0, 1, 1, nc.vector.tensor_copy)
+        quant_w1(0, 1, 1)
+        for t in range(4):
+            unit(0, 1, t)
+        cast_w1(1, 1, 0, nc.scalar.copy)
+        quant_w1(1, 1, 0)
+        cast_w1(1, 1, 1, nc.scalar.copy)
+        quant_w1(1, 1, 1)
         order_w4(1)
         gather_page(0)
-        for g, s in ((0, 1), (1, 0)):
-            for t in range(4):
-                unit(g, s, t)
-        weave_h(0, 0)
+        for t in range(4):
+            unit(1, 0, t)
+        weave_h(0, 0, nc.scalar.copy)
         quant_h(0, 0)
-        weave_h(1, 0)
+        weave_h(1, 0, nc.scalar.copy)
         quant_h(1, 0)
-        cast_w2(0)
-        cast_w2(1)
+        cast_w2(0, nc.scalar.copy)
+        cast_w2(1, nc.vector.tensor_copy)
         quant_w2()
         for t in range(4):
             unit(1, 1, t)
         gather_page(1)
         gather_page(2)
-        for m in range(2):
-            second_stage(m, 0)
-        for m in range(2):
-            scatter(m, 0)
+        second_stage(0, 0)
+        scatter(0, 0)
         for g in range(2):
-            weave_h(g, 1)
+            weave_h(g, 1, nc.scalar.copy)
             quant_h(g, 1)
-        second_stage(2, 0)
-        scatter(2, 0)
+        for m in (1, 2):
+            second_stage(m, 0)
+        for m in (1, 2):
+            scatter(m, 0)
         for m in range(3):
             second_stage(m, 1)
         for m in range(3):

@@ -49,19 +49,17 @@ def tile_list_marathon_split_caps_kernel(tc, tab_words, tab_scales, offs, w1, b1
 
         for q in range(4):
             nc.vector.memset(tsc[32 * q : 32 * q + 24, :].bitcast(I32), 0)
-        nc.gpsimd.memset(w4s_raw[:].bitcast(I32), 0)
+        nc.vector.memset(vs_both[96:128, :].bitcast(I32), 0)
+        nc.vector.memset(brows[0:96, :], 0.0)
+        nc.vector.memset(brows[96:120, :], 0.0)
+        nc.vector.memset(w4s_raw[:].bitcast(I32), 0)
+        make_identity(nc, ident[:])
         for q in range(4):
-            nc.gpsimd.dma_start(
+            nc.scalar.dma_start(
                 w4s_raw[32 * q : 32 * q + 4, :].bitcast(I32).rearrange("r (a c) -> r a c", a=2),
                 w4_scales[:, 4 * q : 4 * q + 4, :].bitcast(I32).rearrange("a r c -> r a c"),
             )
-        nc.gpsimd.memset(vs_both[96:128, :].bitcast(I32), 0)
-        nc.gpsimd.memset(brows[0:96, :], 0.0)
-        nc.gpsimd.memset(brows[96:120, :], 0.0)
-        make_identity(nc, ident[:])
         b2c = sb("b2c", [P, 3], F32)
-        with nc.allow_non_contiguous_dma(reason="one value to a partition"):
-            nc.gpsimd.dma_start(b2c[:], b2.rearrange("(m p) -> p m", p=P))
 
         def load_tw(a):
             nc.sync.dma_start(tw[a][:].bitcast(I32), tab_words[a].rearrange("p t i -> p (t i)").bitcast(I32))
@@ -104,10 +102,12 @@ def tile_list_marathon_split_caps_kernel(tc, tab_words, tab_scales, offs, w1, b1
         load_page(0)
         load_w1(1, 1)
         load_w4(1)
-        load_page(1)
         load_w2(0)
         load_w2(1)
+        load_page(1)
         load_page(2)
+        with nc.allow_non_contiguous_dma(reason="one value to a partition"):
+            nc.sync.dma_start(b2c[:], b2.rearrange("(m p) -> p m", p=P))
 
         for g in range(2):
             nc.tensor.transpose(banks[7][:, P * g : P * (g + 1)], brows[:, P * g : P * (g + 1)], ident[:])
@@ -151,7 +151,7 @@ def tile_list_marathon_split_caps_kernel(tc, tab_words, tab_scales, offs, w1, b1
         w4s = sb("w4s", [P, 2 * H], U8)
 
         def order_w4_scales():
-            nc.gpsimd.tensor_copy(
+            nc.vector.tensor_copy(
                 w4s[:].bitcast(I32).rearrange("p (u t q) -> p u t q", t=4, q=32),
                 w4s_raw[:].bitcast(I32).rearrange("p (u q t) -> p u t q", t=4, q=32),
             )
@@ -245,13 +245,13 @@ def tile_list_marathon_split_caps_kernel(tc, tab_words, tab_scales, offs, w1, b1
         gather_words(0, 0)
         gather_words(0, 1)
         cast_w1(0, 0, 0, by_activation)
-        cast_w1(0, 0, 1, nc.vector.tensor_copy)
+        cast_w1(0, 0, 1, nc.scalar.copy)
         quant_w1(0, 0, 0)
         quant_w1(0, 0, 1)
         gather_words(1, 0)
         order_w4_scales()
         cast_w1(1, 0, 0, nc.scalar.copy)
-        cast_w1(1, 0, 1, nc.vector.tensor_copy)
+        cast_w1(1, 0, 1, nc.scalar.copy)
         quant_w1(1, 0, 0)
         order_w4(0)
         quant_w1(1, 0, 1)
@@ -260,25 +260,25 @@ def tile_list_marathon_split_caps_kernel(tc, tab_words, tab_scales, offs, w1, b1
             unit(0, 0, t)
         cast_w1(0, 1, 0, nc.scalar.copy)
         quant_w1(0, 1, 0)
-        cast_w1(0, 1, 1, nc.vector.tensor_copy)
+        cast_w1(0, 1, 1, nc.scalar.copy)
         quant_w1(0, 1, 1)
-        for t in range(4):
-            unit(0, 1, t)
         cast_w1(1, 1, 0, nc.scalar.copy)
         quant_w1(1, 1, 0)
         cast_w1(1, 1, 1, nc.scalar.copy)
         quant_w1(1, 1, 1)
+        for t in range(4):
+            unit(0, 1, t)
         order_w4(1)
         gather_page(0)
         for t in range(4):
             unit(1, 0, t)
+        cast_w2(0, nc.scalar.copy)
+        cast_w2(1, nc.scalar.copy)
+        quant_w2()
         weave_h(0, 0, nc.scalar.copy)
         quant_h(0, 0)
         weave_h(1, 0, nc.scalar.copy)
         quant_h(1, 0)
-        cast_w2(0, nc.scalar.copy)
-        cast_w2(1, nc.vector.tensor_copy)
-        quant_w2()
         for t in range(4):
             unit(1, 1, t)
         gather_page(1)

@@ -127,9 +127,10 @@ def tile_list_marathon_split_caps_kernel(tc, tab_words, tab_scales, offs, w1, b1
             nc.vector.tensor_copy(vw[a, s][:], tw[a][:].indirect(half_list(s)))
 
         def cast_w1(a, g, u, copy):
-            dst = w1_bf[a, g][:].rearrange("p (t q i j) -> p t q j i", t=4, i=4, j=4)
-            src = w1_raw[a, g][:].rearrange("p j (q t i) -> p t q j i", t=4, i=4)
-            copy(dst[:, 2 * u : 2 * u + 2], src[:, 2 * u : 2 * u + 2])
+            dst = w1_bf[a, g][:].rearrange("p (t q h i j) -> p t q h j i", t=4, h=2, i=2, j=4)
+            src = w1_raw[a, g][:].rearrange("p j (q t h i) -> p t q h j i", t=4, h=2, i=2)
+            for t in (2 * u, 2 * u + 1):
+                copy(dst[:, t], src[:, t])
 
         def quant_w1(a, g, u):
             cols = slice(256 * u, 256 * (u + 1))
@@ -138,14 +139,8 @@ def tile_list_marathon_split_caps_kernel(tc, tab_words, tab_scales, offs, w1, b1
             )
 
         def by_activation(dst, src):
-            for t in range(2):
-                nc.scalar.activation(dst[:, t], src[:, t], ACT.Copy)
-
-        def on_gpsimd(dst, src):
-            half = dst.shape[1] // 2
-            for u in range(2):
-                part = slice(half * u, half * (u + 1))
-                nc.gpsimd.tensor_scalar(dst[:, part], src[:, part], 1.0, 0.0, ALU.mult, ALU.add)
+            for h in range(2):
+                nc.scalar.activation(dst[:, :, h], src[:, :, h], ACT.Copy)
 
         w4c = [sb(f"w4c{g}", [P, 2 * 2 * KP], U8) for g in range(2)]
         w4s = sb("w4s", [P, 2 * H], U8)
@@ -199,10 +194,10 @@ def tile_list_marathon_split_caps_kernel(tc, tab_words, tab_scales, offs, w1, b1
             )
 
         def weave_h(g, s, copy):
-            dst = h_bf[g, s][:].rearrange("p (c i t) -> p c t i", i=4, t=4)
-            src = h_planes[g, s][:].rearrange("p t (c i) -> p c t i", i=4)
+            dst = h_bf[g, s][:].rearrange("p (c i t) -> p c t i", i=2, t=4)
+            src = h_planes[g, s][:].rearrange("p t (c i) -> p c t i", i=2)
             for u in range(2):
-                copy(dst[:, 64 * u : 64 * (u + 1)], src[:, 64 * u : 64 * (u + 1)])
+                copy(dst[:, 128 * u : 128 * (u + 1)], src[:, 128 * u : 128 * (u + 1)])
 
         def quant_h(g, s):
             nc.vector.quantize_mx(h_codes[g, s][:].bitcast(FP8X4), h_sc[g, s][:], h_bf[g, s][:])
@@ -213,8 +208,8 @@ def tile_list_marathon_split_caps_kernel(tc, tab_words, tab_scales, offs, w1, b1
 
         def cast_w2(g, copy):
             copy(
-                w2_bf[:, 4 * N * g : 4 * N * (g + 1)].rearrange("p (c i t) -> p c t i", i=4, t=4),
-                w2_raw[g][:].rearrange("p t (c i) -> p c t i", i=4),
+                w2_bf[:, 4 * N * g : 4 * N * (g + 1)].rearrange("p (c i t) -> p c t i", i=2, t=4),
+                w2_raw[g][:].rearrange("p t (c i) -> p c t i", i=2),
             )
 
         def quant_w2():
@@ -262,12 +257,12 @@ def tile_list_marathon_split_caps_kernel(tc, tab_words, tab_scales, offs, w1, b1
         quant_w1(0, 1, 0)
         cast_w1(0, 1, 1, nc.scalar.copy)
         quant_w1(0, 1, 1)
+        for t in range(4):
+            unit(0, 1, t)
         cast_w1(1, 1, 0, nc.scalar.copy)
         quant_w1(1, 1, 0)
         cast_w1(1, 1, 1, nc.scalar.copy)
         quant_w1(1, 1, 1)
-        for t in range(4):
-            unit(0, 1, t)
         order_w4(1)
         gather_page(0)
         for t in range(4):

@@ -18,11 +18,16 @@ ALU = mybir.AluOpType
 ACT = mybir.ActivationFunctionType
 
 P = 128
-KP = 512
+PASS = 512
 HALF = 512
+QUAD = 32
+ROW0 = 24
+SPAN = 3 * QUAD + 4
 
 
-def tile_list_marathon_split_caps_kernel(tc, tab_words, tab_scales, offs, w1, b1, w4_words, w4_scales, b4, w2, b2, gT, out):
+def tile_list_marathon_split_caps_kernel(
+    tc, tab_words, tab_scales, offs, w1, b1, w4_words, w4_scales, b4, w2, b2, gT, out
+):
     nc = tc.nc
     with ExitStack() as ctx:
         keep = ctx.enter_context(tc.tile_pool(name="keep", bufs=1))
@@ -31,71 +36,97 @@ def tile_list_marathon_split_caps_kernel(tc, tab_words, tab_scales, offs, w1, b1
         def sb(name, shape, dtype):
             return keep.tile(shape, dtype, name=name, align_bytes=64)
 
-        pairs = [(a, g) for g in range(2) for a in range(2)]
+        ag_pairs = [(a, g) for g in range(2) for a in range(2)]
+        gs_pairs = [(g, s) for s in range(2) for g in range(2)]
+
         offsets = keep.tile([P, S // 16], U16, name="offsets")
-        tsc = sb("tsc", [P, T], U8)
-        brows = sb("brows", [P, 2 * P], F32)
-        w4s_raw = sb("w4s_raw", [P, 2 * H], U8)
-        vs_both = sb("vs_both", [P, 2 * S], U8)
-        vs = [vs_both[:, S * a : S * (a + 1)] for a in range(2)]
-        vs_raw = sb("vs_raw", [P, S], U8)
+        tab_sc = sb("tab_sc", [P, T], U8)
+        bias_rows = sb("bias_rows", [P, PASS], F32)
+        bias_raw = sb("bias_raw", [4, PASS], F32)
+        w4_sc_raw = sb("w4_sc_raw", [P, 2 * H], U8)
+        v_sc_both = sb("v_sc_both", [P, 2 * S], U8)
+        v_sc = [v_sc_both[:, S * a : S * (a + 1)] for a in range(2)]
+        v_sc_raw = sb("v_sc_raw", [P, S], U8)
         ident = sb("ident", [P, P], F32)
-        tw = [sb(f"tw{a}", [P, T], U32) for a in range(2)]
-        w1_raw = {(a, g): sb(f"w1_raw{a}{g}", [P, 4, KP], F32) for a, g in pairs}
-        w4_raw = [sb(f"w4_raw{g}", [P, 2 * 2 * KP], U8) for g in range(2)]
+        tab_w = [sb(f"tab_w{a}", [P, T], U32) for a in range(2)]
+        w1_raw = {(a, g): sb(f"w1_raw{a}{g}", [P, 4, PASS], F32) for a, g in ag_pairs}
+        w4_raw = [sb(f"w4_raw{g}", [P, 2 * 2 * PASS], U8) for g in range(2)]
         w2_raw = [sb(f"w2_raw{g}", [P, 4, N], F32) for g in range(2)]
         page = [sb(f"page{m}", [P, T], F32) for m in range(3)]
         banks = [psum.tile([P, HALF], F32, name=f"bank{b}") for b in range(8)]
+        b2_col = sb("b2_col", [P, 3], F32)
+        v_words = {(a, s): sb(f"v_words{a}{s}", [P, HALF], U32) for a in range(2) for s in range(2)}
+        w1_bf = {(a, g): sb(f"w1_bf{a}{g}", [P, 4 * PASS], BF16) for a, g in ag_pairs}
+        w1_codes = {(a, g): sb(f"w1_codes{a}{g}", [P, PASS], U32) for a, g in ag_pairs}
+        w1_sc = {(a, g): sb(f"w1_sc{a}{g}", [P, PASS], U8) for a, g in ag_pairs}
+        w4_codes = [sb(f"w4_codes{g}", [P, 2 * 2 * PASS], U8) for g in range(2)]
+        w4_sc = sb("w4_sc", [P, 2 * H], U8)
+        picked = [sb(f"picked{m}", [P, S], F32) for m in range(3)]
+        h_rows = {(g, s): sb(f"h_rows{g}{s}", [P, 4, HALF], BF16) for g, s in gs_pairs}
+        woven = [sb(f"woven{i}", [P, 4 * HALF], BF16) for i in range(2)]
+        h_codes = {(g, s): sb(f"h_codes{g}{s}", [P, HALF], U32) for g, s in gs_pairs}
+        h_sc = {(g, s): sb(f"h_sc{g}{s}", [P, HALF], U8) for g, s in gs_pairs}
+        a_sb = [sb(f"a_sb{t}", [P, HALF], F32) for t in range(4)]
+        w2_bf = sb("w2_bf", [P, 2 * 4 * N], BF16)
+        w2_codes = sb("w2_codes", [P, 2 * N], U32)
+        w2_sc = sb("w2_sc", [P, 2 * N], U8)
+        capped = {(m, 1): sb(f"capped{m}", [P, HALF], F32)[:] for m in range(3)}
+        bias = sb("bias", [P, 4, 4], F32)
+
+        h_bf = {(g, s): woven[(g + s) % 2] for g, s in gs_pairs}
+        capped[0, 0] = a_sb[3][:]
+        for m in (1, 2):
+            capped[m, 0] = woven[0][:].bitcast(F32)[:, HALF * (m - 1) : HALF * m]
 
         for q in range(4):
-            nc.vector.memset(tsc[32 * q : 32 * q + 24, :].bitcast(I32), 0)
-        nc.vector.memset(vs_both[96:128, :].bitcast(I32), 0)
-        nc.vector.memset(brows[0:96, :], 0.0)
-        nc.vector.memset(brows[96:120, :], 0.0)
-        nc.vector.memset(w4s_raw[:].bitcast(I32), 0)
+            nc.vector.memset(tab_sc[QUAD * q : QUAD * q + ROW0, :].bitcast(I32), 0)
+        nc.vector.memset(v_sc_both[3 * QUAD : P, :].bitcast(I32), 0)
+        nc.vector.memset(bias_rows[:], 0.0)
+        nc.vector.memset(w4_sc_raw[:].bitcast(I32), 0)
         make_identity(nc, ident[:])
+
         for q in range(4):
             nc.scalar.dma_start(
-                w4s_raw[32 * q : 32 * q + 4, :].bitcast(I32).rearrange("r (a c) -> r a c", a=2),
+                w4_sc_raw[QUAD * q : QUAD * q + 4, :].bitcast(I32).rearrange("r (a c) -> r a c", a=2),
                 w4_scales[:, 4 * q : 4 * q + 4, :].bitcast(I32).rearrange("a r c -> r a c"),
             )
-        b2c = sb("b2c", [P, 3], F32)
 
-        def load_tw(a):
-            nc.sync.dma_start(tw[a][:].bitcast(I32), tab_words[a].rearrange("p t i -> p (t i)").bitcast(I32))
+        def load_table(a):
+            nc.sync.dma_start(tab_w[a][:].bitcast(I32), tab_words[a].rearrange("p t i -> p (t i)").bitcast(I32))
 
         def load_w1(a, g):
-            nc.sync.dma_start(
-                w1_raw[a, g][:], w1[KP * a : KP * (a + 1), KP * g : KP * (g + 1)].rearrange("(p j) c -> p j c", j=4)
-            )
+            block = w1[PASS * a : PASS * (a + 1), PASS * g : PASS * (g + 1)]
+            nc.sync.dma_start(w1_raw[a, g][:], block.rearrange("(p j) c -> p j c", j=4))
 
         def load_w4(g):
             nc.sync.dma_start(
                 w4_raw[g][:].bitcast(I32).rearrange("p (a c) -> p a c", a=2),
-                w4_words[:, :, 2 * KP * g : 2 * KP * (g + 1)].bitcast(I32).rearrange("a p c -> p a c"),
+                w4_words[:, :, 2 * PASS * g : 2 * PASS * (g + 1)].bitcast(I32).rearrange("a p c -> p a c"),
             )
 
         def load_page(m):
             nc.sync.dma_start(page[m][:], gT[P * m : P * (m + 1), :])
 
         def load_w2(g):
-            rows = w2[KP * g : KP * (g + 1), :].rearrange("(q t i) n -> t q i n", t=4, i=4)
+            rows = w2[PASS * g : PASS * (g + 1), :].rearrange("(q t i) n -> t q i n", t=4, i=4)
             for t in range(4):
                 nc.sync.dma_start(w2_raw[g][:, t, :], rows[t])
 
         nc.sync.dma_start(offsets[:], offs)
         for q in range(4):
             nc.sync.dma_start(
-                tsc[32 * q + 24 : 32 * q + 32, :].bitcast(I32), tab_scales[:, 4 * q : 4 * q + 4, :].bitcast(I32)
+                tab_sc[QUAD * q + ROW0 : QUAD * (q + 1), :].bitcast(I32),
+                tab_scales[:, 4 * q : 4 * q + 4, :].bitcast(I32),
             )
-        load_tw(0)
-        load_w1(0, 0)
-        load_tw(1)
+        load_table(0)
         for v, vec in enumerate((b1, b4)):
-            nc.sync.dma_start(brows[120 + 4 * v : 124 + 4 * v, :], vec.rearrange("(q t i) -> t q i", t=4, i=4))
-        nc.vector.tensor_copy(vs_raw[:], tsc[:].indirect(offsets[:]))
+            nc.sync.dma_start(bias_raw[2 * v : 2 * v + 2, :], vec.rearrange("(g c) -> g c", g=2))
+        load_w1(0, 0)
+        load_table(1)
+        nc.vector.tensor_copy(v_sc_raw[:], tab_sc[:].indirect(offsets[:]))
         for a in range(2):
-            nc.sync.dma_start(vs[a][0:100, :].bitcast(I32), vs_raw[24 + 4 * a : 124 + 4 * a, :].bitcast(I32))
+            first = ROW0 + 4 * a
+            nc.sync.dma_start(v_sc[a][0:SPAN, :].bitcast(I32), v_sc_raw[first : first + SPAN, :].bitcast(I32))
         load_w1(1, 0)
         load_w4(0)
         load_w1(0, 1)
@@ -106,132 +137,101 @@ def tile_list_marathon_split_caps_kernel(tc, tab_words, tab_scales, offs, w1, b1
         load_w2(1)
         load_page(1)
         load_page(2)
-        with nc.allow_non_contiguous_dma(reason="one value to a partition"):
-            nc.sync.dma_start(b2c[:], b2.rearrange("(m p) -> p m", p=P))
+        with nc.allow_non_contiguous_dma(reason="one value of b2 to a partition"):
+            nc.sync.dma_start(b2_col[:], b2.rearrange("(m p) -> p m", p=P))
 
-        for g in range(2):
-            nc.tensor.transpose(banks[7][:, P * g : P * (g + 1)], brows[:, P * g : P * (g + 1)], ident[:])
-        bias = sb("bias", [P, 2, 16], F32)
-        nc.scalar.copy(bias[:], banks[7][:, 0 : 2 * P].rearrange("p (g c) -> p g c", g=2)[:, :, 112:128])
-
+        nc.scalar.copy(
+            bias_rows[0:4, :].rearrange("v (t q i) -> v t q i", t=4, i=4),
+            bias_raw[:].rearrange("v (q t i) -> v t q i", t=4, i=4),
+        )
 
         def half_list(s):
-            return offsets[:, 32 * s : 32 * (s + 1)]
-
-        vw = {(a, s): sb(f"vw{a}{s}", [P, HALF], U32) for a in range(2) for s in range(2)}
-        w1_bf = {(a, g): sb(f"w1_bf{a}{g}", [P, 4 * KP], BF16) for a, g in pairs}
-        w1_codes = {(a, g): sb(f"w1_codes{a}{g}", [P, KP], U32) for a, g in pairs}
-        w1_sc = {(a, g): sb(f"w1_sc{a}{g}", [P, KP], U8) for a, g in pairs}
+            return offsets[:, HALF // 16 * s : HALF // 16 * (s + 1)]
 
         def gather_words(a, s):
-            nc.vector.tensor_copy(vw[a, s][:], tw[a][:].indirect(half_list(s)))
+            nc.vector.tensor_copy(v_words[a, s][:], tab_w[a][:].indirect(half_list(s)))
 
         def cast_w1(a, g, u, copy):
-            dst = w1_bf[a, g][:].rearrange("p (t q h i j) -> p t q h j i", t=4, h=2, i=2, j=4)
-            src = w1_raw[a, g][:].rearrange("p j (q t h i) -> p t q h j i", t=4, h=2, i=2)
+            dst = w1_bf[a, g][:].rearrange("p (t q e i j) -> p t q e j i", t=4, e=2, i=2, j=4)
+            src = w1_raw[a, g][:].rearrange("p j (q t e i) -> p t q e j i", t=4, e=2, i=2)
             for t in (2 * u, 2 * u + 1):
                 copy(dst[:, t], src[:, t])
 
+        def copy_by_activation(dst, src):
+            for e in range(2):
+                nc.scalar.activation(dst[:, :, e], src[:, :, e], ACT.Copy)
+
         def quant_w1(a, g, u):
-            cols = slice(256 * u, 256 * (u + 1))
-            nc.vector.quantize_mx(
-                w1_codes[a, g][:, cols].bitcast(FP8X4), w1_sc[a, g][:, cols], w1_bf[a, g][:, 1024 * u : 1024 * (u + 1)]
-            )
-
-        def by_activation(dst, src):
-            for h in range(2):
-                nc.scalar.activation(dst[:, :, h], src[:, :, h], ACT.Copy)
-
-        w4c = [sb(f"w4c{g}", [P, 2 * 2 * KP], U8) for g in range(2)]
-        w4s = sb("w4s", [P, 2 * H], U8)
+            cols = slice(2 * P * u, 2 * P * (u + 1))
+            values = w1_bf[a, g][:, 8 * P * u : 8 * P * (u + 1)]
+            nc.vector.quantize_mx(w1_codes[a, g][:, cols].bitcast(FP8X4), w1_sc[a, g][:, cols], values)
 
         def order_w4_scales():
             nc.vector.tensor_copy(
-                w4s[:].bitcast(I32).rearrange("p (u t q) -> p u t q", t=4, q=32),
-                w4s_raw[:].bitcast(I32).rearrange("p (u q t) -> p u t q", t=4, q=32),
+                w4_sc[:].bitcast(I32).rearrange("p (u t q) -> p u t q", t=4, q=32),
+                w4_sc_raw[:].bitcast(I32).rearrange("p (u q t) -> p u t q", t=4, q=32),
             )
 
-        def order_w4(g):
+        def order_w4_words(g):
             nc.vector.tensor_copy(
-                w4c[g][:].bitcast(I32).rearrange("p (a t q e) -> p a t q e", t=4, q=32, e=2),
+                w4_codes[g][:].bitcast(I32).rearrange("p (a t q e) -> p a t q e", t=4, q=32, e=2),
                 w4_raw[g][:].bitcast(I32).rearrange("p (a q t e) -> p a t q e", t=4, q=32, e=2),
             )
-
-        picked = [sb(f"picked{m}", [P, S], F32) for m in range(3)]
 
         def gather_page(m):
             nc.vector.tensor_copy(picked[m][:], page[m][:].indirect(offsets[:]))
 
-        gs_pairs = [(0, 0), (1, 0), (0, 1), (1, 1)]
-        h_planes = {(g, s): sb(f"h_planes{g}{s}", [P, 4, HALF], BF16) for g, s in gs_pairs}
-        woven = [sb(f"woven{i}", [P, 4 * HALF], BF16) for i in range(2)]
-        h_bf = {(0, 0): woven[0], (1, 0): woven[1], (0, 1): woven[1], (1, 1): woven[0]}
-        h_codes = {(g, s): sb(f"h_codes{g}{s}", [P, HALF], U32) for g, s in gs_pairs}
-        h_sc = {(g, s): sb(f"h_sc{g}{s}", [P, HALF], U8) for g, s in gs_pairs}
-        a_sb = [sb(f"a_sb{i}", [P, HALF], F32) for i in range(4)]
-        units = []
-
-        def unit(g, s, t):
-            cols = slice(HALF * s, HALF * (s + 1))
-            slot = len(units) % 4
-            units.append((g, s, t))
-            pa, pb = banks[2 * slot], banks[2 * slot + 1]
-            for a in range(2):
-                nc.tensor.matmul_mx(
-                    pa[:], w1_codes[a, g][:, P * t : P * (t + 1)].bitcast(FP8X4), w1_sc[a, g][:, P * t : P * (t + 1)],
-                    vw[a, s][:].bitcast(FP8X4), vs[a][:, cols], start=(a == 0), stop=(a == 1),
+        def first_products(g, s):
+            entries = slice(HALF * s, HALF * (s + 1))
+            for t in range(4):
+                bank_a, bank_b = banks[2 * t], banks[2 * t + 1]
+                cols = slice(P * t, P * (t + 1))
+                for a in range(2):
+                    nc.tensor.matmul_mx(
+                        bank_a[:], w1_codes[a, g][:, cols].bitcast(FP8X4), w1_sc[a, g][:, cols],
+                        v_words[a, s][:].bitcast(FP8X4), v_sc[a][:, entries], start=(a == 0), stop=(a == 1),
+                    )
+                for a in range(2):
+                    word0 = PASS * a + P * t
+                    scale0 = H * a + PASS * g + P * t
+                    nc.tensor.matmul_mx(
+                        bank_b[:], w4_codes[g][:, 2 * word0 : 2 * (word0 + P)].bitcast(FP4X4),
+                        w4_sc[:, scale0 : scale0 + P],
+                        v_words[a, s][:].bitcast(FP8X4), v_sc[a][:, entries], start=(a == 0), stop=(a == 1),
+                    )
+                nc.scalar.activation(a_sb[t][:], bank_a[:], ACT.Identity, bias=bias[:, t, g : g + 1])
+                nc.vector.scalar_tensor_tensor(
+                    h_rows[g, s][:, t, :], bank_b[:], bias[:, t, 2 + g : 3 + g], a_sb[t][:], ALU.add, ALU.max
                 )
-            for a in range(2):
-                c0 = KP * a + P * t
-                s0 = H * a + KP * g + P * t
-                nc.tensor.matmul_mx(
-                    pb[:], w4c[g][:, 2 * c0 : 2 * (c0 + P)].bitcast(FP4X4), w4s[:, s0 : s0 + P],
-                    vw[a, s][:].bitcast(FP8X4), vs[a][:, cols], start=(a == 0), stop=(a == 1),
-                )
-            nc.scalar.activation(a_sb[slot][:], pa[:], ACT.Identity, bias=bias[:, g, 8 + t : 9 + t])
-            nc.vector.scalar_tensor_tensor(
-                h_planes[g, s][:, t, :], pb[:], bias[:, g, 12 + t : 13 + t], a_sb[slot][:], ALU.add, ALU.max
-            )
 
-        def weave_h(g, s, copy):
+        def quantise_h(g, s):
             dst = h_bf[g, s][:].rearrange("p (c i t) -> p c t i", i=2, t=4)
-            src = h_planes[g, s][:].rearrange("p t (c i) -> p c t i", i=2)
+            src = h_rows[g, s][:].rearrange("p t (c i) -> p c t i", i=2)
             for u in range(2):
-                copy(dst[:, 128 * u : 128 * (u + 1)], src[:, 128 * u : 128 * (u + 1)])
-
-        def quant_h(g, s):
+                part = slice(HALF // 4 * u, HALF // 4 * (u + 1))
+                nc.scalar.copy(dst[:, part], src[:, part])
             nc.vector.quantize_mx(h_codes[g, s][:].bitcast(FP8X4), h_sc[g, s][:], h_bf[g, s][:])
 
-        w2_bf = sb("w2_bf", [P, 2 * 4 * N], BF16)
-        w2_codes = sb("w2_codes", [P, 2 * N], U32)
-        w2_sc = sb("w2_sc", [P, 2 * N], U8)
-
-        def cast_w2(g, copy):
-            copy(
-                w2_bf[:, 4 * N * g : 4 * N * (g + 1)].rearrange("p (c i t) -> p c t i", i=2, t=4),
-                w2_raw[g][:].rearrange("p t (c i) -> p c t i", i=2),
-            )
-
-        def quant_w2():
-            for lo, hi in ((0, 512), (512, 768)):
+        def quantise_w2():
+            for g in range(2):
+                nc.scalar.copy(
+                    w2_bf[:, 4 * N * g : 4 * N * (g + 1)].rearrange("p (c i t) -> p c t i", i=2, t=4),
+                    w2_raw[g][:].rearrange("p t (c i) -> p c t i", i=2),
+                )
+            for lo, hi in ((0, 512), (512, 2 * N)):
                 nc.vector.quantize_mx(w2_codes[:, lo:hi].bitcast(FP8X4), w2_sc[:, lo:hi], w2_bf[:, 4 * lo : 4 * hi])
 
-        capped = {(m, 1): sb(f"capped{m}", [P, HALF], F32)[:] for m in range(3)}
-        capped[0, 0] = a_sb[3][:]
-        for m in (1, 2):
-            capped[m, 0] = woven[0][:].bitcast(F32)[:, HALF * (m - 1) : HALF * m]
-        y_bank = {(0, 0): 0, (1, 0): 1, (2, 0): 2, (0, 1): 3, (1, 1): 4, (2, 1): 5}
-
-        def second_stage(m, s):
-            py = banks[y_bank[m, s]]
+        def third_product(m, s):
+            bank_y = banks[3 * s + m]
             for g in range(2):
-                c0 = N * g + P * m
+                cols = slice(N * g + P * m, N * g + P * (m + 1))
                 nc.tensor.matmul_mx(
-                    py[:], w2_codes[:, c0 : c0 + P].bitcast(FP8X4), w2_sc[:, c0 : c0 + P],
+                    bank_y[:], w2_codes[:, cols].bitcast(FP8X4), w2_sc[:, cols],
                     h_codes[g, s][:].bitcast(FP8X4), h_sc[g, s][:], start=(g == 0), stop=(g == 1),
                 )
             nc.vector.scalar_tensor_tensor(
-                capped[m, s], py[:], b2c[:, m : m + 1], picked[m][:, HALF * s : HALF * (s + 1)], ALU.add, ALU.min
+                capped[m, s], bank_y[:], b2_col[:, m : m + 1], picked[m][:, HALF * s : HALF * (s + 1)],
+                ALU.add, ALU.min,
             )
 
         def scatter(m, s):
@@ -239,8 +239,11 @@ def tile_list_marathon_split_caps_kernel(tc, tab_words, tab_scales, offs, w1, b1
 
         gather_words(0, 0)
         gather_words(0, 1)
-        cast_w1(0, 0, 0, by_activation)
+        cast_w1(0, 0, 0, copy_by_activation)
         cast_w1(0, 0, 1, nc.scalar.copy)
+        for t in range(4):
+            nc.tensor.transpose(banks[7][:, P * t : P * (t + 1)], bias_rows[:, P * t : P * (t + 1)], ident[:])
+        nc.scalar.copy(bias[:], banks[7][:].rearrange("p (t c) -> p t c", t=4)[:, :, 0:4])
         quant_w1(0, 0, 0)
         quant_w1(0, 0, 1)
         gather_words(1, 0)
@@ -248,47 +251,36 @@ def tile_list_marathon_split_caps_kernel(tc, tab_words, tab_scales, offs, w1, b1
         cast_w1(1, 0, 0, nc.scalar.copy)
         cast_w1(1, 0, 1, nc.scalar.copy)
         quant_w1(1, 0, 0)
-        order_w4(0)
+        order_w4_words(0)
         quant_w1(1, 0, 1)
         gather_words(1, 1)
-        for t in range(4):
-            unit(0, 0, t)
-        cast_w1(0, 1, 0, nc.scalar.copy)
-        quant_w1(0, 1, 0)
-        cast_w1(0, 1, 1, nc.scalar.copy)
-        quant_w1(0, 1, 1)
-        for t in range(4):
-            unit(0, 1, t)
-        cast_w1(1, 1, 0, nc.scalar.copy)
-        quant_w1(1, 1, 0)
-        cast_w1(1, 1, 1, nc.scalar.copy)
-        quant_w1(1, 1, 1)
-        order_w4(1)
+
+        for s in range(2):
+            first_products(0, s)
+            for u in range(2):
+                cast_w1(s, 1, u, nc.scalar.copy)
+                quant_w1(s, 1, u)
+        order_w4_words(1)
         gather_page(0)
-        for t in range(4):
-            unit(1, 0, t)
-        cast_w2(0, nc.scalar.copy)
-        cast_w2(1, nc.scalar.copy)
-        quant_w2()
-        weave_h(0, 0, nc.scalar.copy)
-        quant_h(0, 0)
-        weave_h(1, 0, nc.scalar.copy)
-        quant_h(1, 0)
-        for t in range(4):
-            unit(1, 1, t)
+
+        first_products(1, 0)
+        quantise_w2()
+        for g in range(2):
+            quantise_h(g, 0)
+        first_products(1, 1)
         gather_page(1)
         gather_page(2)
-        second_stage(0, 0)
+
+        third_product(0, 0)
         scatter(0, 0)
         for g in range(2):
-            weave_h(g, 1, nc.scalar.copy)
-            quant_h(g, 1)
+            quantise_h(g, 1)
         for m in (1, 2):
-            second_stage(m, 0)
+            third_product(m, 0)
         for m in (1, 2):
             scatter(m, 0)
         for m in range(3):
-            second_stage(m, 1)
+            third_product(m, 1)
         for m in range(3):
             scatter(m, 1)
             nc.sync.dma_start(out[P * m : P * (m + 1), :], page[m][:])

@@ -21,7 +21,7 @@ P = 128
 PASS = 512
 HALF = 512
 QUAD = 32
-ROW0 = 24
+SHIFT = 16
 SPAN = 3 * QUAD + 4
 
 
@@ -33,63 +33,62 @@ def tile_list_marathon_split_caps_kernel(
         keep = ctx.enter_context(tc.tile_pool(name="keep", bufs=1))
         psum = ctx.enter_context(tc.psum_pool(name="psum", bufs=1))
 
-        def sb(name, shape, dtype):
-            return keep.tile(shape, dtype, name=name, align_bytes=64)
+        def sb(name, shape, dtype, tag=None):
+            return keep.tile(shape, dtype, name=name, tag=tag or name, align_bytes=64)
 
         ag_pairs = [(a, g) for g in range(2) for a in range(2)]
         gs_pairs = [(g, s) for s in range(2) for g in range(2)]
 
         offsets = keep.tile([P, S // 16], U16, name="offsets")
         tab_sc = sb("tab_sc", [P, T], U8)
+        v_sc = [sb(f"v_sc{a}", [P, S], U8) for a in range(2)]
         bias_rows = sb("bias_rows", [P, PASS], F32)
         bias_raw = sb("bias_raw", [4, PASS], F32)
-        w4_sc_raw = sb("w4_sc_raw", [P, 2 * H], U8)
-        v_sc_both = sb("v_sc_both", [P, 2 * S], U8)
-        v_sc = [v_sc_both[:, S * a : S * (a + 1)] for a in range(2)]
-        v_sc_raw = sb("v_sc_raw", [P, S], U8)
-        ident = sb("ident", [P, P], F32)
-        tab_w = [sb(f"tab_w{a}", [P, T], U32) for a in range(2)]
-        w1_raw = {(a, g): sb(f"w1_raw{a}{g}", [P, 4, PASS], F32) for a, g in ag_pairs}
-        w4_raw = [sb(f"w4_raw{g}", [P, 2 * 2 * PASS], U8) for g in range(2)]
-        w2_raw = [sb(f"w2_raw{g}", [P, 4, N], F32) for g in range(2)]
-        page = [sb(f"page{m}", [P, T], F32) for m in range(3)]
-        banks = [psum.tile([P, HALF], F32, name=f"bank{b}") for b in range(8)]
+        bias = sb("bias", [P, 4, 4], F32)
         b2_col = sb("b2_col", [P, 3], F32)
-        v_words = {(a, s): sb(f"v_words{a}{s}", [P, HALF], U32) for a in range(2) for s in range(2)}
+        ident = sb("ident", [P, P], F32)
+        w4_sc_raw = sb("w4_sc_raw", [P, 2 * H], U8)
+        w4_sc = sb("w4_sc", [P, 2 * H], U8)
+        w4_raw = sb("w4_raw", [P, 4 * H], U8)
+        w4_codes = sb("w4_codes", [P, 4 * H], U8)
+        tab_w = [sb(f"tab_w{a}", [P, T], U32) for a in range(2)]
+        v_words = {(a, s): sb(f"v_words{a}{s}", [P, HALF], U32) for a, s in ((0, 0), (1, 0), (1, 1))}
+        w1_raw = {(a, g): sb(f"w1_raw{a}{g}", [P, 4, PASS], F32) for a, g in ag_pairs}
         w1_bf = {(a, g): sb(f"w1_bf{a}{g}", [P, 4 * PASS], BF16) for a, g in ag_pairs}
         w1_codes = {(a, g): sb(f"w1_codes{a}{g}", [P, PASS], U32) for a, g in ag_pairs}
         w1_sc = {(a, g): sb(f"w1_sc{a}{g}", [P, PASS], U8) for a, g in ag_pairs}
-        w4_codes = [sb(f"w4_codes{g}", [P, 2 * 2 * PASS], U8) for g in range(2)]
-        w4_sc = sb("w4_sc", [P, 2 * H], U8)
-        picked = [sb(f"picked{m}", [P, S], F32) for m in range(3)]
-        h_rows = {(g, s): sb(f"h_rows{g}{s}", [P, 4, HALF], BF16) for g, s in gs_pairs}
-        woven = [sb(f"woven{i}", [P, 4 * HALF], BF16) for i in range(2)]
-        h_codes = {(g, s): sb(f"h_codes{g}{s}", [P, HALF], U32) for g, s in gs_pairs}
-        h_sc = {(g, s): sb(f"h_sc{g}{s}", [P, HALF], U8) for g, s in gs_pairs}
-        a_sb = [sb(f"a_sb{t}", [P, HALF], F32) for t in range(4)]
+        w2_raw = [sb(f"w2_raw{g}", [P, 4, N], F32) for g in range(2)]
         w2_bf = sb("w2_bf", [P, 2 * 4 * N], BF16)
         w2_codes = sb("w2_codes", [P, 2 * N], U32)
         w2_sc = sb("w2_sc", [P, 2 * N], U8)
-        capped = {(m, 1): sb(f"capped{m}", [P, HALF], F32)[:] for m in range(3)}
-        bias = sb("bias", [P, 4, 4], F32)
+        page = [sb(f"page{m}", [P, T], F32) for m in range(3)]
+        picked = {(m, s): sb(f"picked{m}{s}", [P, HALF], F32)[:] for m in range(3) for s in range(2) if (m, s) != (2, 1)}
+        picked[2, 1] = w2_bf[:].bitcast(F32)[:, 2 * HALF : 3 * HALF]
+        b_sb = {(g, 0, t): sb(f"b_sb{g}0{t}", [P, HALF], F32)[:] for g in range(2) for t in range(4)}
+        h_rows = {(g, s): sb(f"h_rows{g}{s}", [P, 4, HALF], BF16)[:] for g, s in gs_pairs[1:]}
+        h_rows[0, 0] = w1_bf[0, 1][:].rearrange("p (t c) -> p t c", t=4)
+        a_bf = [w2_bf[:, 0 : 4 * HALF], sb("a_bf1", [P, 4 * HALF], BF16)[:]]
+        b_bf = [w1_bf[0, 1][:], w2_raw[1][:].rearrange("p t n -> p (t n)").bitcast(BF16)[:, 0 : 4 * HALF]]
+        woven = [sb(f"woven{i}", [P, 4 * HALF], BF16) for i in range(2)]
+        h_codes = {(g, s): sb(f"h_codes{g}{s}", [P, HALF], U32) for g, s in gs_pairs}
+        h_sc = {(g, s): sb(f"h_sc{g}{s}", [P, HALF], U8) for g, s in gs_pairs}
+        banks = [psum.tile([P, HALF], F32, name=f"bank{b}") for b in range(8)]
 
-        h_bf = {(g, s): woven[(g + s) % 2] for g, s in gs_pairs}
-        capped[0, 0] = a_sb[3][:]
-        for m in (1, 2):
-            capped[m, 0] = woven[0][:].bitcast(F32)[:, HALF * (m - 1) : HALF * m]
+        h_bf = {(g, s): woven[g][:] for g, s in gs_pairs}
+        h_bf[0, 0] = w1_raw[1, 1][:].rearrange("p k c -> p (k c)").bitcast(BF16)[:, 0 : 4 * HALF]
+        capped = {(m, 1): b_sb[0, 0, m] for m in range(3)}
+        capped[0, 0] = b_sb[0, 0, 3]
+        capped[1, 0] = a_bf[1].bitcast(F32)[:, 0:HALF]
+        capped[2, 0] = woven[1][:].bitcast(F32)[:, 0:HALF]
 
-        for q in range(4):
-            nc.vector.memset(tab_sc[QUAD * q : QUAD * q + ROW0, :].bitcast(I32), 0)
-        nc.vector.memset(v_sc_both[3 * QUAD : P, :].bitcast(I32), 0)
-        nc.vector.memset(bias_rows[:], 0.0)
+        nc.sync.dma_start(offsets[:], offs)
+        nc.gpsimd.memset(tab_sc[:].bitcast(I32), 0)
         nc.vector.memset(w4_sc_raw[:].bitcast(I32), 0)
+        nc.vector.memset(v_sc[1][3 * QUAD : P, :].bitcast(I32), 0)
         make_identity(nc, ident[:])
-
-        for q in range(4):
-            nc.scalar.dma_start(
-                w4_sc_raw[QUAD * q : QUAD * q + 4, :].bitcast(I32).rearrange("r (a c) -> r a c", a=2),
-                w4_scales[:, 4 * q : 4 * q + 4, :].bitcast(I32).rearrange("a r c -> r a c"),
-            )
+        nc.scalar.activation(
+            bias_rows[:].rearrange("p (t c) -> p t c", t=4), ident[:].unsqueeze(1).to_broadcast([P, 4, P]), ACT.Identity, scale=0.0
+        )
 
         def load_table(a):
             nc.sync.dma_start(tab_w[a][:].bitcast(I32), tab_words[a].rearrange("p t i -> p (t i)").bitcast(I32))
@@ -98,52 +97,49 @@ def tile_list_marathon_split_caps_kernel(
             block = w1[PASS * a : PASS * (a + 1), PASS * g : PASS * (g + 1)]
             nc.sync.dma_start(w1_raw[a, g][:], block.rearrange("(p j) c -> p j c", j=4))
 
-        def load_w4(g):
-            nc.sync.dma_start(
-                w4_raw[g][:].bitcast(I32).rearrange("p (a c) -> p a c", a=2),
-                w4_words[:, :, 2 * PASS * g : 2 * PASS * (g + 1)].bitcast(I32).rearrange("a p c -> p a c"),
-            )
-
         def load_page(m):
             nc.sync.dma_start(page[m][:], gT[P * m : P * (m + 1), :])
 
         def load_w2(g):
-            rows = w2[PASS * g : PASS * (g + 1), :].rearrange("(q t i) n -> t q i n", t=4, i=4)
+            rows = w2[PASS * g : PASS * (g + 1), :].rearrange("(j t i) n -> t j i n", t=4, i=8)
             for t in range(4):
                 nc.sync.dma_start(w2_raw[g][:, t, :], rows[t])
 
-        nc.sync.dma_start(offsets[:], offs)
+        tab_rows = tab_scales.bitcast(I32).rearrange("a (q r) c -> r q a c", r=4)
+        nc.sync.dma_start(bias_raw[2:4, :], b4.rearrange("(g c) -> g c", g=2))
+        for r in range(4):
+            nc.sync.dma_start(tab_sc[r:P:SHIFT, :].bitcast(I32), tab_rows[r])
+        load_table(0)
+        nc.sync.dma_start(
+            w4_raw[:].bitcast(I32).rearrange("p (a c) -> p a c", a=2), w4_words.bitcast(I32).rearrange("a p c -> p a c")
+        )
         for q in range(4):
             nc.sync.dma_start(
-                tab_sc[QUAD * q + ROW0 : QUAD * (q + 1), :].bitcast(I32),
-                tab_scales[:, 4 * q : 4 * q + 4, :].bitcast(I32),
+                w4_sc_raw[QUAD * q : QUAD * q + 4, :].bitcast(I32).rearrange("r (a c) -> r a c", a=2),
+                w4_scales[:, 4 * q : 4 * q + 4, :].bitcast(I32).rearrange("a r c -> r a c"),
             )
-        load_table(0)
-        for v, vec in enumerate((b1, b4)):
-            nc.sync.dma_start(bias_raw[2 * v : 2 * v + 2, :], vec.rearrange("(g c) -> g c", g=2))
-        load_w1(0, 0)
+        nc.sync.dma_start(bias_raw[0:2, :], b1.rearrange("(g c) -> g c", g=2))
         load_table(1)
-        nc.vector.tensor_copy(v_sc_raw[:], tab_sc[:].indirect(offsets[:]))
-        for a in range(2):
-            first = ROW0 + 4 * a
-            nc.sync.dma_start(v_sc[a][0:SPAN, :].bitcast(I32), v_sc_raw[first : first + SPAN, :].bitcast(I32))
-        load_w1(1, 0)
-        load_w4(0)
-        load_w1(0, 1)
+        nc.vector.tensor_copy(v_sc[0][:], tab_sc[:].indirect(offsets[:]))
+        nc.sync.dma_start(v_sc[1][0:SPAN, :].bitcast(I32), v_sc[0][SHIFT : SHIFT + SPAN, :].bitcast(I32))
+        for a, g in ag_pairs:
+            load_w1(a, g)
         load_page(0)
-        load_w1(1, 1)
-        load_w4(1)
         load_w2(0)
-        load_w2(1)
         load_page(1)
         load_page(2)
+        load_w2(1)
         with nc.allow_non_contiguous_dma(reason="one value of b2 to a partition"):
             nc.sync.dma_start(b2_col[:], b2.rearrange("(m p) -> p m", p=P))
 
-        nc.scalar.copy(
-            bias_rows[0:4, :].rearrange("v (t q i) -> v t q i", t=4, i=4),
-            bias_raw[:].rearrange("v (q t i) -> v t q i", t=4, i=4),
+        nc.scalar.activation(
+            bias_rows[0:4, :].rearrange("v (t j i) -> v t j i", t=4, i=8),
+            bias_raw[:].rearrange("v (j t i) -> v t j i", t=4, i=8),
+            ACT.Copy,
         )
+        for t in range(4):
+            nc.tensor.transpose(banks[7][:, P * t : P * (t + 1)], bias_rows[:, P * t : P * (t + 1)], ident[:])
+        nc.scalar.copy(bias[:], banks[7][:].rearrange("p (t c) -> p t c", t=4)[:, :, 0:4])
 
         def half_list(s):
             return offsets[:, HALF // 16 * s : HALF // 16 * (s + 1)]
@@ -151,78 +147,106 @@ def tile_list_marathon_split_caps_kernel(
         def gather_words(a, s):
             nc.vector.tensor_copy(v_words[a, s][:], tab_w[a][:].indirect(half_list(s)))
 
-        def cast_w1(a, g, u, copy):
-            dst = w1_bf[a, g][:].rearrange("p (t q e i j) -> p t q e j i", t=4, e=2, i=2, j=4)
-            src = w1_raw[a, g][:].rearrange("p j (q t e i) -> p t q e j i", t=4, e=2, i=2)
-            for t in (2 * u, 2 * u + 1):
+        def cast_w1(a, g, copy):
+            dst = w1_bf[a, g][:].rearrange("p (t j e i k) -> p t j e k i", t=4, e=2, i=4, k=4)
+            src = w1_raw[a, g][:].rearrange("p k (j t e i) -> p t j e k i", t=4, e=2, i=4)
+            for t in range(4):
                 copy(dst[:, t], src[:, t])
 
-        def copy_by_activation(dst, src):
-            for e in range(2):
-                nc.scalar.activation(dst[:, :, e], src[:, :, e], ACT.Copy)
+        def quant_w1(a, g):
+            for u in range(2):
+                cols = slice(2 * P * u, 2 * P * (u + 1))
+                values = w1_bf[a, g][:, 8 * P * u : 8 * P * (u + 1)]
+                nc.vector.quantize_mx(w1_codes[a, g][:, cols].bitcast(FP8X4), w1_sc[a, g][:, cols], values)
 
-        def quant_w1(a, g, u):
-            cols = slice(2 * P * u, 2 * P * (u + 1))
-            values = w1_bf[a, g][:, 8 * P * u : 8 * P * (u + 1)]
-            nc.vector.quantize_mx(w1_codes[a, g][:, cols].bitcast(FP8X4), w1_sc[a, g][:, cols], values)
-
-        def order_w4_scales():
-            nc.vector.tensor_copy(
-                w4_sc[:].bitcast(I32).rearrange("p (u t q) -> p u t q", t=4, q=32),
-                w4_sc_raw[:].bitcast(I32).rearrange("p (u q t) -> p u t q", t=4, q=32),
-            )
-
-        def order_w4_words(g):
-            nc.vector.tensor_copy(
-                w4_codes[g][:].bitcast(I32).rearrange("p (a t q e) -> p a t q e", t=4, q=32, e=2),
-                w4_raw[g][:].bitcast(I32).rearrange("p (a q t e) -> p a t q e", t=4, q=32, e=2),
-            )
+        def order_w4():
+            for dst, src, e in ((w4_sc, w4_sc_raw, 2), (w4_codes, w4_raw, 4)):
+                nc.vector.tensor_copy(
+                    dst[:].bitcast(I32).rearrange("p (u t j e) -> p u t j e", t=4, j=16, e=e),
+                    src[:].bitcast(I32).rearrange("p (u j t e) -> p u t j e", t=4, j=16, e=e),
+                )
 
         def gather_page(m):
-            nc.vector.tensor_copy(picked[m][:], page[m][:].indirect(offsets[:]))
+            for s in range(2):
+                nc.vector.tensor_copy(picked[m, s], page[m][:].indirect(half_list(s)))
 
-        def first_products(g, s):
+        def product_b(g, s, bank0):
+            entries = slice(HALF * s, HALF * (s + 1))
+            for a in range(2):
+                for t in range(4):
+                    col0 = H * a + PASS * g + P * t
+                    nc.tensor.matmul_mx(
+                        banks[bank0 + t][:], w4_codes[:, 2 * col0 : 2 * (col0 + P)].bitcast(FP4X4),
+                        w4_sc[:, col0 : col0 + P],
+                        v_words[a, s][:].bitcast(FP8X4), v_sc[a][:, entries], start=(a == 0), stop=(a == 1),
+                    )
+            for t in range(4):
+                nc.scalar.activation(b_sb[g, s, t], banks[bank0 + t][:], ACT.Identity, bias=bias[:, t, 2 + g : 3 + g])
+
+        def product_a(g, s, bank0):
             entries = slice(HALF * s, HALF * (s + 1))
             for t in range(4):
-                bank_a, bank_b = banks[2 * t], banks[2 * t + 1]
                 cols = slice(P * t, P * (t + 1))
                 for a in range(2):
                     nc.tensor.matmul_mx(
-                        bank_a[:], w1_codes[a, g][:, cols].bitcast(FP8X4), w1_sc[a, g][:, cols],
+                        banks[bank0 + t][:], w1_codes[a, g][:, cols].bitcast(FP8X4), w1_sc[a, g][:, cols],
                         v_words[a, s][:].bitcast(FP8X4), v_sc[a][:, entries], start=(a == 0), stop=(a == 1),
                     )
-                for a in range(2):
-                    word0 = PASS * a + P * t
-                    scale0 = H * a + PASS * g + P * t
-                    nc.tensor.matmul_mx(
-                        bank_b[:], w4_codes[g][:, 2 * word0 : 2 * (word0 + P)].bitcast(FP4X4),
-                        w4_sc[:, scale0 : scale0 + P],
-                        v_words[a, s][:].bitcast(FP8X4), v_sc[a][:, entries], start=(a == 0), stop=(a == 1),
-                    )
-                nc.scalar.activation(a_sb[t][:], bank_a[:], ACT.Identity, bias=bias[:, t, g : g + 1])
                 nc.vector.scalar_tensor_tensor(
-                    h_rows[g, s][:, t, :], bank_b[:], bias[:, t, 2 + g : 3 + g], a_sb[t][:], ALU.add, ALU.max
+                    h_rows[g, s][:, t, :], banks[bank0 + t][:], bias[:, t, g : g + 1], b_sb[g, s, t],
+                    ALU.add, ALU.max,
                 )
 
-        def quantise_h(g, s):
-            dst = h_bf[g, s][:].rearrange("p (c i t) -> p c t i", i=2, t=4)
-            src = h_rows[g, s][:].rearrange("p t (c i) -> p c t i", i=2)
-            for u in range(2):
-                part = slice(HALF // 4 * u, HALF // 4 * (u + 1))
-                nc.scalar.copy(dst[:, part], src[:, part])
-            nc.vector.quantize_mx(h_codes[g, s][:].bitcast(FP8X4), h_sc[g, s][:], h_bf[g, s][:])
+        def rounded_b(g, bank_ids):
+            for t in range(4):
+                for a in range(2):
+                    col0 = H * a + PASS * g + P * t
+                    nc.tensor.matmul_mx(
+                        banks[bank_ids[t]][:], w4_codes[:, 2 * col0 : 2 * (col0 + P)].bitcast(FP4X4),
+                        w4_sc[:, col0 : col0 + P],
+                        v_words[a, 1][:].bitcast(FP8X4), v_sc[a][:, HALF:S], start=(a == 0), stop=(a == 1),
+                    )
+                nc.scalar.activation(
+                    b_bf[g][:, HALF * t : HALF * (t + 1)], banks[bank_ids[t]][:], ACT.Identity,
+                    bias=bias[:, t, 2 + g : 3 + g],
+                )
 
-        def quantise_w2():
+        def rounded_a(g):
+            for t in range(4):
+                cols = slice(P * t, P * (t + 1))
+                for a in range(2):
+                    nc.tensor.matmul_mx(
+                        banks[t][:], w1_codes[a, g][:, cols].bitcast(FP8X4), w1_sc[a, g][:, cols],
+                        v_words[a, 1][:].bitcast(FP8X4), v_sc[a][:, HALF:S], start=(a == 0), stop=(a == 1),
+                    )
+                nc.scalar.activation(
+                    a_bf[g][:, HALF * t : HALF * (t + 1)], banks[t][:], ACT.Identity, bias=bias[:, t, g : g + 1]
+                )
+
+        def rounded_max(g):
+            nc.vector.tensor_tensor(h_rows[g, 1].rearrange("p t c -> p (t c)"), a_bf[g], b_bf[g], ALU.max)
+
+        def weave_h(g, s):
+            dst = h_bf[g, s].rearrange("p (c i t) -> p c t i", i=4, t=4)
+            src = h_rows[g, s].rearrange("p t (c i) -> p c t i", i=4)
+            nc.scalar.copy(dst, src)
+
+        def quant_h(g, s):
+            nc.vector.quantize_mx(h_codes[g, s][:].bitcast(FP8X4), h_sc[g, s][:], h_bf[g, s])
+
+        def cast_w2():
             for g in range(2):
                 nc.scalar.copy(
-                    w2_bf[:, 4 * N * g : 4 * N * (g + 1)].rearrange("p (c i t) -> p c t i", i=2, t=4),
-                    w2_raw[g][:].rearrange("p t (c i) -> p c t i", i=2),
+                    w2_bf[:, 4 * N * g : 4 * N * (g + 1)].rearrange("p (c i t) -> p c t i", i=4, t=4),
+                    w2_raw[g][:].rearrange("p t (c i) -> p c t i", i=4),
                 )
+
+        def quant_w2():
             for lo, hi in ((0, 512), (512, 2 * N)):
                 nc.vector.quantize_mx(w2_codes[:, lo:hi].bitcast(FP8X4), w2_sc[:, lo:hi], w2_bf[:, 4 * lo : 4 * hi])
 
         def third_product(m, s):
-            bank_y = banks[3 * s + m]
+            bank_y = banks[5 + m]
             for g in range(2):
                 cols = slice(N * g + P * m, N * g + P * (m + 1))
                 nc.tensor.matmul_mx(
@@ -230,7 +254,7 @@ def tile_list_marathon_split_caps_kernel(
                     h_codes[g, s][:].bitcast(FP8X4), h_sc[g, s][:], start=(g == 0), stop=(g == 1),
                 )
             nc.vector.scalar_tensor_tensor(
-                capped[m, s], bank_y[:], b2_col[:, m : m + 1], picked[m][:, HALF * s : HALF * (s + 1)],
+                capped[m, s], bank_y[:], b2_col[:, m : m + 1], picked[m, s],
                 ALU.add, ALU.min,
             )
 
@@ -238,47 +262,45 @@ def tile_list_marathon_split_caps_kernel(
             nc.vector.tensor_copy(page[m][:].indirect(half_list(s)), capped[m, s])
 
         gather_words(0, 0)
+        order_w4()
+        v_words[0, 1] = sb("v_words01", [P, HALF], U32, tag="w4_sc_raw")
         gather_words(0, 1)
-        cast_w1(0, 0, 0, copy_by_activation)
-        cast_w1(0, 0, 1, nc.scalar.copy)
-        for t in range(4):
-            nc.tensor.transpose(banks[7][:, P * t : P * (t + 1)], bias_rows[:, P * t : P * (t + 1)], ident[:])
-        nc.scalar.copy(bias[:], banks[7][:].rearrange("p (t c) -> p t c", t=4)[:, :, 0:4])
-        quant_w1(0, 0, 0)
-        quant_w1(0, 0, 1)
         gather_words(1, 0)
-        order_w4_scales()
-        cast_w1(1, 0, 0, nc.scalar.copy)
-        cast_w1(1, 0, 1, nc.scalar.copy)
-        quant_w1(1, 0, 0)
-        order_w4_words(0)
-        quant_w1(1, 0, 1)
         gather_words(1, 1)
-
-        for s in range(2):
-            first_products(0, s)
-            for u in range(2):
-                cast_w1(s, 1, u, nc.scalar.copy)
-                quant_w1(s, 1, u)
-        order_w4_words(1)
+        product_b(0, 0, 0)
+        product_b(1, 0, 4)
+        for a, g in ag_pairs[:3]:
+            cast_w1(a, g, nc.vector.tensor_copy)
+            quant_w1(a, g)
+        product_a(0, 0, 0)
+        cast_w1(1, 1, nc.scalar.copy)
+        quant_w1(1, 1)
         gather_page(0)
-
-        first_products(1, 0)
-        quantise_w2()
-        for g in range(2):
-            quantise_h(g, 0)
-        first_products(1, 1)
+        product_a(1, 0, 4)
+        weave_h(0, 0)
+        quant_h(0, 0)
+        weave_h(1, 0)
+        cast_w2()
+        rounded_b(0, (0, 1, 2, 3))
         gather_page(1)
+        quant_h(1, 0)
+        quant_w2()
+        rounded_b(1, (5, 6, 7, 4))
         gather_page(2)
-
         third_product(0, 0)
         scatter(0, 0)
-        for g in range(2):
-            quantise_h(g, 1)
-        for m in (1, 2):
-            third_product(m, 0)
-        for m in (1, 2):
-            scatter(m, 0)
+        rounded_a(0)
+        rounded_a(1)
+        rounded_max(0)
+        rounded_max(1)
+        weave_h(0, 1)
+        weave_h(1, 1)
+        third_product(1, 0)
+        scatter(1, 0)
+        quant_h(0, 1)
+        quant_h(1, 1)
+        third_product(2, 0)
+        scatter(2, 0)
         for m in range(3):
             third_product(m, 1)
         for m in range(3):

@@ -235,8 +235,8 @@ def tile_list_marathon_split_caps_kernel(
             nc.vector.quantize_mx(h_codes[g, s][:].bitcast(FP8X4), h_sc[g, s][:], h_bf[g, s])
 
         def cast_w2():
-            for g in range(2):
-                nc.scalar.copy(
+            for g, copy in enumerate((nc.scalar.copy, nc.vector.tensor_copy)):
+                copy(
                     w2_bf[:, 4 * N * g : 4 * N * (g + 1)].rearrange("p (c i t) -> p c t i", i=4, t=4),
                     w2_raw[g][:].rearrange("p t (c i) -> p c t i", i=4),
                 )

@@ -153,6 +153,12 @@ def tile_list_marathon_split_caps_kernel(
             for t in range(4):
                 copy(dst[:, t], src[:, t])
 
+        def cast_w1_in_order(a, g):
+            dst = w1_bf[a, g][:].rearrange("p (t j i k) -> p t j i k", t=4, i=8, k=4)
+            src = w1_raw[a, g][:].rearrange("p k (j t i) -> p t j i k", t=4, i=8)
+            for u in range(2):
+                nc.vector.tensor_copy(dst[:, 2 * u : 2 * u + 2], src[:, 2 * u : 2 * u + 2])
+
         def quant_w1(a, g):
             for u in range(2):
                 cols = slice(2 * P * u, 2 * P * (u + 1))
@@ -235,11 +241,13 @@ def tile_list_marathon_split_caps_kernel(
             nc.vector.quantize_mx(h_codes[g, s][:].bitcast(FP8X4), h_sc[g, s][:], h_bf[g, s])
 
         def cast_w2():
-            for g, copy in enumerate((nc.scalar.copy, nc.vector.tensor_copy)):
-                copy(
-                    w2_bf[:, 4 * N * g : 4 * N * (g + 1)].rearrange("p (c i t) -> p c t i", i=4, t=4),
-                    w2_raw[g][:].rearrange("p t (c i) -> p c t i", i=4),
-                )
+            nc.scalar.copy(
+                w2_bf[:, 0 : 4 * N].rearrange("p (c i t) -> p c t i", i=4, t=4),
+                w2_raw[0][:].rearrange("p t (c i) -> p c t i", i=4),
+            )
+            nc.vector.tensor_copy(
+                w2_bf[:, 4 * N : 8 * N].rearrange("p (c t) -> p c t", t=4), w2_raw[1][:].rearrange("p t c -> p c t")
+            )
 
         def quant_w2():
             for lo, hi in ((0, 512), (512, 2 * N)):
@@ -270,7 +278,7 @@ def tile_list_marathon_split_caps_kernel(
         product_b(0, 0, 0)
         product_b(1, 0, 4)
         for a, g in ag_pairs[:3]:
-            cast_w1(a, g, nc.vector.tensor_copy)
+            cast_w1_in_order(a, g)
             quant_w1(a, g)
         product_a(0, 0, 0)
         cast_w1(1, 1, nc.scalar.copy)

@@ -44,8 +44,7 @@ def tile_list_marathon_split_caps_kernel(
         v_sc = [sb(f"v_sc{a}", [P, S], U8) for a in range(2)]
         bias_rows = sb("bias_rows", [P, PASS], F32)
         bias_raw = sb("bias_raw", [4, PASS], F32)
-        bias = sb("bias", [P, 4, 4], F32)
-        b2_col = sb("b2_col", [P, 3], F32)
+        bias = sb("bias", [P, 4, 5], F32)
         ident = sb("ident", [P, P], F32)
         w4_sc_raw = sb("w4_sc_raw", [P, 2 * H], U8)
         w4_sc = sb("w4_sc", [P, 2 * H], U8)
@@ -55,27 +54,27 @@ def tile_list_marathon_split_caps_kernel(
         v_words = {(a, s): sb(f"v_words{a}{s}", [P, HALF], U32) for a, s in ((0, 0), (1, 0), (1, 1))}
         w1_raw = {(a, g): sb(f"w1_raw{a}{g}", [P, 4, PASS], F32) for a, g in ag_pairs}
         w1_bf = {(a, g): sb(f"w1_bf{a}{g}", [P, 4 * PASS], BF16) for a, g in ag_pairs}
-        w1_codes = {(a, g): sb(f"w1_codes{a}{g}", [P, PASS], U32) for a, g in ag_pairs}
+        w1_codes = {(a, g): sb(f"w1_codes{a}{g}", [P, PASS], U32)[:] for a, g in ag_pairs if (a, g) != (0, 1)}
         w1_sc = {(a, g): sb(f"w1_sc{a}{g}", [P, PASS], U8) for a, g in ag_pairs}
         w2_raw = [sb(f"w2_raw{g}", [P, 4, N], F32) for g in range(2)]
         w2_bf = sb("w2_bf", [P, 2 * 4 * N], BF16)
         w2_codes = sb("w2_codes", [P, 2 * N], U32)
         w2_sc = sb("w2_sc", [P, 2 * N], U8)
         page = [sb(f"page{m}", [P, T], F32) for m in range(3)]
-        picked = {(m, s): sb(f"picked{m}{s}", [P, HALF], F32)[:] for m in range(3) for s in range(2) if (m, s) != (2, 1)}
-        picked[2, 1] = w2_bf[:].bitcast(F32)[:, 2 * HALF : 3 * HALF]
-        b_sb = {(g, 0, t): sb(f"b_sb{g}0{t}", [P, HALF], F32)[:] for g in range(2) for t in range(4)}
-        h_rows = {(g, s): sb(f"h_rows{g}{s}", [P, 4, HALF], BF16)[:] for g, s in gs_pairs[1:]}
-        h_rows[0, 0] = w1_bf[0, 1][:].rearrange("p (t c) -> p t c", t=4)
+        picked = {(m, s): sb(f"picked{m}{s}", [P, HALF], F32)[:] for m in range(3) for s in range(2) }
+        b_sb = {(0, 0, t): sb(f"b_sb{t}", [P, HALF], F32)[:] for t in range(4)}
+        for t in range(4):
+            b_sb[1, 0, t] = w1_raw[0, 1][:, t, :]
+        h_rows = {(g, s): sb(f"h_rows{g}{s}", [P, 4, HALF], BF16)[:] for g, s in gs_pairs}
         a_bf = [w2_bf[:, 0 : 4 * HALF], sb("a_bf1", [P, 4 * HALF], BF16)[:]]
-        b_bf = [w1_bf[0, 1][:], w2_raw[1][:].rearrange("p t n -> p (t n)").bitcast(BF16)[:, 0 : 4 * HALF]]
+        b_bf = [h_rows[1, 0].rearrange("p t c -> p (t c)"), w1_bf[0, 0][:]]
         woven = [sb(f"woven{i}", [P, 4 * HALF], BF16) for i in range(2)]
         h_codes = {(g, s): sb(f"h_codes{g}{s}", [P, HALF], U32) for g, s in gs_pairs}
         h_sc = {(g, s): sb(f"h_sc{g}{s}", [P, HALF], U8) for g, s in gs_pairs}
         banks = [psum.tile([P, HALF], F32, name=f"bank{b}") for b in range(8)]
 
         h_bf = {(g, s): woven[g][:] for g, s in gs_pairs}
-        h_bf[0, 0] = w1_raw[1, 1][:].rearrange("p k c -> p (k c)").bitcast(BF16)[:, 0 : 4 * HALF]
+        h_bf[1, 0] = w2_raw[1][:].rearrange("p t n -> p (t n)").bitcast(BF16)[:, 0 : 4 * HALF]
         capped = {(m, 1): b_sb[0, 0, m] for m in range(3)}
         capped[0, 0] = b_sb[0, 0, 3]
         capped[1, 0] = a_bf[1].bitcast(F32)[:, 0:HALF]
@@ -89,6 +88,8 @@ def tile_list_marathon_split_caps_kernel(
         nc.scalar.activation(
             bias_rows[:].rearrange("p (t c) -> p t c", t=4), ident[:].unsqueeze(1).to_broadcast([P, 4, P]), ACT.Identity, scale=0.0
         )
+
+        nc.gpsimd.dma_start(bias_rows[4:5, 0:N], b2.rearrange("(o c) -> o c", o=1))
 
         def load_table(a):
             nc.sync.dma_start(tab_w[a][:].bitcast(I32), tab_words[a].rearrange("p t i -> p (t i)").bitcast(I32))
@@ -126,11 +127,9 @@ def tile_list_marathon_split_caps_kernel(
             load_w1(a, g)
         load_page(0)
         load_w2(0)
+        load_w2(1)
         load_page(1)
         load_page(2)
-        load_w2(1)
-        with nc.allow_non_contiguous_dma(reason="one value of b2 to a partition"):
-            nc.sync.dma_start(b2_col[:], b2.rearrange("(m p) -> p m", p=P))
 
         nc.scalar.activation(
             bias_rows[0:4, :].rearrange("v (t j i) -> v t j i", t=4, i=8),
@@ -139,7 +138,7 @@ def tile_list_marathon_split_caps_kernel(
         )
         for t in range(4):
             nc.tensor.transpose(banks[7][:, P * t : P * (t + 1)], bias_rows[:, P * t : P * (t + 1)], ident[:])
-        nc.scalar.copy(bias[:], banks[7][:].rearrange("p (t c) -> p t c", t=4)[:, :, 0:4])
+        nc.scalar.copy(bias[:], banks[7][:].rearrange("p (t c) -> p t c", t=4)[:, :, 0:5])
 
         def half_list(s):
             return offsets[:, HALF // 16 * s : HALF // 16 * (s + 1)]
@@ -186,6 +185,8 @@ def tile_list_marathon_split_caps_kernel(
                         w4_sc[:, col0 : col0 + P],
                         v_words[a, s][:].bitcast(FP8X4), v_sc[a][:, entries], start=(a == 0), stop=(a == 1),
                     )
+
+        def copy_b(g, s, bank0):
             for t in range(4):
                 nc.scalar.activation(b_sb[g, s, t], banks[bank0 + t][:], ACT.Identity, bias=bias[:, t, 2 + g : 3 + g])
 
@@ -217,16 +218,16 @@ def tile_list_marathon_split_caps_kernel(
                     bias=bias[:, t, 2 + g : 3 + g],
                 )
 
-        def rounded_a(g):
+        def rounded_a(g, bank_ids):
             for t in range(4):
                 cols = slice(P * t, P * (t + 1))
                 for a in range(2):
                     nc.tensor.matmul_mx(
-                        banks[t][:], w1_codes[a, g][:, cols].bitcast(FP8X4), w1_sc[a, g][:, cols],
+                        banks[bank_ids[t]][:], w1_codes[a, g][:, cols].bitcast(FP8X4), w1_sc[a, g][:, cols],
                         v_words[a, 1][:].bitcast(FP8X4), v_sc[a][:, HALF:S], start=(a == 0), stop=(a == 1),
                     )
                 nc.scalar.activation(
-                    a_bf[g][:, HALF * t : HALF * (t + 1)], banks[t][:], ACT.Identity, bias=bias[:, t, g : g + 1]
+                    a_bf[g][:, HALF * t : HALF * (t + 1)], banks[bank_ids[t]][:], ACT.Identity, bias=bias[:, t, g : g + 1]
                 )
 
         def rounded_max(g):
@@ -245,8 +246,9 @@ def tile_list_marathon_split_caps_kernel(
                 w2_bf[:, 0 : 4 * N].rearrange("p (c i t) -> p c t i", i=4, t=4),
                 w2_raw[0][:].rearrange("p t (c i) -> p c t i", i=4),
             )
-            nc.vector.tensor_copy(
-                w2_bf[:, 4 * N : 8 * N].rearrange("p (c t) -> p c t", t=4), w2_raw[1][:].rearrange("p t c -> p c t")
+            nc.scalar.copy(
+                w2_bf[:, 4 * N : 8 * N].rearrange("p (c i t) -> p c t i", i=4, t=4),
+                w2_raw[1][:].rearrange("p t (c i) -> p c t i", i=4),
             )
 
         def quant_w2():
@@ -254,7 +256,7 @@ def tile_list_marathon_split_caps_kernel(
                 nc.vector.quantize_mx(w2_codes[:, lo:hi].bitcast(FP8X4), w2_sc[:, lo:hi], w2_bf[:, 4 * lo : 4 * hi])
 
         def third_product(m, s):
-            bank_y = banks[5 + m]
+            bank_y = banks[4 + m]
             for g in range(2):
                 cols = slice(N * g + P * m, N * g + P * (m + 1))
                 nc.tensor.matmul_mx(
@@ -262,7 +264,7 @@ def tile_list_marathon_split_caps_kernel(
                     h_codes[g, s][:].bitcast(FP8X4), h_sc[g, s][:], start=(g == 0), stop=(g == 1),
                 )
             nc.vector.scalar_tensor_tensor(
-                capped[m, s], bank_y[:], b2_col[:, m : m + 1], picked[m, s],
+                capped[m, s], bank_y[:], bias[:, m, 4:5], picked[m, s],
                 ALU.add, ALU.min,
             )
 
@@ -277,28 +279,33 @@ def tile_list_marathon_split_caps_kernel(
         gather_words(1, 1)
         product_b(0, 0, 0)
         product_b(1, 0, 4)
-        for a, g in ag_pairs[:3]:
-            cast_w1_in_order(a, g)
-            quant_w1(a, g)
+        copy_b(0, 0, 0)
+        for a in range(2):
+            cast_w1_in_order(a, 0)
+            quant_w1(a, 0)
         product_a(0, 0, 0)
-        cast_w1(1, 1, nc.scalar.copy)
+        cast_w1(0, 1, nc.scalar.copy)
+        copy_b(1, 0, 4)
+        cast_w1_in_order(1, 1)
         quant_w1(1, 1)
+        w1_codes[0, 1] = sb("w1_codes01", [P, PASS], U32, tag="w1_raw11")[:]
+        quant_w1(0, 1)
         gather_page(0)
         product_a(1, 0, 4)
         weave_h(0, 0)
         quant_h(0, 0)
-        weave_h(1, 0)
         cast_w2()
-        rounded_b(0, (0, 1, 2, 3))
+        quant_w2()
+        weave_h(1, 0)
         gather_page(1)
         quant_h(1, 0)
-        quant_w2()
-        rounded_b(1, (5, 6, 7, 4))
         gather_page(2)
+        rounded_b(0, (0, 1, 2, 3))
+        rounded_a(0, (4, 5, 6, 7))
         third_product(0, 0)
         scatter(0, 0)
-        rounded_a(0)
-        rounded_a(1)
+        rounded_b(1, (0, 1, 2, 3))
+        rounded_a(1, (7, 0, 1, 2))
         rounded_max(0)
         rounded_max(1)
         weave_h(0, 1)

@@ -49,12 +49,12 @@ def tile_list_marathon_split_caps_kernel(
         w4_sc_raw = sb("w4_sc_raw", [P, 2 * H], U8)
         w4_sc = sb("w4_sc", [P, 2 * H], U8)
         w4_raw = sb("w4_raw", [P, 4 * H], U8)
-        w4_codes = sb("w4_codes", [P, 4 * H], U8)
+        w4_codes = [sb("w4_codes0", [P, 2 * H], U8)]
         tab_w = [sb(f"tab_w{a}", [P, T], U32) for a in range(2)]
         v_words = {(a, s): sb(f"v_words{a}{s}", [P, HALF], U32) for a, s in ((0, 0), (1, 0), (1, 1))}
         w1_raw = {(a, g): sb(f"w1_raw{a}{g}", [P, 4, PASS], F32) for a, g in ag_pairs}
         w1_bf = {(a, g): sb(f"w1_bf{a}{g}", [P, 4 * PASS], BF16) for a, g in ag_pairs}
-        w1_codes = {(a, g): sb(f"w1_codes{a}{g}", [P, PASS], U32)[:] for a, g in ag_pairs if (a, g) != (0, 1)}
+        w1_codes = {(a, g): sb(f"w1_codes{a}{g}", [P, PASS], U32)[:] for a, g in ag_pairs}
         w1_sc = {(a, g): sb(f"w1_sc{a}{g}", [P, PASS], U8) for a, g in ag_pairs}
         w2_raw = [sb(f"w2_raw{g}", [P, 4, N], F32) for g in range(2)]
         w2_bf = sb("w2_bf", [P, 2 * 4 * N], BF16)
@@ -64,16 +64,18 @@ def tile_list_marathon_split_caps_kernel(
         picked = {(m, s): sb(f"picked{m}{s}", [P, HALF], F32)[:] for m in range(3) for s in range(2) }
         b_sb = {(0, 0, t): sb(f"b_sb{t}", [P, HALF], F32)[:] for t in range(4)}
         for t in range(4):
-            b_sb[1, 0, t] = w1_raw[0, 1][:, t, :]
-        h_rows = {(g, s): sb(f"h_rows{g}{s}", [P, 4, HALF], BF16)[:] for g, s in gs_pairs}
-        a_bf = [w2_bf[:, 0 : 4 * HALF], sb("a_bf1", [P, 4 * HALF], BF16)[:]]
-        b_bf = [h_rows[1, 0].rearrange("p t c -> p (t c)"), w1_bf[0, 0][:]]
+            b_sb[1, 0, t] = sb(f"b_sb1{t}", [P, HALF], F32)[:]
+        h_rows = {(g, s): sb(f"h_rows{g}{s}", [P, 4, HALF], BF16)[:] for g, s in gs_pairs[1:]}
+        h_rows[0, 0] = w1_bf[0, 1][:].rearrange("p (t c) -> p t c", t=4)
+        a_bf = [h_rows[1, 0].rearrange("p t c -> p (t c)"), w1_bf[1, 0][:]]
+        b_bf = [w1_bf[0, 0][:], w2_bf[:, 0 : 4 * HALF]]
         woven = [sb(f"woven{i}", [P, 4 * HALF], BF16) for i in range(2)]
         h_codes = {(g, s): sb(f"h_codes{g}{s}", [P, HALF], U32) for g, s in gs_pairs}
         h_sc = {(g, s): sb(f"h_sc{g}{s}", [P, HALF], U8) for g, s in gs_pairs}
         banks = [psum.tile([P, HALF], F32, name=f"bank{b}") for b in range(8)]
 
         h_bf = {(g, s): woven[g][:] for g, s in gs_pairs}
+        h_bf[0, 0] = w1_raw[1, 1][:].rearrange("p k c -> p (k c)").bitcast(BF16)[:, 0 : 4 * HALF]
         h_bf[1, 0] = w2_raw[1][:].rearrange("p t n -> p (t n)").bitcast(BF16)[:, 0 : 4 * HALF]
         capped = {(m, 1): b_sb[0, 0, m] for m in range(3)}
         capped[0, 0] = b_sb[0, 0, 3]
@@ -164,12 +166,17 @@ def tile_list_marathon_split_caps_kernel(
                 values = w1_bf[a, g][:, 8 * P * u : 8 * P * (u + 1)]
                 nc.vector.quantize_mx(w1_codes[a, g][:, cols].bitcast(FP8X4), w1_sc[a, g][:, cols], values)
 
-        def order_w4():
-            for dst, src, e in ((w4_sc, w4_sc_raw, 2), (w4_codes, w4_raw, 4)):
-                nc.vector.tensor_copy(
-                    dst[:].bitcast(I32).rearrange("p (u t j e) -> p u t j e", t=4, j=16, e=e),
-                    src[:].bitcast(I32).rearrange("p (u j t e) -> p u t j e", t=4, j=16, e=e),
-                )
+        def order_w4_scales():
+            nc.vector.tensor_copy(
+                w4_sc[:].bitcast(I32).rearrange("p (u t j e) -> p u t j e", t=4, j=16, e=2),
+                w4_sc_raw[:].bitcast(I32).rearrange("p (u j t e) -> p u t j e", t=4, j=16, e=2),
+            )
+
+        def order_w4_words(g):
+            nc.vector.tensor_copy(
+                w4_codes[g][:].bitcast(I32).rearrange("p (a t j e) -> p a t j e", t=4, j=16, e=4),
+                w4_raw[:].bitcast(I32).rearrange("p (a g j t e) -> p g a t j e", g=2, t=4, j=16, e=4)[:, g],
+            )
 
         def gather_page(m):
             for s in range(2):
@@ -181,7 +188,7 @@ def tile_list_marathon_split_caps_kernel(
                 for t in range(4):
                     col0 = H * a + PASS * g + P * t
                     nc.tensor.matmul_mx(
-                        banks[bank0 + t][:], w4_codes[:, 2 * col0 : 2 * (col0 + P)].bitcast(FP4X4),
+                        banks[bank0 + t][:], w4_codes[g][:, 2 * (PASS * a + P * t) : 2 * (PASS * a + P * (t + 1))].bitcast(FP4X4),
                         w4_sc[:, col0 : col0 + P],
                         v_words[a, s][:].bitcast(FP8X4), v_sc[a][:, entries], start=(a == 0), stop=(a == 1),
                     )
@@ -209,7 +216,7 @@ def tile_list_marathon_split_caps_kernel(
                 for a in range(2):
                     col0 = H * a + PASS * g + P * t
                     nc.tensor.matmul_mx(
-                        banks[bank_ids[t]][:], w4_codes[:, 2 * col0 : 2 * (col0 + P)].bitcast(FP4X4),
+                        banks[bank_ids[t]][:], w4_codes[g][:, 2 * (PASS * a + P * t) : 2 * (PASS * a + P * (t + 1))].bitcast(FP4X4),
                         w4_sc[:, col0 : col0 + P],
                         v_words[a, 1][:].bitcast(FP8X4), v_sc[a][:, HALF:S], start=(a == 0), stop=(a == 1),
                     )
@@ -272,26 +279,27 @@ def tile_list_marathon_split_caps_kernel(
             nc.vector.tensor_copy(page[m][:].indirect(half_list(s)), capped[m, s])
 
         gather_words(0, 0)
-        order_w4()
+        order_w4_scales()
+        order_w4_words(0)
         v_words[0, 1] = sb("v_words01", [P, HALF], U32, tag="w4_sc_raw")
         gather_words(0, 1)
         gather_words(1, 0)
         gather_words(1, 1)
+        w4_codes.append(sb("w4_codes1", [P, 2 * H], U8, tag="tab_w1"))
+        order_w4_words(1)
         product_b(0, 0, 0)
-        product_b(1, 0, 4)
         copy_b(0, 0, 0)
-        for a in range(2):
-            cast_w1_in_order(a, 0)
-            quant_w1(a, 0)
-        product_a(0, 0, 0)
-        cast_w1(0, 1, nc.scalar.copy)
+        product_b(1, 0, 4)
         copy_b(1, 0, 4)
-        cast_w1_in_order(1, 1)
+        for a, g in ag_pairs[:3]:
+            cast_w1_in_order(a, g)
+            quant_w1(a, g)
+        rounded_b(0, (0, 1, 2, 3))
+        product_a(0, 0, 4)
+        cast_w1(1, 1, nc.scalar.copy)
         quant_w1(1, 1)
-        w1_codes[0, 1] = sb("w1_codes01", [P, PASS], U32, tag="w1_raw11")[:]
-        quant_w1(0, 1)
         gather_page(0)
-        product_a(1, 0, 4)
+        product_a(1, 0, 0)
         weave_h(0, 0)
         quant_h(0, 0)
         cast_w2()
@@ -300,7 +308,6 @@ def tile_list_marathon_split_caps_kernel(
         gather_page(1)
         quant_h(1, 0)
         gather_page(2)
-        rounded_b(0, (0, 1, 2, 3))
         rounded_a(0, (4, 5, 6, 7))
         third_product(0, 0)
         scatter(0, 0)

@@ -48,7 +48,7 @@ def tile_list_marathon_split_caps_kernel(
         ident = sb("ident", [P, P], F32)
         w4_sc_raw = sb("w4_sc_raw", [P, 2 * H], U8)
         w4_sc = sb("w4_sc", [P, 2 * H], U8)
-        w4_raw = sb("w4_raw", [P, 4 * H], U8)
+        w4_raw = [sb(f"w4_raw{g}", [P, 2 * H], U8) for g in range(2)]
         w4_codes = [sb("w4_codes0", [P, 2 * H], U8)]
         tab_w = [sb(f"tab_w{a}", [P, T], U32) for a in range(2)]
         v_words = {(a, s): sb(f"v_words{a}{s}", [P, HALF], U32) for a, s in ((0, 0), (1, 0), (1, 1))}
@@ -75,7 +75,6 @@ def tile_list_marathon_split_caps_kernel(
         banks = [psum.tile([P, HALF], F32, name=f"bank{b}") for b in range(8)]
 
         h_bf = {(g, s): woven[g][:] for g, s in gs_pairs}
-        h_bf[0, 0] = w1_raw[1, 1][:].rearrange("p k c -> p (k c)").bitcast(BF16)[:, 0 : 4 * HALF]
         h_bf[1, 0] = w2_raw[1][:].rearrange("p t n -> p (t n)").bitcast(BF16)[:, 0 : 4 * HALF]
         capped = {(m, 1): b_sb[0, 0, m] for m in range(3)}
         capped[0, 0] = b_sb[0, 0, 3]
@@ -84,13 +83,15 @@ def tile_list_marathon_split_caps_kernel(
 
         nc.sync.dma_start(offsets[:], offs)
         nc.gpsimd.memset(tab_sc[:].bitcast(I32), 0)
-        nc.vector.memset(w4_sc_raw[:].bitcast(I32), 0)
-        nc.vector.memset(v_sc[1][3 * QUAD : P, :].bitcast(I32), 0)
-        make_identity(nc, ident[:])
+        nc.vector.memset(bias_rows[:, 0:P], 0.0)
         nc.scalar.activation(
-            bias_rows[:].rearrange("p (t c) -> p t c", t=4), ident[:].unsqueeze(1).to_broadcast([P, 4, P]), ACT.Identity, scale=0.0
+            bias_rows[:, P:PASS].rearrange("p (t c) -> p t c", t=3),
+            bias_rows[:, 0:P].unsqueeze(1).to_broadcast([P, 3, P]),
+            ACT.Identity,
         )
-
+        nc.vector.memset(w4_sc_raw[:].bitcast(I32), 0)
+        nc.vector.memset(v_sc[1][:].bitcast(I32), 0)
+        make_identity(nc, ident[:])
         nc.gpsimd.dma_start(bias_rows[4:5, 0:N], b2.rearrange("(o c) -> o c", o=1))
 
         def load_table(a):
@@ -99,6 +100,12 @@ def tile_list_marathon_split_caps_kernel(
         def load_w1(a, g):
             block = w1[PASS * a : PASS * (a + 1), PASS * g : PASS * (g + 1)]
             nc.sync.dma_start(w1_raw[a, g][:], block.rearrange("(p j) c -> p j c", j=4))
+
+        def load_w4(g):
+            nc.sync.dma_start(
+                w4_raw[g][:].bitcast(I32).rearrange("p (a c) -> p a c", a=2),
+                w4_words[:, :, H * g : H * (g + 1)].bitcast(I32).rearrange("a p c -> p a c"),
+            )
 
         def load_page(m):
             nc.sync.dma_start(page[m][:], gT[P * m : P * (m + 1), :])
@@ -113,18 +120,16 @@ def tile_list_marathon_split_caps_kernel(
         for r in range(4):
             nc.sync.dma_start(tab_sc[r:P:SHIFT, :].bitcast(I32), tab_rows[r])
         load_table(0)
-        nc.sync.dma_start(
-            w4_raw[:].bitcast(I32).rearrange("p (a c) -> p a c", a=2), w4_words.bitcast(I32).rearrange("a p c -> p a c")
-        )
-        for q in range(4):
-            nc.sync.dma_start(
-                w4_sc_raw[QUAD * q : QUAD * q + 4, :].bitcast(I32).rearrange("r (a c) -> r a c", a=2),
-                w4_scales[:, 4 * q : 4 * q + 4, :].bitcast(I32).rearrange("a r c -> r a c"),
-            )
+        load_w4(0)
+        w4_rows = w4_scales.bitcast(I32).rearrange("a (q r) c -> r q a c", r=4)
+        for r in range(4):
+            nc.sync.dma_start(w4_sc_raw[r:P:QUAD, :].bitcast(I32).rearrange("q (a c) -> q a c", a=2), w4_rows[r])
         nc.sync.dma_start(bias_raw[0:2, :], b1.rearrange("(g c) -> g c", g=2))
         load_table(1)
         nc.vector.tensor_copy(v_sc[0][:], tab_sc[:].indirect(offsets[:]))
-        nc.sync.dma_start(v_sc[1][0:SPAN, :].bitcast(I32), v_sc[0][SHIFT : SHIFT + SPAN, :].bitcast(I32))
+        for r in range(4):
+            nc.sync.dma_start(v_sc[1][r:P:QUAD, :].bitcast(I32), v_sc[0][SHIFT + r : P : QUAD, :].bitcast(I32))
+        load_w4(1)
         for a, g in ag_pairs:
             load_w1(a, g)
         load_page(0)
@@ -136,7 +141,7 @@ def tile_list_marathon_split_caps_kernel(
         nc.scalar.activation(
             bias_rows[0:4, :].rearrange("v (t j i) -> v t j i", t=4, i=8),
             bias_raw[:].rearrange("v (j t i) -> v t j i", t=4, i=8),
-            ACT.Copy,
+            ACT.Identity,
         )
         for t in range(4):
             nc.tensor.transpose(banks[7][:, P * t : P * (t + 1)], bias_rows[:, P * t : P * (t + 1)], ident[:])
@@ -148,16 +153,16 @@ def tile_list_marathon_split_caps_kernel(
         def gather_words(a, s):
             nc.vector.tensor_copy(v_words[a, s][:], tab_w[a][:].indirect(half_list(s)))
 
-        def cast_w1(a, g, copy):
+        def cast_w1(a, g, copy, tiles):
             dst = w1_bf[a, g][:].rearrange("p (t j e i k) -> p t j e k i", t=4, e=2, i=4, k=4)
             src = w1_raw[a, g][:].rearrange("p k (j t e i) -> p t j e k i", t=4, e=2, i=4)
-            for t in range(4):
+            for t in tiles:
                 copy(dst[:, t], src[:, t])
 
-        def cast_w1_in_order(a, g):
+        def cast_w1_in_order(a, g, halves=range(2)):
             dst = w1_bf[a, g][:].rearrange("p (t j i k) -> p t j i k", t=4, i=8, k=4)
             src = w1_raw[a, g][:].rearrange("p k (j t i) -> p t j i k", t=4, i=8)
-            for u in range(2):
+            for u in halves:
                 nc.vector.tensor_copy(dst[:, 2 * u : 2 * u + 2], src[:, 2 * u : 2 * u + 2])
 
         def quant_w1(a, g):
@@ -175,7 +180,7 @@ def tile_list_marathon_split_caps_kernel(
         def order_w4_words(g):
             nc.vector.tensor_copy(
                 w4_codes[g][:].bitcast(I32).rearrange("p (a t j e) -> p a t j e", t=4, j=16, e=4),
-                w4_raw[:].bitcast(I32).rearrange("p (a g j t e) -> p g a t j e", g=2, t=4, j=16, e=4)[:, g],
+                w4_raw[g][:].bitcast(I32).rearrange("p (a j t e) -> p a t j e", t=4, j=16, e=4),
             )
 
         def gather_page(m):
@@ -296,7 +301,8 @@ def tile_list_marathon_split_caps_kernel(
             quant_w1(a, g)
         rounded_b(0, (0, 1, 2, 3))
         product_a(0, 0, 4)
-        cast_w1(1, 1, nc.scalar.copy)
+        cast_w1(1, 1, nc.scalar.copy, (0, 1))
+        cast_w1_in_order(1, 1, (1,))
         quant_w1(1, 1)
         gather_page(0)
         product_a(1, 0, 0)
@@ -310,10 +316,10 @@ def tile_list_marathon_split_caps_kernel(
         gather_page(2)
         rounded_a(0, (4, 5, 6, 7))
         third_product(0, 0)
+        rounded_max(0)
         scatter(0, 0)
         rounded_b(1, (0, 1, 2, 3))
         rounded_a(1, (7, 0, 1, 2))
-        rounded_max(0)
         rounded_max(1)
         weave_h(0, 1)
         weave_h(1, 1)

@@ -44,7 +44,8 @@ def tile_list_marathon_split_caps_kernel(
         v_sc = [sb(f"v_sc{a}", [P, S], U8) for a in range(2)]
         bias_rows = sb("bias_rows", [P, PASS], F32)
         bias_raw = sb("bias_raw", [4, PASS], F32)
-        bias = sb("bias", [P, 4, 5], F32)
+        bias = sb("bias", [P, 4, 4], F32)
+        b2_col = sb("b2_col", [P, 3], F32)
         ident = sb("ident", [P, P], F32)
         w4_sc_raw = sb("w4_sc_raw", [P, 2 * H], U8)
         w4_sc = sb("w4_sc", [P, 2 * H], U8)
@@ -92,7 +93,6 @@ def tile_list_marathon_split_caps_kernel(
         nc.vector.memset(w4_sc_raw[:].bitcast(I32), 0)
         nc.vector.memset(v_sc[1][:].bitcast(I32), 0)
         make_identity(nc, ident[:])
-        nc.gpsimd.dma_start(bias_rows[4:5, 0:N], b2.rearrange("(o c) -> o c", o=1))
 
         def load_table(a):
             nc.sync.dma_start(tab_w[a][:].bitcast(I32), tab_words[a].rearrange("p t i -> p (t i)").bitcast(I32))
@@ -145,7 +145,8 @@ def tile_list_marathon_split_caps_kernel(
         )
         for t in range(4):
             nc.tensor.transpose(banks[7][:, P * t : P * (t + 1)], bias_rows[:, P * t : P * (t + 1)], ident[:])
-        nc.scalar.copy(bias[:], banks[7][:].rearrange("p (t c) -> p t c", t=4)[:, :, 0:5])
+        nc.scalar.copy(bias[:], banks[7][:].rearrange("p (t c) -> p t c", t=4)[:, :, 0:4])
+        nc.gpsimd.dma_start(bias_rows[0:1, 0:N], b2.rearrange("(o c) -> o c", o=1))
 
         def half_list(s):
             return offsets[:, HALF // 16 * s : HALF // 16 * (s + 1)]
@@ -183,8 +184,8 @@ def tile_list_marathon_split_caps_kernel(
                 w4_raw[g][:].bitcast(I32).rearrange("p (a j t e) -> p a t j e", t=4, j=16, e=4),
             )
 
-        def gather_page(m):
-            for s in range(2):
+        def gather_page(m, halves=range(2)):
+            for s in halves:
                 nc.vector.tensor_copy(picked[m, s], page[m][:].indirect(half_list(s)))
 
         def product_b(g, s, bank0):
@@ -276,7 +277,7 @@ def tile_list_marathon_split_caps_kernel(
                     h_codes[g, s][:].bitcast(FP8X4), h_sc[g, s][:], start=(g == 0), stop=(g == 1),
                 )
             nc.vector.scalar_tensor_tensor(
-                capped[m, s], bank_y[:], bias[:, m, 4:5], picked[m, s],
+                capped[m, s], bank_y[:], b2_col[:, m : m + 1], picked[m, s],
                 ALU.add, ALU.min,
             )
 
@@ -301,11 +302,15 @@ def tile_list_marathon_split_caps_kernel(
             quant_w1(a, g)
         rounded_b(0, (0, 1, 2, 3))
         product_a(0, 0, 4)
+        for m in range(3):
+            nc.tensor.transpose(banks[7][:, P * m : P * (m + 1)], bias_rows[:, P * m : P * (m + 1)], ident[:])
+        nc.scalar.copy(b2_col[:], banks[7][:, 0 : 3 * P : P])
         cast_w1(1, 1, nc.scalar.copy, (0, 1))
         cast_w1_in_order(1, 1, (1,))
         quant_w1(1, 1)
-        gather_page(0)
+        gather_page(0, (0,))
         product_a(1, 0, 0)
+        gather_page(0, (1,))
         weave_h(0, 0)
         quant_h(0, 0)
         cast_w2()

@@ -21,8 +21,8 @@ P = 128
 PASS = 512
 HALF = 512
 QUAD = 32
+SHARE = 320
 SHIFT = 16
-SPAN = 3 * QUAD + 4
 
 
 def tile_list_marathon_split_caps_kernel(
@@ -43,7 +43,7 @@ def tile_list_marathon_split_caps_kernel(
         tab_sc = sb("tab_sc", [P, T], U8)
         v_sc = [sb(f"v_sc{a}", [P, S], U8) for a in range(2)]
         bias_rows = sb("bias_rows", [P, PASS], F32)
-        bias_raw = sb("bias_raw", [4, PASS], F32)
+        bias_raw = sb("bias_raw", [2 * QUAD, PASS], F32)
         bias = sb("bias", [P, 4, 4], F32)
         b2_col = sb("b2_col", [P, 3], F32)
         ident = sb("ident", [P, P], F32)
@@ -57,30 +57,40 @@ def tile_list_marathon_split_caps_kernel(
         w1_bf = {(a, g): sb(f"w1_bf{a}{g}", [P, 4 * PASS], BF16) for a, g in ag_pairs}
         w1_codes = {(a, g): sb(f"w1_codes{a}{g}", [P, PASS], U32)[:] for a, g in ag_pairs}
         w1_sc = {(a, g): sb(f"w1_sc{a}{g}", [P, PASS], U8) for a, g in ag_pairs}
-        w2_raw = [sb(f"w2_raw{g}", [P, 4, N], F32) for g in range(2)]
-        w2_bf = sb("w2_bf", [P, 2 * 4 * N], BF16)
+        w2_raw = sb("w2_raw", [P, 2, 4, N], F32)
         w2_codes = sb("w2_codes", [P, 2 * N], U32)
         w2_sc = sb("w2_sc", [P, 2 * N], U8)
         page = [sb(f"page{m}", [P, T], F32) for m in range(3)]
-        picked = {(m, s): sb(f"picked{m}{s}", [P, HALF], F32)[:] for m in range(3) for s in range(2) }
-        b_sb = {(0, 0, t): sb(f"b_sb{t}", [P, HALF], F32)[:] for t in range(4)}
-        for t in range(4):
-            b_sb[1, 0, t] = sb(f"b_sb1{t}", [P, HALF], F32)[:]
-        h_rows = {(g, s): sb(f"h_rows{g}{s}", [P, 4, HALF], BF16)[:] for g, s in gs_pairs[1:]}
-        h_rows[0, 0] = w1_bf[0, 1][:].rearrange("p (t c) -> p t c", t=4)
-        a_bf = [h_rows[1, 0].rearrange("p t c -> p (t c)"), w1_bf[1, 0][:]]
-        b_bf = [w1_bf[0, 0][:], w2_bf[:, 0 : 4 * HALF]]
-        woven = [sb(f"woven{i}", [P, 4 * HALF], BF16) for i in range(2)]
+        b_first = {(g, t): sb(f"b_first{g}{t}", [P, HALF], F32)[:] for g in range(2) for t in range(4)}
+        rows_first = sb("rows_first", [P, 4, HALF], BF16)
+        rows_last = sb("rows_last", [P, 4, HALF], BF16)
+        late = sb("late", [P, 12, HALF], BF16)
+        woven = {gs: sb(f"woven{gs[0]}{gs[1]}", [P, 4 * HALF], BF16) for gs in gs_pairs[1:]}
+        w2_last = sb("w2_last", [P, 8 * P], BF16)
         h_codes = {(g, s): sb(f"h_codes{g}{s}", [P, HALF], U32) for g, s in gs_pairs}
         h_sc = {(g, s): sb(f"h_sc{g}{s}", [P, HALF], U8) for g, s in gs_pairs}
         banks = [psum.tile([P, HALF], F32, name=f"bank{b}") for b in range(8)]
 
-        h_bf = {(g, s): woven[g][:] for g, s in gs_pairs}
-        h_bf[1, 0] = w2_raw[1][:].rearrange("p t n -> p (t n)").bitcast(BF16)[:, 0 : 4 * HALF]
-        capped = {(m, 1): b_sb[0, 0, m] for m in range(3)}
-        capped[0, 0] = b_sb[0, 0, 3]
-        capped[1, 0] = a_bf[1].bitcast(F32)[:, 0:HALF]
-        capped[2, 0] = woven[1][:].bitcast(F32)[:, 0:HALF]
+        def flat(tile):
+            return tile[:].rearrange("p j c -> p (j c)")
+
+        def by_tile(values):
+            return values.rearrange("p (t c) -> p t c", t=4)
+
+        h_rows = {(0, 0): by_tile(w1_bf[0, 1][:]), (1, 0): rows_first[:], (0, 1): late[:, 8:12, :], (1, 1): rows_last[:]}
+        h_bf = {gs: tile[:] for gs, tile in woven.items()}
+        h_bf[0, 0] = w1_bf[1, 1][:]
+        a_bf = [by_tile(flat(w1_raw[1, 1]).bitcast(BF16)[:, 0 : 4 * HALF]), late[:, 4:8, :]]
+        b_bf = [by_tile(w1_bf[0, 0][:]), late[:, 0:4, :]]
+        edge = 4 * HALF - HALF // 2
+        w2_bf = [
+            flat(late)[:, edge : edge + 8 * HALF].rearrange("p (g x) -> p g x", g=2)[:, :, 0:HALF],
+            woven[0, 1][:, 0 : 8 * P].rearrange("p (g x) -> p g x", g=2),
+            w2_last[:].rearrange("p (g x) -> p g x", g=2),
+        ]
+        picked = [sb("picked0", [P, HALF], F32)[:], flat(rows_last).bitcast(F32)[:, 0:HALF]]
+        capped = [b_first[0, 0], b_first[0, 1]]
+        ceiling, excess, room = w1_raw[0, 0], w1_raw[1, 0], w1_raw[0, 1]
 
         nc.sync.dma_start(offsets[:], offs)
         nc.gpsimd.memset(tab_sc[:].bitcast(I32), 0)
@@ -113,40 +123,44 @@ def tile_list_marathon_split_caps_kernel(
         def load_w2(g):
             rows = w2[PASS * g : PASS * (g + 1), :].rearrange("(j t i) n -> t j i n", t=4, i=8)
             for t in range(4):
-                nc.sync.dma_start(w2_raw[g][:, t, :], rows[t])
+                nc.sync.dma_start(w2_raw[:, g, t, :], rows[t])
 
         tab_rows = tab_scales.bitcast(I32).rearrange("a (q r) c -> r q a c", r=4)
         nc.sync.dma_start(bias_raw[2:4, :], b4.rearrange("(g c) -> g c", g=2))
+        nc.sync.dma_start(bias_raw[0:2, :], b1.rearrange("(g c) -> g c", g=2))
         for r in range(4):
             nc.sync.dma_start(tab_sc[r:P:SHIFT, :].bitcast(I32), tab_rows[r])
         load_table(0)
+        nc.sync.dma_start(bias_raw[QUAD : QUAD + 1, 0:N], b2.rearrange("(o c) -> o c", o=1))
         load_w4(0)
         w4_rows = w4_scales.bitcast(I32).rearrange("a (q r) c -> r q a c", r=4)
         for r in range(4):
             nc.sync.dma_start(w4_sc_raw[r:P:QUAD, :].bitcast(I32).rearrange("q (a c) -> q a c", a=2), w4_rows[r])
-        nc.sync.dma_start(bias_raw[0:2, :], b1.rearrange("(g c) -> g c", g=2))
         load_table(1)
         nc.vector.tensor_copy(v_sc[0][:], tab_sc[:].indirect(offsets[:]))
         for r in range(4):
             nc.sync.dma_start(v_sc[1][r:P:QUAD, :].bitcast(I32), v_sc[0][SHIFT + r : P : QUAD, :].bitcast(I32))
         load_w4(1)
-        for a, g in ag_pairs:
-            load_w1(a, g)
+        load_w1(0, 0)
+        load_w1(1, 0)
+        load_w1(0, 1)
+        load_w1(1, 1)
         load_page(0)
+        load_page(1)
         load_w2(0)
         load_w2(1)
-        load_page(1)
         load_page(2)
 
         nc.scalar.activation(
             bias_rows[0:4, :].rearrange("v (t j i) -> v t j i", t=4, i=8),
-            bias_raw[:].rearrange("v (j t i) -> v t j i", t=4, i=8),
+            bias_raw[0:4, :].rearrange("v (j t i) -> v t j i", t=4, i=8),
             ACT.Identity,
         )
+        nc.scalar.activation(bias_rows[QUAD : QUAD + 1, 0:N], bias_raw[QUAD : QUAD + 1, 0:N], ACT.Identity)
         for t in range(4):
             nc.tensor.transpose(banks[7][:, P * t : P * (t + 1)], bias_rows[:, P * t : P * (t + 1)], ident[:])
         nc.scalar.copy(bias[:], banks[7][:].rearrange("p (t c) -> p t c", t=4)[:, :, 0:4])
-        nc.gpsimd.dma_start(bias_rows[0:1, 0:N], b2.rearrange("(o c) -> o c", o=1))
+        nc.scalar.copy(b2_col[:], banks[7][:, QUAD : QUAD + 3 * P : P])
 
         def half_list(s):
             return offsets[:, HALF // 16 * s : HALF // 16 * (s + 1)]
@@ -166,8 +180,8 @@ def tile_list_marathon_split_caps_kernel(
             for u in halves:
                 nc.vector.tensor_copy(dst[:, 2 * u : 2 * u + 2], src[:, 2 * u : 2 * u + 2])
 
-        def quant_w1(a, g):
-            for u in range(2):
+        def quant_w1(a, g, halves=range(2)):
+            for u in halves:
                 cols = slice(2 * P * u, 2 * P * (u + 1))
                 values = w1_bf[a, g][:, 8 * P * u : 8 * P * (u + 1)]
                 nc.vector.quantize_mx(w1_codes[a, g][:, cols].bitcast(FP8X4), w1_sc[a, g][:, cols], values)
@@ -184,105 +198,104 @@ def tile_list_marathon_split_caps_kernel(
                 w4_raw[g][:].bitcast(I32).rearrange("p (a j t e) -> p a t j e", t=4, j=16, e=4),
             )
 
-        def gather_page(m, halves=range(2)):
-            for s in halves:
-                nc.vector.tensor_copy(picked[m, s], page[m][:].indirect(half_list(s)))
+        def gather_page(m):
+            nc.vector.tensor_copy(picked[m], page[m][:].indirect(half_list(0)))
 
-        def product_b(g, s, bank0):
-            entries = slice(HALF * s, HALF * (s + 1))
+        def pass_b(g, s, t, a, bank):
+            col0 = H * a + PASS * g + P * t
+            nc.tensor.matmul_mx(
+                banks[bank][:], w4_codes[g][:, 2 * (PASS * a + P * t) : 2 * (PASS * a + P * (t + 1))].bitcast(FP4X4),
+                w4_sc[:, col0 : col0 + P], v_words[a, s][:].bitcast(FP8X4), v_sc[a][:, HALF * s : HALF * (s + 1)],
+                start=(a == 0), stop=(a == 1),
+            )
+
+        def pass_a(g, s, t, a, bank):
+            cols = slice(P * t, P * (t + 1))
+            nc.tensor.matmul_mx(
+                banks[bank][:], w1_codes[a, g][:, cols].bitcast(FP8X4), w1_sc[a, g][:, cols],
+                v_words[a, s][:].bitcast(FP8X4), v_sc[a][:, HALF * s : HALF * (s + 1)], start=(a == 0), stop=(a == 1),
+            )
+
+        def first_b(g, bank0):
             for a in range(2):
                 for t in range(4):
-                    col0 = H * a + PASS * g + P * t
-                    nc.tensor.matmul_mx(
-                        banks[bank0 + t][:], w4_codes[g][:, 2 * (PASS * a + P * t) : 2 * (PASS * a + P * (t + 1))].bitcast(FP4X4),
-                        w4_sc[:, col0 : col0 + P],
-                        v_words[a, s][:].bitcast(FP8X4), v_sc[a][:, entries], start=(a == 0), stop=(a == 1),
-                    )
-
-        def copy_b(g, s, bank0):
+                    pass_b(g, 0, t, a, bank0 + t)
             for t in range(4):
-                nc.scalar.activation(b_sb[g, s, t], banks[bank0 + t][:], ACT.Identity, bias=bias[:, t, 2 + g : 3 + g])
+                nc.scalar.activation(b_first[g, t], banks[bank0 + t][:], ACT.Identity, bias=bias[:, t, 2 + g : 3 + g])
 
-        def product_a(g, s, bank0):
-            entries = slice(HALF * s, HALF * (s + 1))
-            for t in range(4):
-                cols = slice(P * t, P * (t + 1))
-                for a in range(2):
-                    nc.tensor.matmul_mx(
-                        banks[bank0 + t][:], w1_codes[a, g][:, cols].bitcast(FP8X4), w1_sc[a, g][:, cols],
-                        v_words[a, s][:].bitcast(FP8X4), v_sc[a][:, entries], start=(a == 0), stop=(a == 1),
-                    )
+        def first_a(g, bank0, tiles):
+            for a in range(2):
+                for t in tiles:
+                    pass_a(g, 0, t, a, bank0 + t)
+
+        def first_max(g, bank0, tiles):
+            for t in tiles:
                 nc.vector.scalar_tensor_tensor(
-                    h_rows[g, s][:, t, :], banks[bank0 + t][:], bias[:, t, g : g + 1], b_sb[g, s, t],
-                    ALU.add, ALU.max,
+                    h_rows[g, 0][:, t, :], banks[bank0 + t][:], bias[:, t, g : g + 1], b_first[g, t], ALU.add, ALU.max
                 )
 
-        def rounded_b(g, bank_ids):
-            for t in range(4):
-                for a in range(2):
-                    col0 = H * a + PASS * g + P * t
-                    nc.tensor.matmul_mx(
-                        banks[bank_ids[t]][:], w4_codes[g][:, 2 * (PASS * a + P * t) : 2 * (PASS * a + P * (t + 1))].bitcast(FP4X4),
-                        w4_sc[:, col0 : col0 + P],
-                        v_words[a, 1][:].bitcast(FP8X4), v_sc[a][:, HALF:S], start=(a == 0), stop=(a == 1),
-                    )
-                nc.scalar.activation(
-                    b_bf[g][:, HALF * t : HALF * (t + 1)], banks[bank_ids[t]][:], ACT.Identity,
-                    bias=bias[:, t, 2 + g : 3 + g],
-                )
+        def rounded_b(g, t, bank):
+            for a in range(2):
+                pass_b(g, 1, t, a, bank)
+            nc.scalar.activation(b_bf[g][:, t, :], banks[bank][:], ACT.Identity, bias=bias[:, t, 2 + g : 3 + g])
 
-        def rounded_a(g, bank_ids):
-            for t in range(4):
-                cols = slice(P * t, P * (t + 1))
-                for a in range(2):
-                    nc.tensor.matmul_mx(
-                        banks[bank_ids[t]][:], w1_codes[a, g][:, cols].bitcast(FP8X4), w1_sc[a, g][:, cols],
-                        v_words[a, 1][:].bitcast(FP8X4), v_sc[a][:, HALF:S], start=(a == 0), stop=(a == 1),
-                    )
-                nc.scalar.activation(
-                    a_bf[g][:, HALF * t : HALF * (t + 1)], banks[bank_ids[t]][:], ACT.Identity, bias=bias[:, t, g : g + 1]
-                )
+        def rounded_a(g, t, bank):
+            for a in range(2):
+                pass_a(g, 1, t, a, bank)
+            nc.scalar.activation(a_bf[g][:, t, :], banks[bank][:], ACT.Identity, bias=bias[:, t, g : g + 1])
 
         def rounded_max(g):
-            nc.vector.tensor_tensor(h_rows[g, 1].rearrange("p t c -> p (t c)"), a_bf[g], b_bf[g], ALU.max)
+            nc.vector.tensor_tensor(h_rows[g, 1], a_bf[g], b_bf[g], ALU.max)
 
-        def weave_h(g, s):
-            dst = h_bf[g, s].rearrange("p (c i t) -> p c t i", i=4, t=4)
-            src = h_rows[g, s].rearrange("p t (c i) -> p c t i", i=4)
-            nc.scalar.copy(dst, src)
+        def weave_h(g, s, lo=0, hi=HALF):
+            nc.scalar.copy(
+                h_bf[g, s][:, 4 * lo : 4 * hi].rearrange("p (c i t) -> p c t i", i=4, t=4),
+                h_rows[g, s][:, :, lo:hi].rearrange("p t (c i) -> p c t i", i=4),
+            )
+
+        def pool_weave_h(g, s, lo=0, hi=HALF):
+            nc.gpsimd.tensor_scalar(
+                h_bf[g, s][:, 4 * lo : 4 * hi].rearrange("p (c t) -> p c t", t=4),
+                h_rows[g, s][:, :, lo:hi].rearrange("p t c -> p c t"), 1.0, 0.0, ALU.mult, ALU.add,
+            )
 
         def quant_h(g, s):
             nc.vector.quantize_mx(h_codes[g, s][:].bitcast(FP8X4), h_sc[g, s][:], h_bf[g, s])
 
-        def cast_w2():
+        def cast_w2(m):
             nc.scalar.copy(
-                w2_bf[:, 0 : 4 * N].rearrange("p (c i t) -> p c t i", i=4, t=4),
-                w2_raw[0][:].rearrange("p t (c i) -> p c t i", i=4),
-            )
-            nc.scalar.copy(
-                w2_bf[:, 4 * N : 8 * N].rearrange("p (c i t) -> p c t i", i=4, t=4),
-                w2_raw[1][:].rearrange("p t (c i) -> p c t i", i=4),
+                w2_bf[m].rearrange("p g (c i t) -> p g c t i", i=4, t=4),
+                w2_raw[:, :, :, P * m : P * (m + 1)].rearrange("p g t (c i) -> p g c t i", i=4),
             )
 
-        def quant_w2():
-            for lo, hi in ((0, 512), (512, 2 * N)):
-                nc.vector.quantize_mx(w2_codes[:, lo:hi].bitcast(FP8X4), w2_sc[:, lo:hi], w2_bf[:, 4 * lo : 4 * hi])
+        def quant_w2(m, parts):
+            for lo, hi in parts:
+                cols = slice(2 * P * m + P * lo, 2 * P * m + P * hi)
+                values = w2_bf[m][:, lo:hi, :].rearrange("p g x -> p (g x)")
+                nc.vector.quantize_mx(w2_codes[:, cols].bitcast(FP8X4), w2_sc[:, cols], values)
 
-        def third_product(m, s):
-            bank_y = banks[4 + m]
+        def third_product(m, s, bank):
             for g in range(2):
-                cols = slice(N * g + P * m, N * g + P * (m + 1))
+                cols = slice(2 * P * m + P * g, 2 * P * m + P * (g + 1))
                 nc.tensor.matmul_mx(
-                    bank_y[:], w2_codes[:, cols].bitcast(FP8X4), w2_sc[:, cols],
+                    banks[bank][:], w2_codes[:, cols].bitcast(FP8X4), w2_sc[:, cols],
                     h_codes[g, s][:].bitcast(FP8X4), h_sc[g, s][:], start=(g == 0), stop=(g == 1),
                 )
-            nc.vector.scalar_tensor_tensor(
-                capped[m, s], bank_y[:], b2_col[:, m : m + 1], picked[m, s],
-                ALU.add, ALU.min,
-            )
 
-        def scatter(m, s):
-            nc.vector.tensor_copy(page[m][:].indirect(half_list(s)), capped[m, s])
+        def cap(m, bank):
+            nc.vector.scalar_tensor_tensor(capped[m], banks[bank][:], b2_col[:, m : m + 1], picked[m], ALU.add, ALU.min)
+
+        def scatter(m):
+            nc.vector.tensor_copy(page[m][:].indirect(half_list(0)), capped[m])
+
+        def gather_excess(m, s, place, bank):
+            nc.scalar.activation(ceiling[:, place, :], banks[bank][:], ACT.Identity, bias=b2_col[:, m : m + 1])
+            nc.vector.tensor_tensor(excess[:, place, :], page[m][:].indirect(half_list(s)), ceiling[:, place, :], ALU.subtract)
+
+        def scatter_sum(m, s, place):
+            nc.scalar.activation(room[:, place, :], excess[:, place, :], ACT.Relu, scale=-1.0)
+            nc.scalar.activation(excess[:, place, :], room[:, place, :], ACT.Identity, scale=-1.0)
+            nc.vector.tensor_tensor(page[m][:].indirect(half_list(s)), ceiling[:, place, :], excess[:, place, :], ALU.add)
 
         gather_words(0, 0)
         order_w4_scales()
@@ -293,49 +306,59 @@ def tile_list_marathon_split_caps_kernel(
         gather_words(1, 1)
         w4_codes.append(sb("w4_codes1", [P, 2 * H], U8, tag="tab_w1"))
         order_w4_words(1)
-        product_b(0, 0, 0)
-        copy_b(0, 0, 0)
-        product_b(1, 0, 4)
-        copy_b(1, 0, 4)
+        first_b(0, 0)
+        first_b(1, 4)
         for a, g in ag_pairs[:3]:
             cast_w1_in_order(a, g)
             quant_w1(a, g)
-        rounded_b(0, (0, 1, 2, 3))
-        product_a(0, 0, 4)
-        for m in range(3):
-            nc.tensor.transpose(banks[7][:, P * m : P * (m + 1)], bias_rows[:, P * m : P * (m + 1)], ident[:])
-        nc.scalar.copy(b2_col[:], banks[7][:, 0 : 3 * P : P])
+        for t in range(4):
+            rounded_b(0, t, t)
+        for t in range(4):
+            first_a(0, 4, (t,))
+        first_max(0, 4, range(4))
         cast_w1(1, 1, nc.scalar.copy, (0, 1))
         cast_w1_in_order(1, 1, (1,))
-        quant_w1(1, 1)
-        gather_page(0, (0,))
-        product_a(1, 0, 0)
-        gather_page(0, (1,))
-        weave_h(0, 0)
-        quant_h(0, 0)
-        cast_w2()
-        quant_w2()
-        weave_h(1, 0)
+        quant_w1(1, 1, (1, 0))
+        gather_page(0)
+        first_a(1, 0, (2, 3, 0, 1))
+        first_max(1, 0, (2, 3, 0, 1))
+        pool_weave_h(0, 0)
+        for t in range(4):
+            rounded_a(0, t, 4 + t)
+        weave_h(1, 0, 0, SHARE)
+        pool_weave_h(1, 0, SHARE, HALF)
+        for t in range(3):
+            rounded_b(1, t, 4 + t)
         gather_page(1)
+        quant_h(0, 0)
         quant_h(1, 0)
-        gather_page(2)
-        rounded_a(0, (4, 5, 6, 7))
-        third_product(0, 0)
+        cast_w2(0)
+        quant_w2(0, ((0, 1), (1, 2)))
+        third_product(0, 0, 0)
         rounded_max(0)
-        scatter(0, 0)
-        rounded_b(1, (0, 1, 2, 3))
-        rounded_a(1, (7, 0, 1, 2))
-        rounded_max(1)
-        weave_h(0, 1)
-        weave_h(1, 1)
-        third_product(1, 0)
-        scatter(1, 0)
+        cap(0, 0)
+        cast_w2(1)
+        quant_w2(1, ((0, 2),))
+        pool_weave_h(0, 1)
+        scatter(0)
+        cast_w2(2)
+        quant_w2(2, ((0, 2),))
         quant_h(0, 1)
+        rounded_b(1, 3, 7)
+        for t, bank in ((0, 1), (3, 2), (1, 7), (2, 1)):
+            rounded_a(1, t, bank)
+        third_product(1, 0, 7)
+        third_product(2, 0, 1)
+        cap(1, 7)
+        rounded_max(1)
+        gather_excess(2, 0, 3, 1)
+        scatter(1)
+        weave_h(1, 1)
         quant_h(1, 1)
-        third_product(2, 0)
-        scatter(2, 0)
+        scatter_sum(2, 0, 3)
         for m in range(3):
-            third_product(m, 1)
+            third_product(m, 1, 3 + m)
+            gather_excess(m, 1, m, 3 + m)
         for m in range(3):
-            scatter(m, 1)
+            scatter_sum(m, 1, m)
             nc.sync.dma_start(out[P * m : P * (m + 1), :], page[m][:])

@@ -21,7 +21,7 @@ P = 128
 PASS = 512
 HALF = 512
 QUAD = 32
-SHARE = 320
+SHARE = 192
 SHIFT = 16
 
 
@@ -58,15 +58,15 @@ def tile_list_marathon_split_caps_kernel(
         w1_codes = {(a, g): sb(f"w1_codes{a}{g}", [P, PASS], U32)[:] for a, g in ag_pairs}
         w1_sc = {(a, g): sb(f"w1_sc{a}{g}", [P, PASS], U8) for a, g in ag_pairs}
         w2_raw = sb("w2_raw", [P, 2, 4, N], F32)
-        w2_codes = sb("w2_codes", [P, 2 * N], U32)
+        w2_codes = [sb(f"w2_codes{m}", [P, 2 * P], U32) for m in range(2)]
         w2_sc = sb("w2_sc", [P, 2 * N], U8)
         page = [sb(f"page{m}", [P, T], F32) for m in range(3)]
-        b_first = {(g, t): sb(f"b_first{g}{t}", [P, HALF], F32)[:] for g in range(2) for t in range(4)}
+        b_exact = [sb(f"b_exact{t}", [P, HALF], F32)[:] for t in range(4)]
+        first_pair = sb("first_pair", [P, 8, HALF], BF16)
         rows_first = sb("rows_first", [P, 4, HALF], BF16)
         rows_last = sb("rows_last", [P, 4, HALF], BF16)
         late = sb("late", [P, 12, HALF], BF16)
         woven = {gs: sb(f"woven{gs[0]}{gs[1]}", [P, 4 * HALF], BF16) for gs in gs_pairs[1:]}
-        w2_last = sb("w2_last", [P, 8 * P], BF16)
         h_codes = {(g, s): sb(f"h_codes{g}{s}", [P, HALF], U32) for g, s in gs_pairs}
         h_sc = {(g, s): sb(f"h_sc{g}{s}", [P, HALF], U8) for g, s in gs_pairs}
         banks = [psum.tile([P, HALF], F32, name=f"bank{b}") for b in range(8)]
@@ -77,20 +77,18 @@ def tile_list_marathon_split_caps_kernel(
         def by_tile(values):
             return values.rearrange("p (t c) -> p t c", t=4)
 
-        h_rows = {(0, 0): by_tile(w1_bf[0, 1][:]), (1, 0): rows_first[:], (0, 1): late[:, 8:12, :], (1, 1): rows_last[:]}
+        h_rows = {(0, 0): by_tile(w1_bf[1, 1][:]), (1, 0): rows_first[:], (0, 1): late[:, 0:4, :], (1, 1): rows_last[:]}
         h_bf = {gs: tile[:] for gs, tile in woven.items()}
-        h_bf[0, 0] = w1_bf[1, 1][:]
-        a_bf = [by_tile(flat(w1_raw[1, 1]).bitcast(BF16)[:, 0 : 4 * HALF]), late[:, 4:8, :]]
-        b_bf = [by_tile(w1_bf[0, 0][:]), late[:, 0:4, :]]
-        edge = 4 * HALF - HALF // 2
-        w2_bf = [
-            flat(late)[:, edge : edge + 8 * HALF].rearrange("p (g x) -> p g x", g=2)[:, :, 0:HALF],
-            woven[0, 1][:, 0 : 8 * P].rearrange("p (g x) -> p g x", g=2),
-            w2_last[:].rearrange("p (g x) -> p g x", g=2),
-        ]
+        h_bf[0, 0] = w1_bf[0, 1][:]
+        a_bf = {(0, 0): first_pair[:, 0:4, :], (0, 1): by_tile(w1_bf[1, 0][:]), (1, 1): late[:, 8:12, :]}
+        b_bf = {(0, 0): first_pair[:, 4:8, :], (0, 1): by_tile(w1_bf[0, 0][:]), (1, 1): late[:, 4:8, :]}
+        edge = 4 * HALF - P
+        w2_first = flat(late)[:, edge : edge + 8 * HALF].rearrange("p (u x) -> p u x", u=4)[:, :, 0 : 2 * P]
+        w2_later = {1: woven[0, 1][:, 0 : 8 * P], 2: woven[0, 1][:, 8 * P : 16 * P]}
         picked = [sb("picked0", [P, HALF], F32)[:], flat(rows_last).bitcast(F32)[:, 0:HALF]]
-        capped = [b_first[0, 0], b_first[0, 1]]
-        ceiling, excess, room = w1_raw[0, 0], w1_raw[1, 0], w1_raw[0, 1]
+        capped = [b_exact[0], b_exact[1]]
+        ceiling, excess = w1_raw[0, 0], w1_raw[1, 0]
+        room = [w1_raw[0, 1][:, place, :] for place in range(3)] + [flat(rows_last).bitcast(F32)[:, HALF : 2 * HALF]]
 
         nc.sync.dma_start(offsets[:], offs)
         nc.gpsimd.memset(tab_sc[:].bitcast(I32), 0)
@@ -168,12 +166,6 @@ def tile_list_marathon_split_caps_kernel(
         def gather_words(a, s):
             nc.vector.tensor_copy(v_words[a, s][:], tab_w[a][:].indirect(half_list(s)))
 
-        def cast_w1(a, g, copy, tiles):
-            dst = w1_bf[a, g][:].rearrange("p (t j e i k) -> p t j e k i", t=4, e=2, i=4, k=4)
-            src = w1_raw[a, g][:].rearrange("p k (j t e i) -> p t j e k i", t=4, e=2, i=4)
-            for t in tiles:
-                copy(dst[:, t], src[:, t])
-
         def cast_w1_in_order(a, g, halves=range(2)):
             dst = w1_bf[a, g][:].rearrange("p (t j i k) -> p t j i k", t=4, i=8, k=4)
             src = w1_raw[a, g][:].rearrange("p k (j t i) -> p t j i k", t=4, i=8)
@@ -216,36 +208,21 @@ def tile_list_marathon_split_caps_kernel(
                 v_words[a, s][:].bitcast(FP8X4), v_sc[a][:, HALF * s : HALF * (s + 1)], start=(a == 0), stop=(a == 1),
             )
 
-        def first_b(g, bank0):
+        def copy_b(dst, g, t, bank):
+            nc.scalar.activation(dst, banks[bank][:], ACT.Identity, bias=bias[:, t, 2 + g : 3 + g])
+
+        def rounded_b(g, s, t, bank):
             for a in range(2):
-                for t in range(4):
-                    pass_b(g, 0, t, a, bank0 + t)
-            for t in range(4):
-                nc.scalar.activation(b_first[g, t], banks[bank0 + t][:], ACT.Identity, bias=bias[:, t, 2 + g : 3 + g])
+                pass_b(g, s, t, a, bank)
+            copy_b(b_bf[g, s][:, t, :], g, t, bank)
 
-        def first_a(g, bank0, tiles):
+        def rounded_a(g, s, t, bank):
             for a in range(2):
-                for t in tiles:
-                    pass_a(g, 0, t, a, bank0 + t)
+                pass_a(g, s, t, a, bank)
+            nc.scalar.activation(a_bf[g, s][:, t, :], banks[bank][:], ACT.Identity, bias=bias[:, t, g : g + 1])
 
-        def first_max(g, bank0, tiles):
-            for t in tiles:
-                nc.vector.scalar_tensor_tensor(
-                    h_rows[g, 0][:, t, :], banks[bank0 + t][:], bias[:, t, g : g + 1], b_first[g, t], ALU.add, ALU.max
-                )
-
-        def rounded_b(g, t, bank):
-            for a in range(2):
-                pass_b(g, 1, t, a, bank)
-            nc.scalar.activation(b_bf[g][:, t, :], banks[bank][:], ACT.Identity, bias=bias[:, t, 2 + g : 3 + g])
-
-        def rounded_a(g, t, bank):
-            for a in range(2):
-                pass_a(g, 1, t, a, bank)
-            nc.scalar.activation(a_bf[g][:, t, :], banks[bank][:], ACT.Identity, bias=bias[:, t, g : g + 1])
-
-        def rounded_max(g):
-            nc.vector.tensor_tensor(h_rows[g, 1], a_bf[g], b_bf[g], ALU.max)
+        def rounded_max(g, s):
+            nc.vector.tensor_tensor(h_rows[g, s], a_bf[g, s], b_bf[g, s], ALU.max)
 
         def weave_h(g, s, lo=0, hi=HALF):
             nc.scalar.copy(
@@ -262,23 +239,29 @@ def tile_list_marathon_split_caps_kernel(
         def quant_h(g, s):
             nc.vector.quantize_mx(h_codes[g, s][:].bitcast(FP8X4), h_sc[g, s][:], h_bf[g, s])
 
-        def cast_w2(m):
-            nc.scalar.copy(
-                w2_bf[m].rearrange("p g (c i t) -> p g c t i", i=4, t=4),
+        def first_w2():
+            for k in range(2):
+                nc.scalar.copy(
+                    w2_first[:, k:4:2, :].rearrange("p g (c i t) -> p g c t i", i=4, t=4),
+                    w2_raw[:, :, :, P // 2 * k : P // 2 * (k + 1)].rearrange("p g t (c i) -> p g c t i", i=4),
+                )
+            for u in range(4):
+                cols = slice(P // 2 * u, P // 2 * (u + 1))
+                nc.vector.quantize_mx(w2_codes[0][:, cols].bitcast(FP8X4), w2_sc[:, cols], w2_first[:, u, :])
+
+        def later_w2(m):
+            nc.vector.tensor_copy(
+                w2_later[m].rearrange("p (g c i t) -> p g c t i", g=2, i=4, t=4),
                 w2_raw[:, :, :, P * m : P * (m + 1)].rearrange("p g t (c i) -> p g c t i", i=4),
             )
-
-        def quant_w2(m, parts):
-            for lo, hi in parts:
-                cols = slice(2 * P * m + P * lo, 2 * P * m + P * hi)
-                values = w2_bf[m][:, lo:hi, :].rearrange("p g x -> p (g x)")
-                nc.vector.quantize_mx(w2_codes[:, cols].bitcast(FP8X4), w2_sc[:, cols], values)
+            cols = slice(2 * P * m, 2 * P * (m + 1))
+            nc.vector.quantize_mx(w2_codes[m][:].bitcast(FP8X4), w2_sc[:, cols], w2_later[m])
 
         def third_product(m, s, bank):
             for g in range(2):
                 cols = slice(2 * P * m + P * g, 2 * P * m + P * (g + 1))
                 nc.tensor.matmul_mx(
-                    banks[bank][:], w2_codes[:, cols].bitcast(FP8X4), w2_sc[:, cols],
+                    banks[bank][:], w2_codes[m][:, P * g : P * (g + 1)].bitcast(FP8X4), w2_sc[:, cols],
                     h_codes[g, s][:].bitcast(FP8X4), h_sc[g, s][:], start=(g == 0), stop=(g == 1),
                 )
 
@@ -293,8 +276,8 @@ def tile_list_marathon_split_caps_kernel(
             nc.vector.tensor_tensor(excess[:, place, :], page[m][:].indirect(half_list(s)), ceiling[:, place, :], ALU.subtract)
 
         def scatter_sum(m, s, place):
-            nc.scalar.activation(room[:, place, :], excess[:, place, :], ACT.Relu, scale=-1.0)
-            nc.scalar.activation(excess[:, place, :], room[:, place, :], ACT.Identity, scale=-1.0)
+            nc.scalar.activation(room[place], excess[:, place, :], ACT.Relu, scale=-1.0)
+            nc.scalar.activation(excess[:, place, :], room[place], ACT.Identity, scale=-1.0)
             nc.vector.tensor_tensor(page[m][:].indirect(half_list(s)), ceiling[:, place, :], excess[:, place, :], ALU.add)
 
         gather_words(0, 0)
@@ -306,59 +289,62 @@ def tile_list_marathon_split_caps_kernel(
         gather_words(1, 1)
         w4_codes.append(sb("w4_codes1", [P, 2 * H], U8, tag="tab_w1"))
         order_w4_words(1)
-        first_b(0, 0)
-        first_b(1, 4)
-        for a, g in ag_pairs[:3]:
+        for g, rows in ((0, [b_bf[0, 0][:, t, :] for t in range(4)]), (1, b_exact)):
+            for a in range(2):
+                for t in range(4):
+                    pass_b(g, 0, t, a, 4 * g + t)
+            for t in range(4):
+                copy_b(rows[t], g, t, 4 * g + t)
+        for a, g in ag_pairs:
             cast_w1_in_order(a, g)
             quant_w1(a, g)
         for t in range(4):
-            rounded_b(0, t, t)
+            rounded_a(0, 0, t, t)
+        for a in range(2):
+            for t in range(4):
+                pass_a(1, 0, t, a, 4 + t)
         for t in range(4):
-            first_a(0, 4, (t,))
-        first_max(0, 4, range(4))
-        cast_w1(1, 1, nc.scalar.copy, (0, 1))
-        cast_w1_in_order(1, 1, (1,))
-        quant_w1(1, 1, (1, 0))
-        gather_page(0)
-        first_a(1, 0, (2, 3, 0, 1))
-        first_max(1, 0, (2, 3, 0, 1))
+            rounded_b(0, 1, t, t)
+        rounded_max(0, 0)
         pool_weave_h(0, 0)
         for t in range(4):
-            rounded_a(0, t, 4 + t)
+            nc.vector.scalar_tensor_tensor(
+                h_rows[1, 0][:, t, :], banks[4 + t][:], bias[:, t, 1:2], b_exact[t], ALU.add, ALU.max
+            )
+        for t in range(4):
+            rounded_a(0, 1, t, t)
         weave_h(1, 0, 0, SHARE)
         pool_weave_h(1, 0, SHARE, HALF)
-        for t in range(3):
-            rounded_b(1, t, 4 + t)
+        gather_page(0)
         gather_page(1)
         quant_h(0, 0)
         quant_h(1, 0)
-        cast_w2(0)
-        quant_w2(0, ((0, 1), (1, 2)))
+        first_w2()
         third_product(0, 0, 0)
-        rounded_max(0)
+        rounded_max(0, 1)
         cap(0, 0)
-        cast_w2(1)
-        quant_w2(1, ((0, 2),))
+        later_w2(1)
+        w2_codes.append(sb("w2_codes2", [P, 2 * P], U32, tag="picked0"))
+        later_w2(2)
         pool_weave_h(0, 1)
         scatter(0)
-        cast_w2(2)
-        quant_w2(2, ((0, 2),))
         quant_h(0, 1)
-        rounded_b(1, 3, 7)
-        for t, bank in ((0, 1), (3, 2), (1, 7), (2, 1)):
-            rounded_a(1, t, bank)
-        third_product(1, 0, 7)
-        third_product(2, 0, 1)
-        cap(1, 7)
-        rounded_max(1)
-        gather_excess(2, 0, 3, 1)
+        for t in range(4):
+            rounded_b(1, 1, t, 4 + t)
+        for t in range(4):
+            rounded_a(1, 1, t, 1 + t)
+        third_product(1, 0, 3)
+        third_product(2, 0, 4)
+        cap(1, 3)
+        rounded_max(1, 1)
+        gather_excess(2, 0, 3, 4)
         scatter(1)
         weave_h(1, 1)
         quant_h(1, 1)
         scatter_sum(2, 0, 3)
         for m in range(3):
-            third_product(m, 1, 3 + m)
-            gather_excess(m, 1, m, 3 + m)
+            third_product(m, 1, 5 + m)
+            gather_excess(m, 1, m, 5 + m)
         for m in range(3):
             scatter_sum(m, 1, m)
             nc.sync.dma_start(out[P * m : P * (m + 1), :], page[m][:])

@@ -53,7 +53,8 @@ def tile_list_marathon_split_caps_kernel(
         w4_codes = [sb("w4_codes0", [P, 2 * H], U8)]
         tab_w = [sb(f"tab_w{a}", [P, T], U32) for a in range(2)]
         v_words = {(a, s): sb(f"v_words{a}{s}", [P, HALF], U32) for a, s in ((0, 0), (1, 0), (1, 1))}
-        w1_raw = {(a, g): sb(f"w1_raw{a}{g}", [P, 4, PASS], F32) for a, g in ag_pairs}
+        w1_raw = {(a, g): sb(f"w1_raw{a}{g}", [P, 4, PASS], F32) for a, g in ag_pairs[:3]}
+        w1_last = [sb(f"w1_last{u}", [P, 4, PASS // 2], F32) for u in range(2)]
         w1_bf = {(a, g): sb(f"w1_bf{a}{g}", [P, 4 * PASS], BF16) for a, g in ag_pairs}
         w1_codes = {(a, g): sb(f"w1_codes{a}{g}", [P, PASS], U32)[:] for a, g in ag_pairs}
         w1_sc = {(a, g): sb(f"w1_sc{a}{g}", [P, PASS], U8) for a, g in ag_pairs}
@@ -142,7 +143,9 @@ def tile_list_marathon_split_caps_kernel(
         load_w1(0, 0)
         load_w1(1, 0)
         load_w1(0, 1)
-        load_w1(1, 1)
+        for u in range(2):
+            block = w1[PASS : 2 * PASS, PASS + PASS // 2 * u : PASS + PASS // 2 * (u + 1)]
+            nc.sync.dma_start(w1_last[u][:], block.rearrange("(p j) c -> p j c", j=4))
         load_page(0)
         load_page(1)
         load_w2(0)
@@ -295,9 +298,15 @@ def tile_list_marathon_split_caps_kernel(
                     pass_b(g, 0, t, a, 4 * g + t)
             for t in range(4):
                 copy_b(rows[t], g, t, 4 * g + t)
-        for a, g in ag_pairs:
+        for a, g in ag_pairs[:3]:
             cast_w1_in_order(a, g)
             quant_w1(a, g)
+        last_bf = w1_bf[1, 1][:].rearrange("p (t j i k) -> p t j i k", t=4, i=8, k=4)
+        for u in range(2):
+            nc.vector.tensor_copy(
+                last_bf[:, :, 8 * u : 8 * (u + 1)], w1_last[u][:].rearrange("p k (j t i) -> p t j i k", t=4, i=8)
+            )
+        quant_w1(1, 1)
         for t in range(4):
             rounded_a(0, 0, t, t)
         for a in range(2):

@@ -244,7 +244,7 @@ def tile_list_marathon_split_caps_kernel(
 
         def first_w2():
             for k in range(2):
-                nc.scalar.copy(
+                nc.vector.tensor_copy(
                     w2_first[:, k:4:2, :].rearrange("p g (c i t) -> p g c t i", i=4, t=4),
                     w2_raw[:, :, :, P // 2 * k : P // 2 * (k + 1)].rearrange("p g t (c i) -> p g c t i", i=4),
                 )
@@ -252,11 +252,13 @@ def tile_list_marathon_split_caps_kernel(
                 cols = slice(P // 2 * u, P // 2 * (u + 1))
                 nc.vector.quantize_mx(w2_codes[0][:, cols].bitcast(FP8X4), w2_sc[:, cols], w2_first[:, u, :])
 
-        def later_w2(m):
-            nc.vector.tensor_copy(
+        def cast_later_w2(m, copy):
+            copy(
                 w2_later[m].rearrange("p (g c i t) -> p g c t i", g=2, i=4, t=4),
                 w2_raw[:, :, :, P * m : P * (m + 1)].rearrange("p g t (c i) -> p g c t i", i=4),
             )
+
+        def quant_later_w2(m):
             cols = slice(2 * P * m, 2 * P * (m + 1))
             nc.vector.quantize_mx(w2_codes[m][:].bitcast(FP8X4), w2_sc[:, cols], w2_later[m])
 
@@ -330,11 +332,13 @@ def tile_list_marathon_split_caps_kernel(
         quant_h(1, 0)
         first_w2()
         third_product(0, 0, 0)
+        cast_later_w2(1, nc.scalar.copy)
+        cast_later_w2(2, nc.vector.tensor_copy)
         rounded_max(0, 1)
+        quant_later_w2(1)
         cap(0, 0)
-        later_w2(1)
         w2_codes.append(sb("w2_codes2", [P, 2 * P], U32, tag="picked0"))
-        later_w2(2)
+        quant_later_w2(2)
         pool_weave_h(0, 1)
         scatter(0)
         quant_h(0, 1)

@@ -214,6 +214,11 @@ def tile_list_marathon_split_caps_kernel(
         def copy_b(dst, g, t, bank):
             nc.scalar.activation(dst, banks[bank][:], ACT.Identity, bias=bias[:, t, 2 + g : 3 + g])
 
+        def exact_b(t, bank):
+            for a in range(2):
+                pass_b(1, 0, t, a, bank)
+            copy_b(b_exact[t], 1, t, bank)
+
         def rounded_b(g, s, t, bank):
             for a in range(2):
                 pass_b(g, s, t, a, bank)
@@ -294,12 +299,13 @@ def tile_list_marathon_split_caps_kernel(
         gather_words(1, 1)
         w4_codes.append(sb("w4_codes1", [P, 2 * H], U8, tag="tab_w1"))
         order_w4_words(1)
-        for g, rows in ((0, [b_bf[0, 0][:, t, :] for t in range(4)]), (1, b_exact)):
-            for a in range(2):
-                for t in range(4):
-                    pass_b(g, 0, t, a, 4 * g + t)
+        for a in range(2):
             for t in range(4):
-                copy_b(rows[t], g, t, 4 * g + t)
+                pass_b(0, 0, t, a, t)
+        for t in range(4):
+            copy_b(b_bf[0, 0][:, t, :], 0, t, t)
+        for t in range(2):
+            exact_b(t, 4 + t)
         for a, g in ag_pairs[:3]:
             cast_w1_in_order(a, g)
             quant_w1(a, g)
@@ -314,8 +320,10 @@ def tile_list_marathon_split_caps_kernel(
         for a in range(2):
             for t in range(4):
                 pass_a(1, 0, t, a, 4 + t)
+        for t in range(2, 4):
+            exact_b(t, t - 2)
         for t in range(4):
-            rounded_b(0, 1, t, t)
+            rounded_b(0, 1, t, (t + 2) % 4)
         rounded_max(0, 0)
         pool_weave_h(0, 0)
         for t in range(4):
@@ -323,7 +331,7 @@ def tile_list_marathon_split_caps_kernel(
                 h_rows[1, 0][:, t, :], banks[4 + t][:], bias[:, t, 1:2], b_exact[t], ALU.add, ALU.max
             )
         for t in range(4):
-            rounded_a(0, 1, t, t)
+            rounded_a(0, 1, t, (t + 2) % 4)
         weave_h(1, 0, 0, SHARE)
         pool_weave_h(1, 0, SHARE, HALF)
         gather_page(0)

@@ -21,8 +21,8 @@ P = 128
 PASS = 512
 HALF = 512
 QUAD = 32
-SHARE = 192
 SHIFT = 16
+SHARE = 192
 
 
 def tile_list_marathon_split_caps_kernel(
@@ -31,6 +31,7 @@ def tile_list_marathon_split_caps_kernel(
     nc = tc.nc
     with ExitStack() as ctx:
         keep = ctx.enter_context(tc.tile_pool(name="keep", bufs=1))
+        shared = ctx.enter_context(tc.tile_pool(name="shared", bufs=1))
         psum = ctx.enter_context(tc.psum_pool(name="psum", bufs=1))
 
         def sb(name, shape, dtype, tag=None):
@@ -43,53 +44,41 @@ def tile_list_marathon_split_caps_kernel(
         tab_sc = sb("tab_sc", [P, T], U8)
         v_sc = [sb(f"v_sc{a}", [P, S], U8) for a in range(2)]
         bias_rows = sb("bias_rows", [P, PASS], F32)
-        bias_raw = sb("bias_raw", [2 * QUAD, PASS], F32)
+        bias_raw = sb("bias_raw", [4, PASS], F32)
         bias = sb("bias", [P, 4, 4], F32)
         b2_col = sb("b2_col", [P, 3], F32)
         ident = sb("ident", [P, P], F32)
         w4_sc_raw = sb("w4_sc_raw", [P, 2 * H], U8)
         w4_sc = sb("w4_sc", [P, 2 * H], U8)
         w4_raw = [sb(f"w4_raw{g}", [P, 2 * H], U8) for g in range(2)]
-        w4_codes = [sb("w4_codes0", [P, 2 * H], U8)]
+        w4_codes = [sb(f"w4_codes{g}", [P, 2 * H], U8) for g in range(2)]
         tab_w = [sb(f"tab_w{a}", [P, T], U32) for a in range(2)]
-        v_words = {(a, s): sb(f"v_words{a}{s}", [P, HALF], U32) for a, s in ((0, 0), (1, 0), (1, 1))}
+        v_words = {(a, 0): sb(f"v_words{a}0", [P, HALF], U32) for a in range(2)}
         w1_raw = {(a, g): sb(f"w1_raw{a}{g}", [P, 4, PASS], F32) for a, g in ag_pairs[:3]}
         w1_last = [sb(f"w1_last{u}", [P, 4, PASS // 2], F32) for u in range(2)]
         w1_bf = {(a, g): sb(f"w1_bf{a}{g}", [P, 4 * PASS], BF16) for a, g in ag_pairs}
-        w1_codes = {(a, g): sb(f"w1_codes{a}{g}", [P, PASS], U32)[:] for a, g in ag_pairs}
+        w1_codes = {(a, g): sb(f"w1_codes{a}{g}", [P, PASS], U32) for a, g in ag_pairs}
         w1_sc = {(a, g): sb(f"w1_sc{a}{g}", [P, PASS], U8) for a, g in ag_pairs}
-        w2_raw = sb("w2_raw", [P, 2, 4, N], F32)
-        w2_codes = [sb(f"w2_codes{m}", [P, 2 * P], U32) for m in range(2)]
-        w2_sc = sb("w2_sc", [P, 2 * N], U8)
+        w2_raw = shared.tile([P, 2, 4, N], F32, name="w2_raw", offset=0)
+        w2_first = sb("w2_first", [P, 8 * P], BF16)
+        w2_later = sb("w2_later", [P, 16 * P], BF16)
+        w2_codes = sb("w2_codes", [P, 6 * P], U32)
+        w2_sc = sb("w2_sc", [P, 6 * P], U8)
         page = [sb(f"page{m}", [P, T], F32) for m in range(3)]
-        b_exact = [sb(f"b_exact{t}", [P, HALF], F32)[:] for t in range(4)]
-        first_pair = sb("first_pair", [P, 8, HALF], BF16)
-        rows_first = sb("rows_first", [P, 4, HALF], BF16)
-        rows_last = sb("rows_last", [P, 4, HALF], BF16)
-        late = sb("late", [P, 12, HALF], BF16)
-        woven = {gs: sb(f"woven{gs[0]}{gs[1]}", [P, 4 * HALF], BF16) for gs in gs_pairs[1:]}
-        h_codes = {(g, s): sb(f"h_codes{g}{s}", [P, HALF], U32) for g, s in gs_pairs}
+        b_exact = [sb(f"b_exact{t}", [P, HALF], F32) for t in range(4)]
+        a_bf = {(0, s): sb(f"a_bf0{s}", [P, 4, HALF], BF16) for s in range(2)}
+        b_bf = {(0, s): sb(f"b_bf0{s}", [P, 4, HALF], BF16) for s in range(2)}
+        h_rows = {(1, s): sb(f"h_rows1{s}", [P, 4, HALF], BF16) for s in range(2)}
+        h_bf = {(g, 0): sb(f"h_bf{g}0", [P, 4 * HALF], BF16) for g in range(2)}
+        h_codes = {(g, s): sb(f"h_codes{g}{s}", [P, HALF], U32) for g, s in ((0, 0), (1, 1))}
         h_sc = {(g, s): sb(f"h_sc{g}{s}", [P, HALF], U8) for g, s in gs_pairs}
+        fused = [(1, 0), (2, 0), (1, 1), (2, 1)]
+        ceiling = {u: sb(f"ceiling{u[0]}{u[1]}", [P, HALF], F32) for u in fused}
+        excess = {u: sb(f"excess{u[0]}{u[1]}", [P, HALF], F32) for u in fused}
+        room = {(1, 0): sb("room10", [P, 2 * HALF], F32)}
+        room[1, 1] = room[2, 1] = sb("room1", [P, HALF], F32)
+        picked, capped = {}, {}
         banks = [psum.tile([P, HALF], F32, name=f"bank{b}") for b in range(8)]
-
-        def flat(tile):
-            return tile[:].rearrange("p j c -> p (j c)")
-
-        def by_tile(values):
-            return values.rearrange("p (t c) -> p t c", t=4)
-
-        h_rows = {(0, 0): by_tile(w1_bf[1, 1][:]), (1, 0): rows_first[:], (0, 1): late[:, 0:4, :], (1, 1): rows_last[:]}
-        h_bf = {gs: tile[:] for gs, tile in woven.items()}
-        h_bf[0, 0] = w1_bf[0, 1][:]
-        a_bf = {(0, 0): first_pair[:, 0:4, :], (0, 1): by_tile(w1_bf[1, 0][:]), (1, 1): late[:, 8:12, :]}
-        b_bf = {(0, 0): first_pair[:, 4:8, :], (0, 1): by_tile(w1_bf[0, 0][:]), (1, 1): late[:, 4:8, :]}
-        edge = 4 * HALF - P
-        w2_first = flat(late)[:, edge : edge + 8 * HALF].rearrange("p (u x) -> p u x", u=4)[:, :, 0 : 2 * P]
-        w2_later = {1: woven[0, 1][:, 0 : 8 * P], 2: woven[0, 1][:, 8 * P : 16 * P]}
-        picked = [sb("picked0", [P, HALF], F32)[:], flat(rows_last).bitcast(F32)[:, 0:HALF]]
-        capped = [b_exact[0], b_exact[1]]
-        ceiling, excess = w1_raw[0, 0], w1_raw[1, 0]
-        room = [w1_raw[0, 1][:, place, :] for place in range(3)] + [flat(rows_last).bitcast(F32)[:, HALF : 2 * HALF]]
 
         nc.sync.dma_start(offsets[:], offs)
         nc.gpsimd.memset(tab_sc[:].bitcast(I32), 0)
@@ -106,9 +95,8 @@ def tile_list_marathon_split_caps_kernel(
         def load_table(a):
             nc.sync.dma_start(tab_w[a][:].bitcast(I32), tab_words[a].rearrange("p t i -> p (t i)").bitcast(I32))
 
-        def load_w1(a, g):
-            block = w1[PASS * a : PASS * (a + 1), PASS * g : PASS * (g + 1)]
-            nc.sync.dma_start(w1_raw[a, g][:], block.rearrange("(p j) c -> p j c", j=4))
+        def load_w1(dst, a, lo, hi):
+            nc.sync.dma_start(dst[:], w1[PASS * a : PASS * (a + 1), lo:hi].rearrange("(p j) c -> p j c", j=4))
 
         def load_w4(g):
             nc.sync.dma_start(
@@ -126,30 +114,29 @@ def tile_list_marathon_split_caps_kernel(
 
         tab_rows = tab_scales.bitcast(I32).rearrange("a (q r) c -> r q a c", r=4)
         nc.sync.dma_start(bias_raw[2:4, :], b4.rearrange("(g c) -> g c", g=2))
-        nc.sync.dma_start(bias_raw[0:2, :], b1.rearrange("(g c) -> g c", g=2))
         for r in range(4):
             nc.sync.dma_start(tab_sc[r:P:SHIFT, :].bitcast(I32), tab_rows[r])
         load_table(0)
-        nc.sync.dma_start(bias_raw[QUAD : QUAD + 1, 0:N], b2.rearrange("(o c) -> o c", o=1))
         load_w4(0)
         w4_rows = w4_scales.bitcast(I32).rearrange("a (q r) c -> r q a c", r=4)
         for r in range(4):
             nc.sync.dma_start(w4_sc_raw[r:P:QUAD, :].bitcast(I32).rearrange("q (a c) -> q a c", a=2), w4_rows[r])
         load_table(1)
+        nc.sync.dma_start(bias_raw[0:2, :], b1.rearrange("(g c) -> g c", g=2))
         nc.vector.tensor_copy(v_sc[0][:], tab_sc[:].indirect(offsets[:]))
         for r in range(4):
             nc.sync.dma_start(v_sc[1][r:P:QUAD, :].bitcast(I32), v_sc[0][SHIFT + r : P : QUAD, :].bitcast(I32))
         load_w4(1)
-        load_w1(0, 0)
-        load_w1(1, 0)
-        load_w1(0, 1)
+        for a, g in ag_pairs[:3]:
+            load_w1(w1_raw[a, g], a, PASS * g, PASS * (g + 1))
         for u in range(2):
-            block = w1[PASS : 2 * PASS, PASS + PASS // 2 * u : PASS + PASS // 2 * (u + 1)]
-            nc.sync.dma_start(w1_last[u][:], block.rearrange("(p j) c -> p j c", j=4))
+            load_w1(w1_last[u], 1, PASS + PASS // 2 * u, PASS + PASS // 2 * (u + 1))
         load_page(0)
-        load_page(1)
         load_w2(0)
         load_w2(1)
+        with nc.allow_non_contiguous_dma(reason="one bias value a partition and page"):
+            nc.sync.dma_start(b2_col[:], b2.rearrange("(m p) -> p m", p=P))
+        load_page(1)
         load_page(2)
 
         nc.scalar.activation(
@@ -157,11 +144,9 @@ def tile_list_marathon_split_caps_kernel(
             bias_raw[0:4, :].rearrange("v (j t i) -> v t j i", t=4, i=8),
             ACT.Identity,
         )
-        nc.scalar.activation(bias_rows[QUAD : QUAD + 1, 0:N], bias_raw[QUAD : QUAD + 1, 0:N], ACT.Identity)
         for t in range(4):
             nc.tensor.transpose(banks[7][:, P * t : P * (t + 1)], bias_rows[:, P * t : P * (t + 1)], ident[:])
         nc.scalar.copy(bias[:], banks[7][:].rearrange("p (t c) -> p t c", t=4)[:, :, 0:4])
-        nc.scalar.copy(b2_col[:], banks[7][:, QUAD : QUAD + 3 * P : P])
 
         def half_list(s):
             return offsets[:, HALF // 16 * s : HALF // 16 * (s + 1)]
@@ -169,14 +154,20 @@ def tile_list_marathon_split_caps_kernel(
         def gather_words(a, s):
             nc.vector.tensor_copy(v_words[a, s][:], tab_w[a][:].indirect(half_list(s)))
 
-        def cast_w1_in_order(a, g, halves=range(2)):
+        def cast_w1(a, g):
             dst = w1_bf[a, g][:].rearrange("p (t j i k) -> p t j i k", t=4, i=8, k=4)
             src = w1_raw[a, g][:].rearrange("p k (j t i) -> p t j i k", t=4, i=8)
-            for u in halves:
+            for u in range(2):
                 nc.vector.tensor_copy(dst[:, 2 * u : 2 * u + 2], src[:, 2 * u : 2 * u + 2])
 
-        def quant_w1(a, g, halves=range(2)):
-            for u in halves:
+        def cast_last_w1(u):
+            dst = w1_bf[1, 1][:].rearrange("p (t j i k) -> p t j i k", t=4, i=8, k=4)
+            nc.vector.tensor_copy(
+                dst[:, :, 8 * u : 8 * (u + 1)], w1_last[u][:].rearrange("p k (j t i) -> p t j i k", t=4, i=8)
+            )
+
+        def quant_w1(a, g):
+            for u in range(2):
                 cols = slice(2 * P * u, 2 * P * (u + 1))
                 values = w1_bf[a, g][:, 8 * P * u : 8 * P * (u + 1)]
                 nc.vector.quantize_mx(w1_codes[a, g][:, cols].bitcast(FP8X4), w1_sc[a, g][:, cols], values)
@@ -193,9 +184,6 @@ def tile_list_marathon_split_caps_kernel(
                 w4_raw[g][:].bitcast(I32).rearrange("p (a j t e) -> p a t j e", t=4, j=16, e=4),
             )
 
-        def gather_page(m):
-            nc.vector.tensor_copy(picked[m], page[m][:].indirect(half_list(0)))
-
         def pass_b(g, s, t, a, bank):
             col0 = H * a + PASS * g + P * t
             nc.tensor.matmul_mx(
@@ -211,161 +199,178 @@ def tile_list_marathon_split_caps_kernel(
                 v_words[a, s][:].bitcast(FP8X4), v_sc[a][:, HALF * s : HALF * (s + 1)], start=(a == 0), stop=(a == 1),
             )
 
+        def copy_a(dst, g, t, bank):
+            nc.scalar.activation(dst, banks[bank][:], ACT.Identity, bias=bias[:, t, g : g + 1])
+
         def copy_b(dst, g, t, bank):
             nc.scalar.activation(dst, banks[bank][:], ACT.Identity, bias=bias[:, t, 2 + g : 3 + g])
 
-        def exact_b(t, bank):
+        def rounded_a(g, s, t, bank):
             for a in range(2):
-                pass_b(1, 0, t, a, bank)
-            copy_b(b_exact[t], 1, t, bank)
+                pass_a(g, s, t, a, bank)
+            copy_a(a_bf[g, s][:, t, :], g, t, bank)
 
         def rounded_b(g, s, t, bank):
             for a in range(2):
                 pass_b(g, s, t, a, bank)
             copy_b(b_bf[g, s][:, t, :], g, t, bank)
 
-        def rounded_a(g, s, t, bank):
-            for a in range(2):
-                pass_a(g, s, t, a, bank)
-            nc.scalar.activation(a_bf[g, s][:, t, :], banks[bank][:], ACT.Identity, bias=bias[:, t, g : g + 1])
-
         def rounded_max(g, s):
-            nc.vector.tensor_tensor(h_rows[g, s], a_bf[g, s], b_bf[g, s], ALU.max)
+            nc.vector.tensor_tensor(h_rows[g, s][:], a_bf[g, s][:], b_bf[g, s][:], ALU.max)
 
-        def weave_h(g, s, lo=0, hi=HALF):
+        def scalar_weave(g, s, lo, hi):
             nc.scalar.copy(
                 h_bf[g, s][:, 4 * lo : 4 * hi].rearrange("p (c i t) -> p c t i", i=4, t=4),
                 h_rows[g, s][:, :, lo:hi].rearrange("p t (c i) -> p c t i", i=4),
             )
 
-        def pool_weave_h(g, s, lo=0, hi=HALF):
+        def pool_weave(g, s, lo, hi):
             nc.gpsimd.tensor_scalar(
                 h_bf[g, s][:, 4 * lo : 4 * hi].rearrange("p (c t) -> p c t", t=4),
                 h_rows[g, s][:, :, lo:hi].rearrange("p t c -> p c t"), 1.0, 0.0, ALU.mult, ALU.add,
             )
 
         def quant_h(g, s):
-            nc.vector.quantize_mx(h_codes[g, s][:].bitcast(FP8X4), h_sc[g, s][:], h_bf[g, s])
+            nc.vector.quantize_mx(h_codes[g, s][:].bitcast(FP8X4), h_sc[g, s][:], h_bf[g, s][:])
 
-        def first_w2():
-            for k in range(2):
-                nc.vector.tensor_copy(
-                    w2_first[:, k:4:2, :].rearrange("p g (c i t) -> p g c t i", i=4, t=4),
-                    w2_raw[:, :, :, P // 2 * k : P // 2 * (k + 1)].rearrange("p g t (c i) -> p g c t i", i=4),
-                )
-            for u in range(4):
-                cols = slice(P // 2 * u, P // 2 * (u + 1))
-                nc.vector.quantize_mx(w2_codes[0][:, cols].bitcast(FP8X4), w2_sc[:, cols], w2_first[:, u, :])
-
-        def cast_later_w2(m, copy):
-            copy(
-                w2_later[m].rearrange("p (g c i t) -> p g c t i", g=2, i=4, t=4),
-                w2_raw[:, :, :, P * m : P * (m + 1)].rearrange("p g t (c i) -> p g c t i", i=4),
+        def cast_w2(dst, lo, hi):
+            nc.scalar.copy(
+                dst[:].rearrange("p (g c i t) -> p g c t i", g=2, i=4, t=4),
+                w2_raw[:, :, :, lo:hi].rearrange("p g t (c i) -> p g c t i", i=4),
             )
 
-        def quant_later_w2(m):
-            cols = slice(2 * P * m, 2 * P * (m + 1))
-            nc.vector.quantize_mx(w2_codes[m][:].bitcast(FP8X4), w2_sc[:, cols], w2_later[m])
+        def quant_w2(lo, hi, values):
+            nc.vector.quantize_mx(w2_codes[:, lo:hi].bitcast(FP8X4), w2_sc[:, lo:hi], values[:])
 
         def third_product(m, s, bank):
             for g in range(2):
-                cols = slice(2 * P * m + P * g, 2 * P * m + P * (g + 1))
+                lo = P * g if m == 0 else 2 * P * (g + 1) + P * (m - 1)
                 nc.tensor.matmul_mx(
-                    banks[bank][:], w2_codes[m][:, P * g : P * (g + 1)].bitcast(FP8X4), w2_sc[:, cols],
+                    banks[bank][:], w2_codes[:, lo : lo + P].bitcast(FP8X4), w2_sc[:, lo : lo + P],
                     h_codes[g, s][:].bitcast(FP8X4), h_sc[g, s][:], start=(g == 0), stop=(g == 1),
                 )
 
-        def cap(m, bank):
-            nc.vector.scalar_tensor_tensor(capped[m], banks[bank][:], b2_col[:, m : m + 1], picked[m], ALU.add, ALU.min)
+        def gather_first_page(s):
+            nc.vector.tensor_copy(picked[s][:], page[0][:].indirect(half_list(s)))
 
-        def scatter(m):
-            nc.vector.tensor_copy(page[m][:].indirect(half_list(0)), capped[m])
+        def cap(s, bank):
+            nc.vector.scalar_tensor_tensor(capped[s][:], banks[bank][:], b2_col[:, 0:1], picked[s][:], ALU.add, ALU.min)
 
-        def gather_excess(m, s, place, bank):
-            nc.scalar.activation(ceiling[:, place, :], banks[bank][:], ACT.Identity, bias=b2_col[:, m : m + 1])
-            nc.vector.tensor_tensor(excess[:, place, :], page[m][:].indirect(half_list(s)), ceiling[:, place, :], ALU.subtract)
+        def scatter(s):
+            nc.vector.tensor_copy(page[0][:].indirect(half_list(s)), capped[s][:])
 
-        def scatter_sum(m, s, place):
-            nc.scalar.activation(room[place], excess[:, place, :], ACT.Relu, scale=-1.0)
-            nc.scalar.activation(excess[:, place, :], room[place], ACT.Identity, scale=-1.0)
-            nc.vector.tensor_tensor(page[m][:].indirect(half_list(s)), ceiling[:, place, :], excess[:, place, :], ALU.add)
+        def copy_ceiling(m, s, bank):
+            nc.scalar.activation(ceiling[m, s][:], banks[bank][:], ACT.Identity, bias=b2_col[:, m : m + 1])
+
+        def gather_excess(m, s):
+            nc.vector.tensor_tensor(excess[m, s][:], page[m][:].indirect(half_list(s)), ceiling[m, s][:], ALU.subtract)
+
+        def clip(m, s):
+            nc.scalar.activation(room[m, s][:, 0:HALF], excess[m, s][:], ACT.Relu, scale=-1.0)
+            nc.scalar.activation(excess[m, s][:], room[m, s][:, 0:HALF], ACT.Identity, scale=-1.0)
+
+        def scatter_sum(m, s):
+            nc.vector.tensor_tensor(page[m][:].indirect(half_list(s)), ceiling[m, s][:], excess[m, s][:], ALU.add)
+
+        def store(m):
+            nc.sync.dma_start(out[P * m : P * (m + 1), :], page[m][:])
 
         gather_words(0, 0)
         order_w4_scales()
         order_w4_words(0)
-        v_words[0, 1] = sb("v_words01", [P, HALF], U32, tag="w4_sc_raw")
-        gather_words(0, 1)
         gather_words(1, 0)
-        gather_words(1, 1)
-        w4_codes.append(sb("w4_codes1", [P, 2 * H], U8, tag="tab_w1"))
         order_w4_words(1)
+        for a in range(2):
+            v_words[a, 1] = sb(f"v_words{a}1", [P, HALF], U32, tag=f"w4_raw{1 - a}")
+            gather_words(a, 1)
         for a in range(2):
             for t in range(4):
                 pass_b(0, 0, t, a, t)
         for t in range(4):
             copy_b(b_bf[0, 0][:, t, :], 0, t, t)
+        for t in range(4):
+            for a in range(2):
+                pass_b(1, 0, t, a, 4 + t)
+            copy_b(b_exact[t][:], 1, t, 4 + t)
         for t in range(2):
-            exact_b(t, 4 + t)
+            rounded_b(0, 1, t, 4 + t)
         for a, g in ag_pairs[:3]:
-            cast_w1_in_order(a, g)
+            cast_w1(a, g)
             quant_w1(a, g)
-        last_bf = w1_bf[1, 1][:].rearrange("p (t j i k) -> p t j i k", t=4, i=8, k=4)
         for u in range(2):
-            nc.vector.tensor_copy(
-                last_bf[:, :, 8 * u : 8 * (u + 1)], w1_last[u][:].rearrange("p k (j t i) -> p t j i k", t=4, i=8)
-            )
+            cast_last_w1(u)
         quant_w1(1, 1)
         for t in range(4):
             rounded_a(0, 0, t, t)
         for a in range(2):
             for t in range(4):
                 pass_a(1, 0, t, a, 4 + t)
-        for t in range(2, 4):
-            exact_b(t, t - 2)
-        for t in range(4):
-            rounded_b(0, 1, t, (t + 2) % 4)
+        h_rows[0, 0] = sb("h_rows00", [P, 4, HALF], BF16, tag="w1_bf11")
         rounded_max(0, 0)
-        pool_weave_h(0, 0)
+        pool_weave(0, 0, 0, HALF)
         for t in range(4):
             nc.vector.scalar_tensor_tensor(
-                h_rows[1, 0][:, t, :], banks[4 + t][:], bias[:, t, 1:2], b_exact[t], ALU.add, ALU.max
+                h_rows[1, 0][:, t, :], banks[4 + t][:], bias[:, t, 1:2], b_exact[t][:], ALU.add, ALU.max
             )
-        for t in range(4):
-            rounded_a(0, 1, t, (t + 2) % 4)
-        weave_h(1, 0, 0, SHARE)
-        pool_weave_h(1, 0, SHARE, HALF)
-        gather_page(0)
-        gather_page(1)
+        scalar_weave(1, 0, 0, SHARE)
+        pool_weave(1, 0, SHARE, HALF)
+        for t in range(2, 4):
+            rounded_b(0, 1, t, t - 2)
+        for t, bank in enumerate((2, 4, 5, 6)):
+            rounded_a(0, 1, t, bank)
+        for s in range(2):
+            picked[s] = sb(f"picked{s}", [P, HALF], F32, tag=f"b_exact{2 + s}")
+            gather_first_page(s)
+        cast_w2(w2_first, 0, P)
+        cast_w2(w2_later, P, N)
         quant_h(0, 0)
+        quant_w2(0, 2 * P, w2_first)
+        h_codes[1, 0] = sb("h_codes10", [P, HALF], U32, tag="w2_first")
         quant_h(1, 0)
-        first_w2()
-        third_product(0, 0, 0)
-        cast_later_w2(1, nc.scalar.copy)
-        cast_later_w2(2, nc.vector.tensor_copy)
+        third_product(0, 0, 3)
+        h_rows[0, 1] = sb("h_rows01", [P, 4, HALF], BF16, tag="h_bf10")
         rounded_max(0, 1)
-        quant_later_w2(1)
-        cap(0, 0)
-        w2_codes.append(sb("w2_codes2", [P, 2 * P], U32, tag="picked0"))
-        quant_later_w2(2)
-        pool_weave_h(0, 1)
+        capped[0] = shared.tile([P, HALF], F32, name="capped0", offset=0)
+        cap(0, 3)
+        quant_w2(2 * P, 6 * P, w2_later)
+        h_bf[0, 1] = sb("h_bf01", [P, 4 * HALF], BF16, tag="w2_later")
+        pool_weave(0, 1, 0, HALF)
         scatter(0)
-        quant_h(0, 1)
-        for t in range(4):
-            rounded_b(1, 1, t, 4 + t)
-        for t in range(4):
-            rounded_a(1, 1, t, 1 + t)
-        third_product(1, 0, 3)
-        third_product(2, 0, 4)
-        cap(1, 3)
+        b_bf[1, 1] = shared.tile([P, 4, HALF], BF16, name="b_bf11", offset=4 * HALF)
+        for t, bank in enumerate((7, 4, 5, 6)):
+            rounded_b(1, 1, t, bank)
+        third_product(1, 0, 0)
+        copy_ceiling(1, 0, 0)
+        gather_excess(1, 0)
+        a_bf[1, 1] = shared.tile([P, 4, HALF], BF16, name="a_bf11", offset=12 * HALF)
+        for t, bank in enumerate((3, 7, 4, 5)):
+            rounded_a(1, 1, t, bank)
+        third_product(2, 0, 1)
+        copy_ceiling(2, 0, 1)
         rounded_max(1, 1)
-        gather_excess(2, 0, 3, 4)
-        scatter(1)
-        weave_h(1, 1)
+        gather_excess(2, 0)
+        clip(1, 0)
+        scatter_sum(1, 0)
+        h_bf[1, 1] = sb("h_bf11", [P, 4 * HALF], BF16, tag="room10")
+        scalar_weave(1, 1, 0, HALF)
+        h_codes[0, 1] = sb("h_codes01", [P, HALF], U32, tag="excess10")
+        quant_h(0, 1)
         quant_h(1, 1)
-        scatter_sum(2, 0, 3)
-        for m in range(3):
-            third_product(m, 1, 5 + m)
-            gather_excess(m, 1, m, 5 + m)
-        for m in range(3):
-            scatter_sum(m, 1, m)
-            nc.sync.dma_start(out[P * m : P * (m + 1), :], page[m][:])
+        room[2, 0] = sb("room20", [P, HALF], F32, tag="h_rows11")
+        clip(2, 0)
+        scatter_sum(2, 0)
+        third_product(1, 1, 0)
+        third_product(0, 1, 2)
+        third_product(2, 1, 6)
+        copy_ceiling(1, 1, 0)
+        capped[1] = sb("capped1", [P, HALF], F32, tag="excess20")
+        cap(1, 2)
+        gather_excess(1, 1)
+        scatter(1)
+        store(0)
+        copy_ceiling(2, 1, 6)
+        gather_excess(2, 1)
+        for m in range(1, 3):
+            clip(m, 1)
+            scatter_sum(m, 1)
+            store(m)

@@ -22,6 +22,7 @@ PASS = 512
 HALF = 512
 QUAD = 32
 SHIFT = 16
+FIRST = 16 * HALF
 SHARE = 192
 
 
@@ -53,15 +54,17 @@ def tile_list_marathon_split_caps_kernel(
         w4_raw = [sb(f"w4_raw{g}", [P, 2 * H], U8) for g in range(2)]
         w4_codes = [sb(f"w4_codes{g}", [P, 2 * H], U8) for g in range(2)]
         tab_w = [sb(f"tab_w{a}", [P, T], U32) for a in range(2)]
-        v_words = {(a, 0): sb(f"v_words{a}0", [P, HALF], U32) for a in range(2)}
+        v_words = {(a, s): sb(f"v_words{a}{s}", [P, HALF], U32) for a, s in ag_pairs}
         w1_raw = {(a, g): sb(f"w1_raw{a}{g}", [P, 4, PASS], F32) for a, g in ag_pairs[:3]}
         w1_last = [sb(f"w1_last{u}", [P, 4, PASS // 2], F32) for u in range(2)]
-        w1_bf = {(a, g): sb(f"w1_bf{a}{g}", [P, 4 * PASS], BF16) for a, g in ag_pairs}
+        w1_bf = {(a, g): sb(f"w1_bf{a}{g}", [P, 4 * PASS], BF16) for a, g in ag_pairs[:3]}
+        arena = sb("arena", [P, 6 * PASS], BF16)
+        w1_bf[1, 1] = arena[:, 2 * PASS : 6 * PASS]
         w1_codes = {(a, g): sb(f"w1_codes{a}{g}", [P, PASS], U32) for a, g in ag_pairs}
         w1_sc = {(a, g): sb(f"w1_sc{a}{g}", [P, PASS], U8) for a, g in ag_pairs}
-        w2_raw = shared.tile([P, 2, 4, N], F32, name="w2_raw", offset=0)
-        w2_first = sb("w2_first", [P, 8 * P], BF16)
-        w2_later = sb("w2_later", [P, 16 * P], BF16)
+        w2_raw = [shared.tile([P, 2, 4, 2 * P], F32, name="w2_raw0", offset=0), sb("w2_raw1", [P, 2, 4, P], F32)]
+        w2_bf = [shared.tile([P, 8 * P], BF16, name="w2_bf0", offset=FIRST + 2 * HALF, align_bytes=64)]
+        w2_bf.extend(sb(f"w2_bf{m}", [P, 16 // m * P], BF16) for m in (1, 2))
         w2_codes = sb("w2_codes", [P, 6 * P], U32)
         w2_sc = sb("w2_sc", [P, 6 * P], U8)
         page = [sb(f"page{m}", [P, T], F32) for m in range(3)]
@@ -70,14 +73,14 @@ def tile_list_marathon_split_caps_kernel(
         b_bf = {(0, s): sb(f"b_bf0{s}", [P, 4, HALF], BF16) for s in range(2)}
         h_rows = {(1, s): sb(f"h_rows1{s}", [P, 4, HALF], BF16) for s in range(2)}
         h_bf = {(g, 0): sb(f"h_bf{g}0", [P, 4 * HALF], BF16) for g in range(2)}
-        h_codes = {(g, s): sb(f"h_codes{g}{s}", [P, HALF], U32) for g, s in ((0, 0), (1, 1))}
+        h_codes = {(g, s): sb(f"h_codes{g}{s}", [P, HALF], U32) for g, s in gs_pairs if (g, s) != (1, 0)}
         h_sc = {(g, s): sb(f"h_sc{g}{s}", [P, HALF], U8) for g, s in gs_pairs}
         fused = [(1, 0), (2, 0), (1, 1), (2, 1)]
-        ceiling = {u: sb(f"ceiling{u[0]}{u[1]}", [P, HALF], F32) for u in fused}
+        ceiling = {u: sb(f"ceiling{u[0]}{u[1]}", [P, HALF], F32) for u in fused if u != (2, 0)}
         excess = {u: sb(f"excess{u[0]}{u[1]}", [P, HALF], F32) for u in fused}
-        room = {(1, 0): sb("room10", [P, 2 * HALF], F32)}
+        room = {(2, 0): sb("room20", [P, HALF], F32)}
         room[1, 1] = room[2, 1] = sb("room1", [P, HALF], F32)
-        picked, capped = {}, {}
+        picked, capped = {}, {1: sb("capped1", [P, HALF], F32)}
         banks = [psum.tile([P, HALF], F32, name=f"bank{b}") for b in range(8)]
 
         nc.sync.dma_start(offsets[:], offs)
@@ -107,10 +110,11 @@ def tile_list_marathon_split_caps_kernel(
         def load_page(m):
             nc.sync.dma_start(page[m][:], gT[P * m : P * (m + 1), :])
 
-        def load_w2(g):
-            rows = w2[PASS * g : PASS * (g + 1), :].rearrange("(j t i) n -> t j i n", t=4, i=8)
-            for t in range(4):
-                nc.sync.dma_start(w2_raw[:, g, t, :], rows[t])
+        def load_w2(dst, lo, hi):
+            rows = w2[:, lo:hi].rearrange("(g j t i) n -> g t j i n", g=2, t=4, i=8)
+            for g in range(2):
+                for t in range(4):
+                    nc.sync.dma_start(dst[:, g, t, :], rows[g, t])
 
         tab_rows = tab_scales.bitcast(I32).rearrange("a (q r) c -> r q a c", r=4)
         nc.sync.dma_start(bias_raw[2:4, :], b4.rearrange("(g c) -> g c", g=2))
@@ -123,21 +127,21 @@ def tile_list_marathon_split_caps_kernel(
             nc.sync.dma_start(w4_sc_raw[r:P:QUAD, :].bitcast(I32).rearrange("q (a c) -> q a c", a=2), w4_rows[r])
         load_table(1)
         nc.sync.dma_start(bias_raw[0:2, :], b1.rearrange("(g c) -> g c", g=2))
+        load_w4(1)
         nc.vector.tensor_copy(v_sc[0][:], tab_sc[:].indirect(offsets[:]))
         for r in range(4):
             nc.sync.dma_start(v_sc[1][r:P:QUAD, :].bitcast(I32), v_sc[0][SHIFT + r : P : QUAD, :].bitcast(I32))
-        load_w4(1)
         for a, g in ag_pairs[:3]:
             load_w1(w1_raw[a, g], a, PASS * g, PASS * (g + 1))
         for u in range(2):
             load_w1(w1_last[u], 1, PASS + PASS // 2 * u, PASS + PASS // 2 * (u + 1))
-        load_page(0)
-        load_w2(0)
-        load_w2(1)
         with nc.allow_non_contiguous_dma(reason="one bias value a partition and page"):
             nc.sync.dma_start(b2_col[:], b2.rearrange("(m p) -> p m", p=P))
+        load_page(0)
+        load_w2(w2_raw[0], 0, 2 * P)
         load_page(1)
         load_page(2)
+        load_w2(w2_raw[1], 2 * P, N)
 
         nc.scalar.activation(
             bias_rows[0:4, :].rearrange("v (t j i) -> v t j i", t=4, i=8),
@@ -160,11 +164,10 @@ def tile_list_marathon_split_caps_kernel(
             for u in range(2):
                 nc.vector.tensor_copy(dst[:, 2 * u : 2 * u + 2], src[:, 2 * u : 2 * u + 2])
 
-        def cast_last_w1(u):
-            dst = w1_bf[1, 1][:].rearrange("p (t j i k) -> p t j i k", t=4, i=8, k=4)
-            nc.vector.tensor_copy(
-                dst[:, :, 8 * u : 8 * (u + 1)], w1_last[u][:].rearrange("p k (j t i) -> p t j i k", t=4, i=8)
-            )
+        def cast_last_w1(u, lo, hi):
+            dst = w1_bf[1, 1].rearrange("p (t j i k) -> p t j i k", t=4, i=8, k=4)
+            src = w1_last[u][:].rearrange("p k (j t i) -> p t j i k", t=4, i=8)
+            nc.vector.tensor_copy(dst[:, lo:hi, 8 * u : 8 * (u + 1)], src[:, lo:hi])
 
         def quant_w1(a, g):
             for u in range(2):
@@ -173,23 +176,23 @@ def tile_list_marathon_split_caps_kernel(
                 nc.vector.quantize_mx(w1_codes[a, g][:, cols].bitcast(FP8X4), w1_sc[a, g][:, cols], values)
 
         def order_w4_scales():
-            nc.vector.tensor_copy(
-                w4_sc[:].bitcast(I32).rearrange("p (u t j e) -> p u t j e", t=4, j=16, e=2),
-                w4_sc_raw[:].bitcast(I32).rearrange("p (u j t e) -> p u t j e", t=4, j=16, e=2),
+            nc.scalar.copy(
+                w4_sc[:].bitcast(U32).rearrange("p (u t j e) -> p u t j e", t=4, j=16, e=2),
+                w4_sc_raw[:].bitcast(U32).rearrange("p (u j t e) -> p u t j e", t=4, j=16, e=2),
             )
 
         def order_w4_words(g):
-            nc.vector.tensor_copy(
-                w4_codes[g][:].bitcast(I32).rearrange("p (a t j e) -> p a t j e", t=4, j=16, e=4),
-                w4_raw[g][:].bitcast(I32).rearrange("p (a j t e) -> p a t j e", t=4, j=16, e=4),
+            nc.scalar.copy(
+                w4_codes[g][:].bitcast(U32).rearrange("p (a t j e) -> p a t j e", t=4, j=16, e=4),
+                w4_raw[g][:].bitcast(U32).rearrange("p (a j t e) -> p a t j e", t=4, j=16, e=4),
             )
 
-        def pass_b(g, s, t, a, bank):
+        def pass_b(g, s, t, a, bank, first=0):
             col0 = H * a + PASS * g + P * t
             nc.tensor.matmul_mx(
                 banks[bank][:], w4_codes[g][:, 2 * (PASS * a + P * t) : 2 * (PASS * a + P * (t + 1))].bitcast(FP4X4),
                 w4_sc[:, col0 : col0 + P], v_words[a, s][:].bitcast(FP8X4), v_sc[a][:, HALF * s : HALF * (s + 1)],
-                start=(a == 0), stop=(a == 1),
+                start=(a == first), stop=(a != first),
             )
 
         def pass_a(g, s, t, a, bank):
@@ -233,20 +236,21 @@ def tile_list_marathon_split_caps_kernel(
         def quant_h(g, s):
             nc.vector.quantize_mx(h_codes[g, s][:].bitcast(FP8X4), h_sc[g, s][:], h_bf[g, s][:])
 
-        def cast_w2(dst, lo, hi):
+        def cast_w2(m):
             nc.scalar.copy(
-                dst[:].rearrange("p (g c i t) -> p g c t i", g=2, i=4, t=4),
-                w2_raw[:, :, :, lo:hi].rearrange("p g t (c i) -> p g c t i", i=4),
+                w2_bf[m][:, 0 : 8 * P].rearrange("p (g c i t) -> p g c t i", g=2, i=4, t=4),
+                w2_raw[m // 2][:, :, :, P * (m % 2) : P * (m % 2 + 1)].rearrange("p g t (c i) -> p g c t i", i=4),
             )
 
-        def quant_w2(lo, hi, values):
-            nc.vector.quantize_mx(w2_codes[:, lo:hi].bitcast(FP8X4), w2_sc[:, lo:hi], values[:])
+        def quant_w2(m):
+            cols = slice(2 * P * m, 2 * P * (m + 1))
+            nc.vector.quantize_mx(w2_codes[:, cols].bitcast(FP8X4), w2_sc[:, cols], w2_bf[m][:, 0 : 8 * P])
 
         def third_product(m, s, bank):
             for g in range(2):
-                lo = P * g if m == 0 else 2 * P * (g + 1) + P * (m - 1)
+                cols = slice(P * (2 * m + g), P * (2 * m + g + 1))
                 nc.tensor.matmul_mx(
-                    banks[bank][:], w2_codes[:, lo : lo + P].bitcast(FP8X4), w2_sc[:, lo : lo + P],
+                    banks[bank][:], w2_codes[:, cols].bitcast(FP8X4), w2_sc[:, cols],
                     h_codes[g, s][:].bitcast(FP8X4), h_sc[g, s][:], start=(g == 0), stop=(g == 1),
                 )
 
@@ -275,37 +279,36 @@ def tile_list_marathon_split_caps_kernel(
         def store(m):
             nc.sync.dma_start(out[P * m : P * (m + 1), :], page[m][:])
 
-        gather_words(0, 0)
-        order_w4_scales()
         order_w4_words(0)
-        gather_words(1, 0)
+        order_w4_scales()
         order_w4_words(1)
         for a in range(2):
-            v_words[a, 1] = sb(f"v_words{a}1", [P, HALF], U32, tag=f"w4_raw{1 - a}")
-            gather_words(a, 1)
+            for s in range(2):
+                gather_words(a, s)
         for a in range(2):
             for t in range(4):
                 pass_b(0, 0, t, a, t)
         for t in range(4):
             copy_b(b_bf[0, 0][:, t, :], 0, t, t)
         for t in range(4):
-            for a in range(2):
-                pass_b(1, 0, t, a, 4 + t)
+            for a in (1, 0):
+                pass_b(1, 0, t, a, 4 + t, first=1)
             copy_b(b_exact[t][:], 1, t, 4 + t)
         for t in range(2):
             rounded_b(0, 1, t, 4 + t)
         for a, g in ag_pairs[:3]:
             cast_w1(a, g)
             quant_w1(a, g)
-        for u in range(2):
-            cast_last_w1(u)
+        cast_last_w1(0, 0, 4)
+        cast_last_w1(1, 0, 2)
+        cast_last_w1(1, 2, 4)
         quant_w1(1, 1)
         for t in range(4):
             rounded_a(0, 0, t, t)
         for a in range(2):
             for t in range(4):
                 pass_a(1, 0, t, a, 4 + t)
-        h_rows[0, 0] = sb("h_rows00", [P, 4, HALF], BF16, tag="w1_bf11")
+        h_rows[0, 0] = arena[:, 0 : 4 * HALF].rearrange("p (t c) -> p t c", t=4)
         rounded_max(0, 0)
         pool_weave(0, 0, 0, HALF)
         for t in range(4):
@@ -321,19 +324,19 @@ def tile_list_marathon_split_caps_kernel(
         for s in range(2):
             picked[s] = sb(f"picked{s}", [P, HALF], F32, tag=f"b_exact{2 + s}")
             gather_first_page(s)
-        cast_w2(w2_first, 0, P)
-        cast_w2(w2_later, P, N)
+        cast_w2(0)
+        cast_w2(1)
         quant_h(0, 0)
-        quant_w2(0, 2 * P, w2_first)
-        h_codes[1, 0] = sb("h_codes10", [P, HALF], U32, tag="w2_first")
+        quant_w2(0)
+        h_codes[1, 0] = shared.tile([P, HALF], U32, name="h_codes10", offset=FIRST, align_bytes=64)
         quant_h(1, 0)
         third_product(0, 0, 3)
-        h_rows[0, 1] = sb("h_rows01", [P, 4, HALF], BF16, tag="h_bf10")
+        h_rows[0, 1] = shared.tile([P, 4, HALF], BF16, name="h_rows01", offset=FIRST + 4 * HALF)
         rounded_max(0, 1)
         capped[0] = shared.tile([P, HALF], F32, name="capped0", offset=0)
         cap(0, 3)
-        quant_w2(2 * P, 6 * P, w2_later)
-        h_bf[0, 1] = sb("h_bf01", [P, 4 * HALF], BF16, tag="w2_later")
+        quant_w2(1)
+        h_bf[0, 1] = sb("h_bf01", [P, 4 * HALF], BF16, tag="w2_bf1")
         pool_weave(0, 1, 0, HALF)
         scatter(0)
         b_bf[1, 1] = shared.tile([P, 4, HALF], BF16, name="b_bf11", offset=4 * HALF)
@@ -342,35 +345,33 @@ def tile_list_marathon_split_caps_kernel(
         third_product(1, 0, 0)
         copy_ceiling(1, 0, 0)
         gather_excess(1, 0)
-        a_bf[1, 1] = shared.tile([P, 4, HALF], BF16, name="a_bf11", offset=12 * HALF)
-        for t, bank in enumerate((3, 7, 4, 5)):
+        a_bf[1, 1] = sb("a_bf11", [P, 4, HALF], BF16)
+        for t, bank in enumerate((7, 4, 5, 3)):
             rounded_a(1, 1, t, bank)
-        third_product(2, 0, 1)
-        copy_ceiling(2, 0, 1)
+        quant_h(0, 1)
         rounded_max(1, 1)
-        gather_excess(2, 0)
+        cast_w2(2)
+        quant_w2(2)
+        room[1, 0] = sb("room10", [P, HALF], F32, tag="w2_raw1")
         clip(1, 0)
         scatter_sum(1, 0)
-        h_bf[1, 1] = sb("h_bf11", [P, 4 * HALF], BF16, tag="room10")
+        h_bf[1, 1] = sb("h_bf11", [P, 4 * HALF], BF16, tag="w2_raw1")
         scalar_weave(1, 1, 0, HALF)
-        h_codes[0, 1] = sb("h_codes01", [P, HALF], U32, tag="excess10")
-        quant_h(0, 1)
         quant_h(1, 1)
-        room[2, 0] = sb("room20", [P, HALF], F32, tag="h_rows11")
-        clip(2, 0)
-        scatter_sum(2, 0)
-        third_product(1, 1, 0)
-        third_product(0, 1, 2)
-        third_product(2, 1, 6)
-        copy_ceiling(1, 1, 0)
-        capped[1] = sb("capped1", [P, HALF], F32, tag="excess20")
+        third_product(2, 0, 1)
+        ceiling[2, 0] = sb("ceiling20", [P, HALF], F32, tag="h_rows11")
+        copy_ceiling(2, 0, 1)
+        gather_excess(2, 0)
+        for m, bank in ((2, 6), (1, 0), (0, 2)):
+            third_product(m, 1, bank)
         cap(1, 2)
-        gather_excess(1, 1)
+        for m, bank in ((2, 6), (1, 0)):
+            copy_ceiling(m, 1, bank)
+            gather_excess(m, 1)
         scatter(1)
         store(0)
-        copy_ceiling(2, 1, 6)
-        gather_excess(2, 1)
-        for m in range(1, 3):
-            clip(m, 1)
-            scatter_sum(m, 1)
-            store(m)
+        for m, s in fused[1:]:
+            clip(m, s)
+            scatter_sum(m, s)
+            if s == 1:
+                store(m)

@@ -23,6 +23,7 @@ HALF = 512
 QUAD = 32
 SHIFT = 16
 FIRST = 16 * HALF
+EARLY_SHARE = 256
 SHARE = 192
 
 
@@ -310,11 +311,12 @@ def tile_list_marathon_split_caps_kernel(
                 pass_a(1, 0, t, a, 4 + t)
         h_rows[0, 0] = arena[:, 0 : 4 * HALF].rearrange("p (t c) -> p t c", t=4)
         rounded_max(0, 0)
-        pool_weave(0, 0, 0, HALF)
+        pool_weave(0, 0, EARLY_SHARE, HALF)
         for t in range(4):
             nc.vector.scalar_tensor_tensor(
                 h_rows[1, 0][:, t, :], banks[4 + t][:], bias[:, t, 1:2], b_exact[t][:], ALU.add, ALU.max
             )
+        scalar_weave(0, 0, 0, EARLY_SHARE)
         scalar_weave(1, 0, 0, SHARE)
         pool_weave(1, 0, SHARE, HALF)
         for t in range(2, 4):

@@ -24,6 +24,7 @@ QUAD = 32
 SHIFT = 16
 FIRST = 16 * HALF
 EARLY_SHARE = 256
+LAST_SHARE = 96
 SHARE = 192
 
 
@@ -65,7 +66,7 @@ def tile_list_marathon_split_caps_kernel(
         w1_sc = {(a, g): sb(f"w1_sc{a}{g}", [P, PASS], U8) for a, g in ag_pairs}
         w2_raw = [shared.tile([P, 2, 4, 2 * P], F32, name="w2_raw0", offset=0), sb("w2_raw1", [P, 2, 4, P], F32)]
         w2_bf = [shared.tile([P, 8 * P], BF16, name="w2_bf0", offset=FIRST + 2 * HALF, align_bytes=64)]
-        w2_bf.extend(sb(f"w2_bf{m}", [P, 16 // m * P], BF16) for m in (1, 2))
+        w2_bf.extend(sb(f"w2_bf{m}", [P, 16 * P], BF16) for m in (1, 2))
         w2_codes = sb("w2_codes", [P, 6 * P], U32)
         w2_sc = sb("w2_sc", [P, 6 * P], U8)
         page = [sb(f"page{m}", [P, T], F32) for m in range(3)]
@@ -74,14 +75,14 @@ def tile_list_marathon_split_caps_kernel(
         b_bf = {(0, s): sb(f"b_bf0{s}", [P, 4, HALF], BF16) for s in range(2)}
         h_rows = {(1, s): sb(f"h_rows1{s}", [P, 4, HALF], BF16) for s in range(2)}
         h_bf = {(g, 0): sb(f"h_bf{g}0", [P, 4 * HALF], BF16) for g in range(2)}
-        h_codes = {(g, s): sb(f"h_codes{g}{s}", [P, HALF], U32) for g, s in gs_pairs if (g, s) != (1, 0)}
+        h_codes = {(g, s): sb(f"h_codes{g}{s}", [P, HALF], U32) for g, s in gs_pairs if (g, s) != (0, 1)}
         h_sc = {(g, s): sb(f"h_sc{g}{s}", [P, HALF], U8) for g, s in gs_pairs}
-        fused = [(1, 0), (2, 0), (1, 1), (2, 1)]
-        ceiling = {u: sb(f"ceiling{u[0]}{u[1]}", [P, HALF], F32) for u in fused if u != (2, 0)}
+        fused = [(2, 0), (1, 1), (2, 1)]
+        ceiling = {u: sb(f"ceiling{u[0]}{u[1]}", [P, HALF], F32) for u in fused}
         excess = {u: sb(f"excess{u[0]}{u[1]}", [P, HALF], F32) for u in fused}
         room = {(2, 0): sb("room20", [P, HALF], F32)}
         room[1, 1] = room[2, 1] = sb("room1", [P, HALF], F32)
-        picked, capped = {}, {1: sb("capped1", [P, HALF], F32)}
+        picked, capped = {(1, 0): sb("picked10", [P, HALF], F32)}, {}
         banks = [psum.tile([P, HALF], F32, name=f"bank{b}") for b in range(8)]
 
         nc.sync.dma_start(offsets[:], offs)
@@ -136,11 +137,11 @@ def tile_list_marathon_split_caps_kernel(
             load_w1(w1_raw[a, g], a, PASS * g, PASS * (g + 1))
         for u in range(2):
             load_w1(w1_last[u], 1, PASS + PASS // 2 * u, PASS + PASS // 2 * (u + 1))
-        with nc.allow_non_contiguous_dma(reason="one bias value a partition and page"):
-            nc.sync.dma_start(b2_col[:], b2.rearrange("(m p) -> p m", p=P))
         load_page(0)
         load_w2(w2_raw[0], 0, 2 * P)
         load_page(1)
+        with nc.allow_non_contiguous_dma(reason="one bias value a partition and page"):
+            nc.sync.dma_start(b2_col[:], b2.rearrange("(m p) -> p m", p=P))
         load_page(2)
         load_w2(w2_raw[1], 2 * P, N)
 
@@ -255,14 +256,16 @@ def tile_list_marathon_split_caps_kernel(
                     h_codes[g, s][:].bitcast(FP8X4), h_sc[g, s][:], start=(g == 0), stop=(g == 1),
                 )
 
-        def gather_first_page(s):
-            nc.vector.tensor_copy(picked[s][:], page[0][:].indirect(half_list(s)))
+        def gather(m, s):
+            nc.vector.tensor_copy(picked[m, s][:], page[m][:].indirect(half_list(s)))
 
-        def cap(s, bank):
-            nc.vector.scalar_tensor_tensor(capped[s][:], banks[bank][:], b2_col[:, 0:1], picked[s][:], ALU.add, ALU.min)
+        def cap(m, s, bank):
+            nc.vector.scalar_tensor_tensor(
+                capped[m, s][:], banks[bank][:], b2_col[:, m : m + 1], picked[m, s][:], ALU.add, ALU.min
+            )
 
-        def scatter(s):
-            nc.vector.tensor_copy(page[0][:].indirect(half_list(s)), capped[s][:])
+        def scatter(m, s):
+            nc.vector.tensor_copy(page[m][:].indirect(half_list(s)), capped[m, s][:])
 
         def copy_ceiling(m, s, bank):
             nc.scalar.activation(ceiling[m, s][:], banks[bank][:], ACT.Identity, bias=b2_col[:, m : m + 1])
@@ -324,56 +327,58 @@ def tile_list_marathon_split_caps_kernel(
         for t, bank in enumerate((2, 4, 5, 6)):
             rounded_a(0, 1, t, bank)
         for s in range(2):
-            picked[s] = sb(f"picked{s}", [P, HALF], F32, tag=f"b_exact{2 + s}")
-            gather_first_page(s)
+            picked[0, s] = sb(f"picked0{s}", [P, HALF], F32, tag=f"b_exact{2 + s}")
+            gather(0, s)
         cast_w2(0)
         cast_w2(1)
         quant_h(0, 0)
-        quant_w2(0)
-        h_codes[1, 0] = shared.tile([P, HALF], U32, name="h_codes10", offset=FIRST, align_bytes=64)
         quant_h(1, 0)
+        quant_w2(0)
         third_product(0, 0, 3)
         h_rows[0, 1] = shared.tile([P, 4, HALF], BF16, name="h_rows01", offset=FIRST + 4 * HALF)
         rounded_max(0, 1)
-        capped[0] = shared.tile([P, HALF], F32, name="capped0", offset=0)
-        cap(0, 3)
         quant_w2(1)
         h_bf[0, 1] = sb("h_bf01", [P, 4 * HALF], BF16, tag="w2_bf1")
         pool_weave(0, 1, 0, HALF)
-        scatter(0)
-        b_bf[1, 1] = shared.tile([P, 4, HALF], BF16, name="b_bf11", offset=4 * HALF)
+        gather(1, 0)
+        capped[0, 0] = sb("capped00", [P, HALF], F32)
+        cap(0, 0, 3)
+        scatter(0, 0)
+        b_bf[1, 1] = shared.tile([P, 4, HALF], BF16, name="b_bf11", offset=0)
         for t, bank in enumerate((7, 4, 5, 6)):
             rounded_b(1, 1, t, bank)
         third_product(1, 0, 0)
-        copy_ceiling(1, 0, 0)
-        gather_excess(1, 0)
         a_bf[1, 1] = sb("a_bf11", [P, 4, HALF], BF16)
         for t, bank in enumerate((7, 4, 5, 3)):
             rounded_a(1, 1, t, bank)
-        quant_h(0, 1)
         rounded_max(1, 1)
         cast_w2(2)
+        capped[1, 0] = sb("capped10", [P, HALF], F32, tag="w2_raw1")
+        cap(1, 0, 0)
         quant_w2(2)
-        room[1, 0] = sb("room10", [P, HALF], F32, tag="w2_raw1")
-        clip(1, 0)
-        scatter_sum(1, 0)
-        h_bf[1, 1] = sb("h_bf11", [P, 4 * HALF], BF16, tag="w2_raw1")
-        scalar_weave(1, 1, 0, HALF)
-        quant_h(1, 1)
+        h_bf[1, 1] = sb("h_bf11", [P, 4 * HALF], BF16, tag="w2_bf2")
+        pool_weave(1, 1, LAST_SHARE, HALF)
+        scalar_weave(1, 1, 0, LAST_SHARE)
+        scatter(1, 0)
         third_product(2, 0, 1)
-        ceiling[2, 0] = sb("ceiling20", [P, HALF], F32, tag="h_rows11")
         copy_ceiling(2, 0, 1)
         gather_excess(2, 0)
-        for m, bank in ((2, 6), (1, 0), (0, 2)):
+        h_codes[0, 1] = sb("h_codes01", [P, HALF], U32, tag="h_rows11")
+        quant_h(0, 1)
+        quant_h(1, 1)
+        clip(2, 0)
+        scatter_sum(2, 0)
+        for m, bank in ((1, 0), (0, 2), (2, 6)):
             third_product(m, 1, bank)
-        cap(1, 2)
-        for m, bank in ((2, 6), (1, 0)):
-            copy_ceiling(m, 1, bank)
-            gather_excess(m, 1)
-        scatter(1)
+        capped[0, 1] = sb("capped01", [P, HALF], F32, tag="room20")
+        cap(0, 1, 2)
+        copy_ceiling(1, 1, 0)
+        gather_excess(1, 1)
+        scatter(0, 1)
         store(0)
-        for m, s in fused[1:]:
-            clip(m, s)
-            scatter_sum(m, s)
-            if s == 1:
-                store(m)
+        copy_ceiling(2, 1, 6)
+        gather_excess(2, 1)
+        for m in (1, 2):
+            clip(m, 1)
+            scatter_sum(m, 1)
+            store(m)

@@ -22,10 +22,10 @@ PASS = 512
 HALF = 512
 QUAD = 32
 SHIFT = 16
-FIRST = 16 * HALF
+FIRST = 8 * HALF
 EARLY_SHARE = 256
 LAST_SHARE = 96
-SHARE = 192
+SHARE = 128
 
 
 def tile_list_marathon_split_caps_kernel(
@@ -64,7 +64,8 @@ def tile_list_marathon_split_caps_kernel(
         w1_bf[1, 1] = arena[:, 2 * PASS : 6 * PASS]
         w1_codes = {(a, g): sb(f"w1_codes{a}{g}", [P, PASS], U32) for a, g in ag_pairs}
         w1_sc = {(a, g): sb(f"w1_sc{a}{g}", [P, PASS], U8) for a, g in ag_pairs}
-        w2_raw = [shared.tile([P, 2, 4, 2 * P], F32, name="w2_raw0", offset=0), sb("w2_raw1", [P, 2, 4, P], F32)]
+        w2_early = [sb("w2_early0", [P, 4, 2 * P], F32), shared.tile([P, 4, 2 * P], F32, name="w2_early1", offset=0)]
+        w2_late = sb("w2_late", [P, 2, 4, P], F32)
         w2_bf = [shared.tile([P, 8 * P], BF16, name="w2_bf0", offset=FIRST + 2 * HALF, align_bytes=64)]
         w2_bf.extend(sb(f"w2_bf{m}", [P, 16 * P], BF16) for m in (1, 2))
         w2_codes = sb("w2_codes", [P, 6 * P], U32)
@@ -112,11 +113,10 @@ def tile_list_marathon_split_caps_kernel(
         def load_page(m):
             nc.sync.dma_start(page[m][:], gT[P * m : P * (m + 1), :])
 
-        def load_w2(dst, lo, hi):
-            rows = w2[:, lo:hi].rearrange("(g j t i) n -> g t j i n", g=2, t=4, i=8)
-            for g in range(2):
-                for t in range(4):
-                    nc.sync.dma_start(dst[:, g, t, :], rows[g, t])
+        def load_w2(dst, g, lo, hi):
+            rows = w2[PASS * g : PASS * (g + 1), lo:hi].rearrange("(j t i) n -> t j i n", t=4, i=8)
+            for t in range(4):
+                nc.sync.dma_start(dst[:, t, :], rows[t])
 
         tab_rows = tab_scales.bitcast(I32).rearrange("a (q r) c -> r q a c", r=4)
         nc.sync.dma_start(bias_raw[2:4, :], b4.rearrange("(g c) -> g c", g=2))
@@ -137,13 +137,15 @@ def tile_list_marathon_split_caps_kernel(
             load_w1(w1_raw[a, g], a, PASS * g, PASS * (g + 1))
         for u in range(2):
             load_w1(w1_last[u], 1, PASS + PASS // 2 * u, PASS + PASS // 2 * (u + 1))
+        load_w2(w2_early[0], 0, 0, 2 * P)
         load_page(0)
-        load_w2(w2_raw[0], 0, 2 * P)
+        load_w2(w2_early[1], 1, 0, 2 * P)
         load_page(1)
         with nc.allow_non_contiguous_dma(reason="one bias value a partition and page"):
             nc.sync.dma_start(b2_col[:], b2.rearrange("(m p) -> p m", p=P))
         load_page(2)
-        load_w2(w2_raw[1], 2 * P, N)
+        for g in range(2):
+            load_w2(w2_late[:, g], g, 2 * P, N)
 
         nc.scalar.activation(
             bias_rows[0:4, :].rearrange("v (t j i) -> v t j i", t=4, i=8),
@@ -238,10 +240,16 @@ def tile_list_marathon_split_caps_kernel(
         def quant_h(g, s):
             nc.vector.quantize_mx(h_codes[g, s][:].bitcast(FP8X4), h_sc[g, s][:], h_bf[g, s][:])
 
-        def cast_w2(m):
+        def cast_early_w2(m, g):
             nc.scalar.copy(
-                w2_bf[m][:, 0 : 8 * P].rearrange("p (g c i t) -> p g c t i", g=2, i=4, t=4),
-                w2_raw[m // 2][:, :, :, P * (m % 2) : P * (m % 2 + 1)].rearrange("p g t (c i) -> p g c t i", i=4),
+                w2_bf[m][:, 4 * P * g : 4 * P * (g + 1)].rearrange("p (c i t) -> p c t i", i=4, t=4),
+                w2_early[g][:, :, P * m : P * (m + 1)].rearrange("p t (c i) -> p c t i", i=4),
+            )
+
+        def cast_late_w2():
+            nc.scalar.copy(
+                w2_bf[2][:, 0 : 8 * P].rearrange("p (g c i t) -> p g c t i", g=2, i=4, t=4),
+                w2_late[:].rearrange("p g t (c i) -> p g c t i", i=4),
             )
 
         def quant_w2(m):
@@ -298,8 +306,6 @@ def tile_list_marathon_split_caps_kernel(
             for a in (1, 0):
                 pass_b(1, 0, t, a, 4 + t, first=1)
             copy_b(b_exact[t][:], 1, t, 4 + t)
-        for t in range(2):
-            rounded_b(0, 1, t, 4 + t)
         for a, g in ag_pairs[:3]:
             cast_w1(a, g)
             quant_w1(a, g)
@@ -320,17 +326,19 @@ def tile_list_marathon_split_caps_kernel(
                 h_rows[1, 0][:, t, :], banks[4 + t][:], bias[:, t, 1:2], b_exact[t][:], ALU.add, ALU.max
             )
         scalar_weave(0, 0, 0, EARLY_SHARE)
+        for m in range(2):
+            cast_early_w2(m, 0)
         scalar_weave(1, 0, 0, SHARE)
         pool_weave(1, 0, SHARE, HALF)
-        for t in range(2, 4):
-            rounded_b(0, 1, t, t - 2)
-        for t, bank in enumerate((2, 4, 5, 6)):
+        for t, bank in enumerate((0, 1, 2, 4)):
+            rounded_b(0, 1, t, bank)
+        for t, bank in enumerate((5, 6, 7, 4)):
             rounded_a(0, 1, t, bank)
         for s in range(2):
             picked[0, s] = sb(f"picked0{s}", [P, HALF], F32, tag=f"b_exact{2 + s}")
             gather(0, s)
-        cast_w2(0)
-        cast_w2(1)
+        for m in range(2):
+            cast_early_w2(m, 1)
         quant_h(0, 0)
         quant_h(1, 0)
         quant_w2(0)
@@ -345,15 +353,15 @@ def tile_list_marathon_split_caps_kernel(
         cap(0, 0, 3)
         scatter(0, 0)
         b_bf[1, 1] = shared.tile([P, 4, HALF], BF16, name="b_bf11", offset=0)
-        for t, bank in enumerate((7, 4, 5, 6)):
+        for t, bank in enumerate((5, 6, 7, 4)):
             rounded_b(1, 1, t, bank)
         third_product(1, 0, 0)
         a_bf[1, 1] = sb("a_bf11", [P, 4, HALF], BF16)
-        for t, bank in enumerate((7, 4, 5, 3)):
+        for t, bank in enumerate((5, 6, 7, 3)):
             rounded_a(1, 1, t, bank)
         rounded_max(1, 1)
-        cast_w2(2)
-        capped[1, 0] = sb("capped10", [P, HALF], F32, tag="w2_raw1")
+        cast_late_w2()
+        capped[1, 0] = sb("capped10", [P, HALF], F32, tag="w2_late")
         cap(1, 0, 0)
         quant_w2(2)
         h_bf[1, 1] = sb("h_bf11", [P, 4 * HALF], BF16, tag="w2_bf2")
@@ -368,7 +376,7 @@ def tile_list_marathon_split_caps_kernel(
         quant_h(1, 1)
         clip(2, 0)
         scatter_sum(2, 0)
-        for m, bank in ((1, 0), (0, 2), (2, 6)):
+        for m, bank in ((1, 0), (0, 2), (2, 4)):
             third_product(m, 1, bank)
         capped[0, 1] = sb("capped01", [P, HALF], F32, tag="room20")
         cap(0, 1, 2)
@@ -376,7 +384,7 @@ def tile_list_marathon_split_caps_kernel(
         gather_excess(1, 1)
         scatter(0, 1)
         store(0)
-        copy_ceiling(2, 1, 6)
+        copy_ceiling(2, 1, 4)
         gather_excess(2, 1)
         for m in (1, 2):
             clip(m, 1)

@@ -23,9 +23,9 @@ HALF = 512
 QUAD = 32
 SHIFT = 16
 FIRST = 8 * HALF
-EARLY_SHARE = 256
+TAIL = 192
 LAST_SHARE = 96
-SHARE = 128
+SHARE = 192
 
 
 def tile_list_marathon_split_caps_kernel(
@@ -58,7 +58,8 @@ def tile_list_marathon_split_caps_kernel(
         tab_w = [sb(f"tab_w{a}", [P, T], U32) for a in range(2)]
         v_words = {(a, s): sb(f"v_words{a}{s}", [P, HALF], U32) for a, s in ag_pairs}
         w1_raw = {(a, g): sb(f"w1_raw{a}{g}", [P, 4, PASS], F32) for a, g in ag_pairs[:3]}
-        w1_last = [sb(f"w1_last{u}", [P, 4, PASS // 2], F32) for u in range(2)]
+        last_cols = ((0, PASS - TAIL), (PASS - TAIL, PASS))
+        w1_last = [sb(f"w1_last{u}", [P, 4, hi - lo], F32) for u, (lo, hi) in enumerate(last_cols)]
         w1_bf = {(a, g): sb(f"w1_bf{a}{g}", [P, 4 * PASS], BF16) for a, g in ag_pairs[:3]}
         arena = sb("arena", [P, 6 * PASS], BF16)
         w1_bf[1, 1] = arena[:, 2 * PASS : 6 * PASS]
@@ -76,7 +77,7 @@ def tile_list_marathon_split_caps_kernel(
         b_bf = {(0, s): sb(f"b_bf0{s}", [P, 4, HALF], BF16) for s in range(2)}
         h_rows = {(1, s): sb(f"h_rows1{s}", [P, 4, HALF], BF16) for s in range(2)}
         h_bf = {(g, 0): sb(f"h_bf{g}0", [P, 4 * HALF], BF16) for g in range(2)}
-        h_codes = {(g, s): sb(f"h_codes{g}{s}", [P, HALF], U32) for g, s in gs_pairs if (g, s) != (0, 1)}
+        h_codes = {(g, s): sb(f"h_codes{g}{s}", [P, HALF], U32) for g, s in gs_pairs if g == 1}
         h_sc = {(g, s): sb(f"h_sc{g}{s}", [P, HALF], U8) for g, s in gs_pairs}
         fused = [(2, 0), (1, 1), (2, 1)]
         ceiling = {u: sb(f"ceiling{u[0]}{u[1]}", [P, HALF], F32) for u in fused}
@@ -135,8 +136,8 @@ def tile_list_marathon_split_caps_kernel(
             nc.sync.dma_start(v_sc[1][r:P:QUAD, :].bitcast(I32), v_sc[0][SHIFT + r : P : QUAD, :].bitcast(I32))
         for a, g in ag_pairs[:3]:
             load_w1(w1_raw[a, g], a, PASS * g, PASS * (g + 1))
-        for u in range(2):
-            load_w1(w1_last[u], 1, PASS + PASS // 2 * u, PASS + PASS // 2 * (u + 1))
+        for u, (lo, hi) in enumerate(last_cols):
+            load_w1(w1_last[u], 1, PASS + lo, PASS + hi)
         load_w2(w2_early[0], 0, 0, 2 * P)
         load_page(0)
         load_w2(w2_early[1], 1, 0, 2 * P)
@@ -171,7 +172,8 @@ def tile_list_marathon_split_caps_kernel(
         def cast_last_w1(u, lo, hi):
             dst = w1_bf[1, 1].rearrange("p (t j i k) -> p t j i k", t=4, i=8, k=4)
             src = w1_last[u][:].rearrange("p k (j t i) -> p t j i k", t=4, i=8)
-            nc.vector.tensor_copy(dst[:, lo:hi, 8 * u : 8 * (u + 1)], src[:, lo:hi])
+            blocks = slice(last_cols[u][0] // 32, last_cols[u][1] // 32)
+            nc.vector.tensor_copy(dst[:, lo:hi, blocks], src[:, lo:hi])
 
         def quant_w1(a, g):
             for u in range(2):
@@ -306,6 +308,7 @@ def tile_list_marathon_split_caps_kernel(
             for a in (1, 0):
                 pass_b(1, 0, t, a, 4 + t, first=1)
             copy_b(b_exact[t][:], 1, t, 4 + t)
+        rounded_b(0, 1, 0, 4)
         for a, g in ag_pairs[:3]:
             cast_w1(a, g)
             quant_w1(a, g)
@@ -320,25 +323,25 @@ def tile_list_marathon_split_caps_kernel(
                 pass_a(1, 0, t, a, 4 + t)
         h_rows[0, 0] = arena[:, 0 : 4 * HALF].rearrange("p (t c) -> p t c", t=4)
         rounded_max(0, 0)
-        pool_weave(0, 0, EARLY_SHARE, HALF)
+        pool_weave(0, 0, 0, HALF)
         for t in range(4):
             nc.vector.scalar_tensor_tensor(
                 h_rows[1, 0][:, t, :], banks[4 + t][:], bias[:, t, 1:2], b_exact[t][:], ALU.add, ALU.max
             )
-        scalar_weave(0, 0, 0, EARLY_SHARE)
         for m in range(2):
             cast_early_w2(m, 0)
         scalar_weave(1, 0, 0, SHARE)
         pool_weave(1, 0, SHARE, HALF)
-        for t, bank in enumerate((0, 1, 2, 4)):
-            rounded_b(0, 1, t, bank)
-        for t, bank in enumerate((5, 6, 7, 4)):
+        for t in range(1, 4):
+            rounded_b(0, 1, t, t - 1)
+        for t, bank in enumerate((4, 5, 6, 7)):
             rounded_a(0, 1, t, bank)
         for s in range(2):
             picked[0, s] = sb(f"picked0{s}", [P, HALF], F32, tag=f"b_exact{2 + s}")
             gather(0, s)
         for m in range(2):
             cast_early_w2(m, 1)
+        h_codes[0, 0] = sb("h_codes00", [P, HALF], U32, tag="h_rows10")
         quant_h(0, 0)
         quant_h(1, 0)
         quant_w2(0)
@@ -353,11 +356,11 @@ def tile_list_marathon_split_caps_kernel(
         cap(0, 0, 3)
         scatter(0, 0)
         b_bf[1, 1] = shared.tile([P, 4, HALF], BF16, name="b_bf11", offset=0)
-        for t, bank in enumerate((5, 6, 7, 4)):
+        for t, bank in enumerate((4, 5, 6, 7)):
             rounded_b(1, 1, t, bank)
         third_product(1, 0, 0)
         a_bf[1, 1] = sb("a_bf11", [P, 4, HALF], BF16)
-        for t, bank in enumerate((5, 6, 7, 3)):
+        for t, bank in enumerate((4, 5, 6, 3)):
             rounded_a(1, 1, t, bank)
         rounded_max(1, 1)
         cast_late_w2()
@@ -376,7 +379,7 @@ def tile_list_marathon_split_caps_kernel(
         quant_h(1, 1)
         clip(2, 0)
         scatter_sum(2, 0)
-        for m, bank in ((1, 0), (0, 2), (2, 4)):
+        for m, bank in ((1, 0), (0, 2), (2, 7)):
             third_product(m, 1, bank)
         capped[0, 1] = sb("capped01", [P, HALF], F32, tag="room20")
         cap(0, 1, 2)
@@ -384,7 +387,7 @@ def tile_list_marathon_split_caps_kernel(
         gather_excess(1, 1)
         scatter(0, 1)
         store(0)
-        copy_ceiling(2, 1, 4)
+        copy_ceiling(2, 1, 7)
         gather_excess(2, 1)
         for m in (1, 2):
             clip(m, 1)

@@ -22,9 +22,8 @@ PASS = 512
 HALF = 512
 QUAD = 32
 SHIFT = 16
-FIRST = 8 * HALF
+FIRST = 18 * HALF
 TAIL = 192
-LAST_SHARE = 96
 SHARE = 192
 
 
@@ -65,10 +64,10 @@ def tile_list_marathon_split_caps_kernel(
         w1_bf[1, 1] = arena[:, 2 * PASS : 6 * PASS]
         w1_codes = {(a, g): sb(f"w1_codes{a}{g}", [P, PASS], U32) for a, g in ag_pairs}
         w1_sc = {(a, g): sb(f"w1_sc{a}{g}", [P, PASS], U8) for a, g in ag_pairs}
-        w2_early = [sb("w2_early0", [P, 4, 2 * P], F32), shared.tile([P, 4, 2 * P], F32, name="w2_early1", offset=0)]
-        w2_late = sb("w2_late", [P, 2, 4, P], F32)
+        w2_early = [sb("w2_early0", [P, 4, 2 * P], F32), sb("w2_early1", [P, 4, 2 * P], F32)]
+        w2_late = shared.tile([P, 2, 4, P], F32, name="w2_late", offset=4 * HALF)
         w2_bf = [shared.tile([P, 8 * P], BF16, name="w2_bf0", offset=FIRST + 2 * HALF, align_bytes=64)]
-        w2_bf.extend(sb(f"w2_bf{m}", [P, 16 * P], BF16) for m in (1, 2))
+        w2_bf.extend(sb(f"w2_bf{m}", [P, 8 * m * P], BF16) for m in (1, 2))
         w2_codes = sb("w2_codes", [P, 6 * P], U32)
         w2_sc = sb("w2_sc", [P, 6 * P], U8)
         page = [sb(f"page{m}", [P, T], F32) for m in range(3)]
@@ -79,12 +78,12 @@ def tile_list_marathon_split_caps_kernel(
         h_bf = {(g, 0): sb(f"h_bf{g}0", [P, 4 * HALF], BF16) for g in range(2)}
         h_codes = {(g, s): sb(f"h_codes{g}{s}", [P, HALF], U32) for g, s in gs_pairs if g == 1}
         h_sc = {(g, s): sb(f"h_sc{g}{s}", [P, HALF], U8) for g, s in gs_pairs}
-        fused = [(2, 0), (1, 1), (2, 1)]
-        ceiling = {u: sb(f"ceiling{u[0]}{u[1]}", [P, HALF], F32) for u in fused}
+        fused = [(1, 0), (2, 0), (1, 1), (2, 1)]
+        ceiling = {u: sb(f"ceiling{u[0]}{u[1]}", [P, HALF], F32) for u in fused[1:]}
         excess = {u: sb(f"excess{u[0]}{u[1]}", [P, HALF], F32) for u in fused}
-        room = {(2, 0): sb("room20", [P, HALF], F32)}
+        room = {(1, 0): sb("room10", [P, 2 * HALF], F32)}
         room[1, 1] = room[2, 1] = sb("room1", [P, HALF], F32)
-        picked, capped = {(1, 0): sb("picked10", [P, HALF], F32)}, {}
+        picked, capped = {}, {}
         banks = [psum.tile([P, HALF], F32, name=f"bank{b}") for b in range(8)]
 
         nc.sync.dma_start(offsets[:], offs)
@@ -141,12 +140,12 @@ def tile_list_marathon_split_caps_kernel(
         load_w2(w2_early[0], 0, 0, 2 * P)
         load_page(0)
         load_w2(w2_early[1], 1, 0, 2 * P)
-        load_page(1)
-        with nc.allow_non_contiguous_dma(reason="one bias value a partition and page"):
-            nc.sync.dma_start(b2_col[:], b2.rearrange("(m p) -> p m", p=P))
-        load_page(2)
         for g in range(2):
             load_w2(w2_late[:, g], g, 2 * P, N)
+        with nc.allow_non_contiguous_dma(reason="one bias value a partition and page"):
+            nc.sync.dma_start(b2_col[:], b2.rearrange("(m p) -> p m", p=P))
+        load_page(1)
+        load_page(2)
 
         nc.scalar.activation(
             bias_rows[0:4, :].rearrange("v (t j i) -> v t j i", t=4, i=8),
@@ -341,6 +340,7 @@ def tile_list_marathon_split_caps_kernel(
             gather(0, s)
         for m in range(2):
             cast_early_w2(m, 1)
+        cast_late_w2()
         h_codes[0, 0] = sb("h_codes00", [P, HALF], U32, tag="h_rows10")
         quant_h(0, 0)
         quant_h(1, 0)
@@ -349,39 +349,39 @@ def tile_list_marathon_split_caps_kernel(
         h_rows[0, 1] = shared.tile([P, 4, HALF], BF16, name="h_rows01", offset=FIRST + 4 * HALF)
         rounded_max(0, 1)
         quant_w2(1)
-        h_bf[0, 1] = sb("h_bf01", [P, 4 * HALF], BF16, tag="w2_bf1")
+        quant_w2(2)
+        h_bf[0, 1] = sb("h_bf01", [P, 4 * HALF], BF16, tag="w2_bf2")
         pool_weave(0, 1, 0, HALF)
-        gather(1, 0)
-        capped[0, 0] = sb("capped00", [P, HALF], F32)
+        capped[0, 0] = shared.tile([P, HALF], F32, name="capped00", offset=6 * HALF)
         cap(0, 0, 3)
         scatter(0, 0)
-        b_bf[1, 1] = shared.tile([P, 4, HALF], BF16, name="b_bf11", offset=0)
-        for t, bank in enumerate((4, 5, 6, 7)):
-            rounded_b(1, 1, t, bank)
+        b_bf[1, 1] = shared.tile([P, 4, HALF], BF16, name="b_bf11", offset=10 * HALF)
+        for t in range(4):
+            rounded_b(1, 1, t, 4 + t)
         third_product(1, 0, 0)
+        ceiling[1, 0] = shared.tile([P, HALF], F32, name="ceiling10", offset=2 * HALF)
+        copy_ceiling(1, 0, 0)
+        gather_excess(1, 0)
         a_bf[1, 1] = sb("a_bf11", [P, 4, HALF], BF16)
         for t, bank in enumerate((4, 5, 6, 3)):
             rounded_a(1, 1, t, bank)
-        rounded_max(1, 1)
-        cast_late_w2()
-        capped[1, 0] = sb("capped10", [P, HALF], F32, tag="w2_late")
-        cap(1, 0, 0)
-        quant_w2(2)
-        h_bf[1, 1] = sb("h_bf11", [P, 4 * HALF], BF16, tag="w2_bf2")
-        pool_weave(1, 1, LAST_SHARE, HALF)
-        scalar_weave(1, 1, 0, LAST_SHARE)
-        scatter(1, 0)
         third_product(2, 0, 1)
         copy_ceiling(2, 0, 1)
+        rounded_max(1, 1)
         gather_excess(2, 0)
-        h_codes[0, 1] = sb("h_codes01", [P, HALF], U32, tag="h_rows11")
+        clip(1, 0)
+        scatter_sum(1, 0)
+        h_bf[1, 1] = sb("h_bf11", [P, 4 * HALF], BF16, tag="room10")
+        scalar_weave(1, 1, 0, HALF)
+        h_codes[0, 1] = sb("h_codes01", [P, HALF], U32, tag="excess10")
         quant_h(0, 1)
         quant_h(1, 1)
+        room[2, 0] = sb("room20", [P, HALF], F32, tag="h_rows11")
         clip(2, 0)
         scatter_sum(2, 0)
         for m, bank in ((1, 0), (0, 2), (2, 7)):
             third_product(m, 1, bank)
-        capped[0, 1] = sb("capped01", [P, HALF], F32, tag="room20")
+        capped[0, 1] = sb("capped01", [P, HALF], F32, tag="h_rows11")
         cap(0, 1, 2)
         copy_ceiling(1, 1, 0)
         gather_excess(1, 1)

@@ -307,7 +307,8 @@ def tile_list_marathon_split_caps_kernel(
             for a in (1, 0):
                 pass_b(1, 0, t, a, 4 + t, first=1)
             copy_b(b_exact[t][:], 1, t, 4 + t)
-        rounded_b(0, 1, 0, 4)
+        for t in range(2):
+            rounded_b(0, 1, t, 4 + t)
         for a, g in ag_pairs[:3]:
             cast_w1(a, g)
             quant_w1(a, g)
@@ -331,9 +332,9 @@ def tile_list_marathon_split_caps_kernel(
             cast_early_w2(m, 0)
         scalar_weave(1, 0, 0, SHARE)
         pool_weave(1, 0, SHARE, HALF)
-        for t in range(1, 4):
-            rounded_b(0, 1, t, t - 1)
-        for t, bank in enumerate((4, 5, 6, 7)):
+        for t in range(2, 4):
+            rounded_b(0, 1, t, t - 2)
+        for t, bank in enumerate((2, 4, 5, 6)):
             rounded_a(0, 1, t, bank)
         for s in range(2):
             picked[0, s] = sb(f"picked0{s}", [P, HALF], F32, tag=f"b_exact{2 + s}")
@@ -356,14 +357,14 @@ def tile_list_marathon_split_caps_kernel(
         cap(0, 0, 3)
         scatter(0, 0)
         b_bf[1, 1] = shared.tile([P, 4, HALF], BF16, name="b_bf11", offset=10 * HALF)
-        for t in range(4):
-            rounded_b(1, 1, t, 4 + t)
+        for t, bank in enumerate((7, 4, 5, 6)):
+            rounded_b(1, 1, t, bank)
         third_product(1, 0, 0)
         ceiling[1, 0] = shared.tile([P, HALF], F32, name="ceiling10", offset=2 * HALF)
         copy_ceiling(1, 0, 0)
         gather_excess(1, 0)
         a_bf[1, 1] = sb("a_bf11", [P, 4, HALF], BF16)
-        for t, bank in enumerate((4, 5, 6, 3)):
+        for t, bank in enumerate((7, 4, 5, 3)):
             rounded_a(1, 1, t, bank)
         third_product(2, 0, 1)
         copy_ceiling(2, 0, 1)
@@ -379,7 +380,7 @@ def tile_list_marathon_split_caps_kernel(
         room[2, 0] = sb("room20", [P, HALF], F32, tag="h_rows11")
         clip(2, 0)
         scatter_sum(2, 0)
-        for m, bank in ((1, 0), (0, 2), (2, 7)):
+        for m, bank in ((1, 0), (0, 2), (2, 6)):
             third_product(m, 1, bank)
         capped[0, 1] = sb("capped01", [P, HALF], F32, tag="h_rows11")
         cap(0, 1, 2)
@@ -387,7 +388,7 @@ def tile_list_marathon_split_caps_kernel(
         gather_excess(1, 1)
         scatter(0, 1)
         store(0)
-        copy_ceiling(2, 1, 7)
+        copy_ceiling(2, 1, 6)
         gather_excess(2, 1)
         for m in (1, 2):
             clip(m, 1)

@@ -55,7 +55,7 @@ def tile_list_marathon_split_caps_kernel(
         w4_raw = [sb(f"w4_raw{g}", [P, 2 * H], U8) for g in range(2)]
         w4_codes = [sb(f"w4_codes{g}", [P, 2 * H], U8) for g in range(2)]
         tab_w = [sb(f"tab_w{a}", [P, T], U32) for a in range(2)]
-        v_words = {(a, s): sb(f"v_words{a}{s}", [P, HALF], U32) for a, s in ag_pairs}
+        v_words = {(a, s): sb(f"v_words{a}{s}", [P, HALF], U32) for a, s in ((0, 0), (1, 0), (1, 1))}
         w1_raw = {(a, g): sb(f"w1_raw{a}{g}", [P, 4, PASS], F32) for a, g in ag_pairs[:3]}
         last_cols = ((0, PASS - TAIL), (PASS - TAIL, PASS))
         w1_last = [sb(f"w1_last{u}", [P, 4, hi - lo], F32) for u, (lo, hi) in enumerate(last_cols)]
@@ -64,17 +64,17 @@ def tile_list_marathon_split_caps_kernel(
         w1_bf[1, 1] = arena[:, 2 * PASS : 6 * PASS]
         w1_codes = {(a, g): sb(f"w1_codes{a}{g}", [P, PASS], U32) for a, g in ag_pairs}
         w1_sc = {(a, g): sb(f"w1_sc{a}{g}", [P, PASS], U8) for a, g in ag_pairs}
-        w2_early = [sb("w2_early0", [P, 4, 2 * P], F32), sb("w2_early1", [P, 4, 2 * P], F32)]
+        w2_early = [sb(f"w2_early{g}", [P, 4, 2 * P], F32) for g in range(2)]
         w2_late = shared.tile([P, 2, 4, P], F32, name="w2_late", offset=4 * HALF)
-        w2_bf = [shared.tile([P, 8 * P], BF16, name="w2_bf0", offset=FIRST + 2 * HALF, align_bytes=64)]
-        w2_bf.extend(sb(f"w2_bf{m}", [P, 8 * m * P], BF16) for m in (1, 2))
+        w2_bf = [sb(f"w2_bf{m}", [P, (16 if m == 2 else 8) * P], BF16) for m in range(3)]
         w2_codes = sb("w2_codes", [P, 6 * P], U32)
         w2_sc = sb("w2_sc", [P, 6 * P], U8)
         page = [sb(f"page{m}", [P, T], F32) for m in range(3)]
         b_exact = [sb(f"b_exact{t}", [P, HALF], F32) for t in range(4)]
         a_bf = {(0, s): sb(f"a_bf0{s}", [P, 4, HALF], BF16) for s in range(2)}
         b_bf = {(0, s): sb(f"b_bf0{s}", [P, 4, HALF], BF16) for s in range(2)}
-        h_rows = {(1, s): sb(f"h_rows1{s}", [P, 4, HALF], BF16) for s in range(2)}
+        h_rows = {(1, 0): sb("h_rows10", [P, 4, HALF], BF16)}
+        h_rows[1, 1] = shared.tile([P, 4, HALF], BF16, name="h_rows11", offset=FIRST, align_bytes=64)
         h_bf = {(g, 0): sb(f"h_bf{g}0", [P, 4 * HALF], BF16) for g in range(2)}
         h_codes = {(g, s): sb(f"h_codes{g}{s}", [P, HALF], U32) for g, s in gs_pairs if g == 1}
         h_sc = {(g, s): sb(f"h_sc{g}{s}", [P, HALF], U8) for g, s in gs_pairs}
@@ -120,6 +120,7 @@ def tile_list_marathon_split_caps_kernel(
 
         tab_rows = tab_scales.bitcast(I32).rearrange("a (q r) c -> r q a c", r=4)
         nc.sync.dma_start(bias_raw[2:4, :], b4.rearrange("(g c) -> g c", g=2))
+        nc.sync.dma_start(bias_raw[0:2, :], b1.rearrange("(g c) -> g c", g=2))
         for r in range(4):
             nc.sync.dma_start(tab_sc[r:P:SHIFT, :].bitcast(I32), tab_rows[r])
         load_table(0)
@@ -128,7 +129,6 @@ def tile_list_marathon_split_caps_kernel(
         for r in range(4):
             nc.sync.dma_start(w4_sc_raw[r:P:QUAD, :].bitcast(I32).rearrange("q (a c) -> q a c", a=2), w4_rows[r])
         load_table(1)
-        nc.sync.dma_start(bias_raw[0:2, :], b1.rearrange("(g c) -> g c", g=2))
         load_w4(1)
         nc.vector.tensor_copy(v_sc[0][:], tab_sc[:].indirect(offsets[:]))
         for r in range(4):
@@ -223,8 +223,13 @@ def tile_list_marathon_split_caps_kernel(
                 pass_b(g, s, t, a, bank)
             copy_b(b_bf[g, s][:, t, :], g, t, bank)
 
-        def rounded_max(g, s):
-            nc.vector.tensor_tensor(h_rows[g, s][:], a_bf[g, s][:], b_bf[g, s][:], ALU.max)
+        def rounded_max(g, s, tiles=4):
+            nc.vector.tensor_tensor(h_rows[g, s][:, 0:tiles], a_bf[g, s][:, 0:tiles], b_bf[g, s][:, 0:tiles], ALU.max)
+
+        def bank_max(g, s, t, bank, b_values):
+            nc.vector.scalar_tensor_tensor(
+                h_rows[g, s][:, t, :], banks[bank][:], bias[:, t, g : g + 1], b_values, ALU.add, ALU.max
+            )
 
         def scalar_weave(g, s, lo, hi):
             nc.scalar.copy(
@@ -295,9 +300,9 @@ def tile_list_marathon_split_caps_kernel(
         order_w4_words(0)
         order_w4_scales()
         order_w4_words(1)
-        for a in range(2):
-            for s in range(2):
-                gather_words(a, s)
+        v_words[0, 1] = sb("v_words01", [P, HALF], U32, tag="w4_raw1")
+        for a, s in ((0, 0), (1, 0), (1, 1), (0, 1)):
+            gather_words(a, s)
         for a in range(2):
             for t in range(4):
                 pass_b(0, 0, t, a, t)
@@ -325,17 +330,17 @@ def tile_list_marathon_split_caps_kernel(
         rounded_max(0, 0)
         pool_weave(0, 0, 0, HALF)
         for t in range(4):
-            nc.vector.scalar_tensor_tensor(
-                h_rows[1, 0][:, t, :], banks[4 + t][:], bias[:, t, 1:2], b_exact[t][:], ALU.add, ALU.max
-            )
+            bank_max(1, 0, t, 4 + t, b_exact[t][:])
         for m in range(2):
             cast_early_w2(m, 0)
         scalar_weave(1, 0, 0, SHARE)
         pool_weave(1, 0, SHARE, HALF)
         for t in range(2, 4):
             rounded_b(0, 1, t, t - 2)
-        for t, bank in enumerate((2, 4, 5, 6)):
-            rounded_a(0, 1, t, bank)
+        for t in range(3):
+            rounded_a(0, 1, t, 4 + t)
+        for a in range(2):
+            pass_a(0, 1, 3, a, 7)
         for s in range(2):
             picked[0, s] = sb(f"picked0{s}", [P, HALF], F32, tag=f"b_exact{2 + s}")
             gather(0, s)
@@ -347,8 +352,9 @@ def tile_list_marathon_split_caps_kernel(
         quant_h(1, 0)
         quant_w2(0)
         third_product(0, 0, 3)
-        h_rows[0, 1] = shared.tile([P, 4, HALF], BF16, name="h_rows01", offset=FIRST + 4 * HALF)
-        rounded_max(0, 1)
+        h_rows[0, 1] = sb("h_rows01", [P, 4, HALF], BF16, tag="w2_early1")
+        rounded_max(0, 1, 3)
+        bank_max(0, 1, 3, 7, b_bf[0, 1][:, 3, :])
         quant_w2(1)
         quant_w2(2)
         h_bf[0, 1] = sb("h_bf01", [P, 4 * HALF], BF16, tag="w2_bf2")
@@ -357,14 +363,14 @@ def tile_list_marathon_split_caps_kernel(
         cap(0, 0, 3)
         scatter(0, 0)
         b_bf[1, 1] = shared.tile([P, 4, HALF], BF16, name="b_bf11", offset=10 * HALF)
-        for t, bank in enumerate((7, 4, 5, 6)):
+        for t, bank in enumerate((4, 5, 6, 7)):
             rounded_b(1, 1, t, bank)
         third_product(1, 0, 0)
         ceiling[1, 0] = shared.tile([P, HALF], F32, name="ceiling10", offset=2 * HALF)
         copy_ceiling(1, 0, 0)
         gather_excess(1, 0)
         a_bf[1, 1] = sb("a_bf11", [P, 4, HALF], BF16)
-        for t, bank in enumerate((7, 4, 5, 3)):
+        for t, bank in enumerate((4, 5, 6, 3)):
             rounded_a(1, 1, t, bank)
         third_product(2, 0, 1)
         copy_ceiling(2, 0, 1)
@@ -374,21 +380,21 @@ def tile_list_marathon_split_caps_kernel(
         scatter_sum(1, 0)
         h_bf[1, 1] = sb("h_bf11", [P, 4 * HALF], BF16, tag="room10")
         scalar_weave(1, 1, 0, HALF)
-        h_codes[0, 1] = sb("h_codes01", [P, HALF], U32, tag="excess10")
+        h_codes[0, 1] = shared.tile([P, HALF], U32, name="h_codes01", offset=FIRST, align_bytes=64)
         quant_h(0, 1)
         quant_h(1, 1)
-        room[2, 0] = sb("room20", [P, HALF], F32, tag="h_rows11")
+        room[2, 0] = shared.tile([P, HALF], F32, name="room20", offset=FIRST + 4 * HALF)
         clip(2, 0)
         scatter_sum(2, 0)
-        for m, bank in ((1, 0), (0, 2), (2, 6)):
+        for m, bank in ((1, 0), (0, 2), (2, 7)):
             third_product(m, 1, bank)
-        capped[0, 1] = sb("capped01", [P, HALF], F32, tag="h_rows11")
+        capped[0, 1] = shared.tile([P, HALF], F32, name="capped01", offset=FIRST + 4 * HALF)
         cap(0, 1, 2)
         copy_ceiling(1, 1, 0)
         gather_excess(1, 1)
         scatter(0, 1)
         store(0)
-        copy_ceiling(2, 1, 6)
+        copy_ceiling(2, 1, 7)
         gather_excess(2, 1)
         for m in (1, 2):
             clip(m, 1)

from contextlib import ExitStack

import concourse.mybir as mybir
from concourse.masks import make_identity

T, S, K, H, N = 2048, 1024, 1024, 1024, 384
FLOPS = 2 * S * (2 * K * H + H * N)

F32 = mybir.dt.float32
BF16 = mybir.dt.bfloat16
I32 = mybir.dt.int32
U32 = mybir.dt.uint32
U16 = mybir.dt.uint16
U8 = mybir.dt.uint8
FP8X4 = mybir.dt.float8_e4m3fn_x4
FP4X4 = mybir.dt.float4_e2m1fn_x4
ALU = mybir.AluOpType
ACT = mybir.ActivationFunctionType

P = 128
PASS = 512
HALF = 512
QUAD = 32
SHIFT = 16
FIRST = 18 * HALF
TAIL = 192
SHARE = 192


def tile_list_marathon_split_caps_kernel(
    tc, tab_words, tab_scales, offs, w1, b1, w4_words, w4_scales, b4, w2, b2, gT, out
):
    nc = tc.nc
    with ExitStack() as ctx:
        keep = ctx.enter_context(tc.tile_pool(name="keep", bufs=1))
        shared = ctx.enter_context(tc.tile_pool(name="shared", bufs=1))
        psum = ctx.enter_context(tc.psum_pool(name="psum", bufs=1))

        def sb(name, shape, dtype, tag=None):
            return keep.tile(shape, dtype, name=name, tag=tag or name, align_bytes=64)

        ag_pairs = [(a, g) for g in range(2) for a in range(2)]
        gs_pairs = [(g, s) for s in range(2) for g in range(2)]

        offsets = keep.tile([P, S // 16], U16, name="offsets")
        tab_sc = sb("tab_sc", [P, T], U8)
        v_sc = [sb(f"v_sc{a}", [P, S], U8) for a in range(2)]
        bias_rows = sb("bias_rows", [P, PASS], F32)
        bias_raw = sb("bias_raw", [4, PASS], F32)
        bias = sb("bias", [P, 4, 4], F32)
        b2_col = sb("b2_col", [P, 3], F32)
        ident = sb("ident", [P, P], F32)
        w4_sc_raw = sb("w4_sc_raw", [P, 2 * H], U8)
        w4_sc = sb("w4_sc", [P, 2 * H], U8)
        w4_raw = [sb(f"w4_raw{g}", [P, 2 * H], U8) for g in range(2)]
        w4_codes = [sb(f"w4_codes{g}", [P, 2 * H], U8) for g in range(2)]
        tab_w = [sb(f"tab_w{a}", [P, T], U32) for a in range(2)]
        v_words = {(a, s): sb(f"v_words{a}{s}", [P, HALF], U32) for a, s in ((0, 0), (1, 0), (1, 1))}
        w1_raw = {(a, g): sb(f"w1_raw{a}{g}", [P, 4, PASS], F32) for a, g in ag_pairs[:3]}
        last_cols = ((0, PASS - TAIL), (PASS - TAIL, PASS))
        w1_last = [sb(f"w1_last{u}", [P, 4, hi - lo], F32) for u, (lo, hi) in enumerate(last_cols)]
        w1_bf = {(a, g): sb(f"w1_bf{a}{g}", [P, 4 * PASS], BF16) for a, g in ag_pairs[:3]}
        arena = sb("arena", [P, 6 * PASS], BF16)
        w1_bf[1, 1] = arena[:, 2 * PASS : 6 * PASS]
        w1_codes = {(a, g): sb(f"w1_codes{a}{g}", [P, PASS], U32) for a, g in ag_pairs}
        w1_sc = {(a, g): sb(f"w1_sc{a}{g}", [P, PASS], U8) for a, g in ag_pairs}
        w2_early = [sb(f"w2_early{g}", [P, 4, 2 * P], F32) for g in range(2)]
        w2_late = shared.tile([P, 2, 4, P], F32, name="w2_late", offset=4 * HALF)
        w2_bf = [sb(f"w2_bf{m}", [P, (16 if m == 2 else 8) * P], BF16) for m in range(3)]
        w2_codes = sb("w2_codes", [P, 6 * P], U32)
        w2_sc = sb("w2_sc", [P, 6 * P], U8)
        page = [sb(f"page{m}", [P, T], F32) for m in range(3)]
        b_exact = [sb(f"b_exact{t}", [P, HALF], F32) for t in range(4)]
        a_bf = {(0, s): sb(f"a_bf0{s}", [P, 4, HALF], BF16) for s in range(2)}
        b_bf = {(0, s): sb(f"b_bf0{s}", [P, 4, HALF], BF16) for s in range(2)}
        h_rows = {(1, 0): sb("h_rows10", [P, 4, HALF], BF16)}
        h_rows[1, 1] = shared.tile([P, 4, HALF], BF16, name="h_rows11", offset=FIRST, align_bytes=64)
        h_bf = {(g, 0): sb(f"h_bf{g}0", [P, 4 * HALF], BF16) for g in range(2)}
        h_codes = {(g, s): sb(f"h_codes{g}{s}", [P, HALF], U32) for g, s in gs_pairs if g == 1}
        h_sc = {(g, s): sb(f"h_sc{g}{s}", [P, HALF], U8) for g, s in gs_pairs}
        fused = [(1, 0), (2, 0), (1, 1), (2, 1)]
        ceiling = {u: sb(f"ceiling{u[0]}{u[1]}", [P, HALF], F32) for u in fused[1:]}
        excess = {u: sb(f"excess{u[0]}{u[1]}", [P, HALF], F32) for u in fused}
        room = {(1, 0): sb("room10", [P, 2 * HALF], F32)}
        room[1, 1] = room[2, 1] = sb("room1", [P, HALF], F32)
        picked, capped = {}, {}
        banks = [psum.tile([P, HALF], F32, name=f"bank{b}") for b in range(8)]

        nc.sync.dma_start(offsets[:], offs)
        nc.gpsimd.memset(tab_sc[:].bitcast(I32), 0)
        nc.vector.memset(bias_rows[:, 0:P], 0.0)
        nc.scalar.activation(
            bias_rows[:, P:PASS].rearrange("p (t c) -> p t c", t=3),
            bias_rows[:, 0:P].unsqueeze(1).to_broadcast([P, 3, P]),
            ACT.Identity,
        )
        nc.vector.memset(w4_sc_raw[:].bitcast(I32), 0)
        nc.vector.memset(v_sc[1][:].bitcast(I32), 0)
        make_identity(nc, ident[:])

        def load_table(a):
            nc.sync.dma_start(tab_w[a][:].bitcast(I32), tab_words[a].rearrange("p t i -> p (t i)").bitcast(I32))

        def load_w1(dst, a, lo, hi):
            nc.sync.dma_start(dst[:], w1[PASS * a : PASS * (a + 1), lo:hi].rearrange("(p j) c -> p j c", j=4))

        def load_w4(g):
            nc.sync.dma_start(
                w4_raw[g][:].bitcast(I32).rearrange("p (a c) -> p a c", a=2),
                w4_words[:, :, H * g : H * (g + 1)].bitcast(I32).rearrange("a p c -> p a c"),
            )

        def load_page(m):
            nc.sync.dma_start(page[m][:], gT[P * m : P * (m + 1), :])

        def load_w2(dst, g, lo, hi):
            rows = w2[PASS * g : PASS * (g + 1), lo:hi].rearrange("(j t i) n -> t j i n", t=4, i=8)
            for t in range(4):
                nc.sync.dma_start(dst[:, t, :], rows[t])

        tab_rows = tab_scales.bitcast(I32).rearrange("a (q r) c -> r q a c", r=4)
        nc.sync.dma_start(bias_raw[2:4, :], b4.rearrange("(g c) -> g c", g=2))
        nc.sync.dma_start(bias_raw[0:2, :], b1.rearrange("(g c) -> g c", g=2))
        for r in range(4):
            nc.sync.dma_start(tab_sc[r:P:SHIFT, :].bitcast(I32), tab_rows[r])
        load_table(0)
        load_w4(0)
        w4_rows = w4_scales.bitcast(I32).rearrange("a (q r) c -> r q a c", r=4)
        for r in range(4):
            nc.sync.dma_start(w4_sc_raw[r:P:QUAD, :].bitcast(I32).rearrange("q (a c) -> q a c", a=2), w4_rows[r])
        load_table(1)
        load_w4(1)
        nc.vector.tensor_copy(v_sc[0][:], tab_sc[:].indirect(offsets[:]))
        for r in range(4):
            nc.sync.dma_start(v_sc[1][r:P:QUAD, :].bitcast(I32), v_sc[0][SHIFT + r : P : QUAD, :].bitcast(I32))
        for a, g in ag_pairs[:3]:
            load_w1(w1_raw[a, g], a, PASS * g, PASS * (g + 1))
        for u, (lo, hi) in enumerate(last_cols):
            load_w1(w1_last[u], 1, PASS + lo, PASS + hi)
        load_w2(w2_early[0], 0, 0, 2 * P)
        load_page(0)
        load_w2(w2_early[1], 1, 0, 2 * P)
        for g in range(2):
            load_w2(w2_late[:, g], g, 2 * P, N)
        with nc.allow_non_contiguous_dma(reason="one bias value a partition and page"):
            nc.sync.dma_start(b2_col[:], b2.rearrange("(m p) -> p m", p=P))
        load_page(1)
        load_page(2)

        nc.scalar.activation(
            bias_rows[0:4, :].rearrange("v (t j i) -> v t j i", t=4, i=8),
            bias_raw[0:4, :].rearrange("v (j t i) -> v t j i", t=4, i=8),
            ACT.Identity,
        )
        for t in range(4):
            nc.tensor.transpose(banks[7][:, P * t : P * (t + 1)], bias_rows[:, P * t : P * (t + 1)], ident[:])
        nc.scalar.copy(bias[:], banks[7][:].rearrange("p (t c) -> p t c", t=4)[:, :, 0:4])

        def half_list(s):
            return offsets[:, HALF // 16 * s : HALF // 16 * (s + 1)]

        def gather_words(a, s):
            nc.vector.tensor_copy(v_words[a, s][:], tab_w[a][:].indirect(half_list(s)))

        def cast_w1(a, g):
            dst = w1_bf[a, g][:].rearrange("p (t j i k) -> p t j i k", t=4, i=8, k=4)
            src = w1_raw[a, g][:].rearrange("p k (j t i) -> p t j i k", t=4, i=8)
            for u in range(2):
                nc.vector.tensor_copy(dst[:, 2 * u : 2 * u + 2], src[:, 2 * u : 2 * u + 2])

        def cast_last_w1(u, lo, hi):
            dst = w1_bf[1, 1].rearrange("p (t j i k) -> p t j i k", t=4, i=8, k=4)
            src = w1_last[u][:].rearrange("p k (j t i) -> p t j i k", t=4, i=8)
            blocks = slice(last_cols[u][0] // 32, last_cols[u][1] // 32)
            nc.vector.tensor_copy(dst[:, lo:hi, blocks], src[:, lo:hi])

        def quant_w1(a, g):
            for u in range(2):
                cols = slice(2 * P * u, 2 * P * (u + 1))
                values = w1_bf[a, g][:, 8 * P * u : 8 * P * (u + 1)]
                nc.vector.quantize_mx(w1_codes[a, g][:, cols].bitcast(FP8X4), w1_sc[a, g][:, cols], values)

        def order_w4_scales():
            nc.scalar.copy(
                w4_sc[:].bitcast(U32).rearrange("p (u t j e) -> p u t j e", t=4, j=16, e=2),
                w4_sc_raw[:].bitcast(U32).rearrange("p (u j t e) -> p u t j e", t=4, j=16, e=2),
            )

        def order_w4_words(g):
            nc.scalar.copy(
                w4_codes[g][:].bitcast(U32).rearrange("p (a t j e) -> p a t j e", t=4, j=16, e=4),
                w4_raw[g][:].bitcast(U32).rearrange("p (a j t e) -> p a t j e", t=4, j=16, e=4),
            )

        def pass_b(g, s, t, a, bank, first=0):
            col0 = H * a + PASS * g + P * t
            nc.tensor.matmul_mx(
                banks[bank][:], w4_codes[g][:, 2 * (PASS * a + P * t) : 2 * (PASS * a + P * (t + 1))].bitcast(FP4X4),
                w4_sc[:, col0 : col0 + P], v_words[a, s][:].bitcast(FP8X4), v_sc[a][:, HALF * s : HALF * (s + 1)],
                start=(a == first), stop=(a != first),
            )

        def pass_a(g, s, t, a, bank):
            cols = slice(P * t, P * (t + 1))
            nc.tensor.matmul_mx(
                banks[bank][:], w1_codes[a, g][:, cols].bitcast(FP8X4), w1_sc[a, g][:, cols],
                v_words[a, s][:].bitcast(FP8X4), v_sc[a][:, HALF * s : HALF * (s + 1)], start=(a == 0), stop=(a == 1),
            )

        def copy_a(dst, g, t, bank):
            nc.scalar.activation(dst, banks[bank][:], ACT.Identity, bias=bias[:, t, g : g + 1])

        def copy_b(dst, g, t, bank):
            nc.scalar.activation(dst, banks[bank][:], ACT.Identity, bias=bias[:, t, 2 + g : 3 + g])

        def rounded_a(g, s, t, bank):
            for a in range(2):
                pass_a(g, s, t, a, bank)
            copy_a(a_bf[g, s][:, t, :], g, t, bank)

        def rounded_b(g, s, t, bank):
            for a in range(2):
                pass_b(g, s, t, a, bank)
            copy_b(b_bf[g, s][:, t, :], g, t, bank)

        def rounded_max(g, s, tiles=4):
            nc.vector.tensor_tensor(h_rows[g, s][:, 0:tiles], a_bf[g, s][:, 0:tiles], b_bf[g, s][:, 0:tiles], ALU.max)

        def bank_max(g, s, t, bank, b_values):
            nc.vector.scalar_tensor_tensor(
                h_rows[g, s][:, t, :], banks[bank][:], bias[:, t, g : g + 1], b_values, ALU.add, ALU.max
            )

        def scalar_weave(g, s, lo, hi):
            nc.scalar.copy(
                h_bf[g, s][:, 4 * lo : 4 * hi].rearrange("p (c i t) -> p c t i", i=4, t=4),
                h_rows[g, s][:, :, lo:hi].rearrange("p t (c i) -> p c t i", i=4),
            )

        def pool_weave(g, s, lo, hi):
            nc.gpsimd.tensor_scalar(
                h_bf[g, s][:, 4 * lo : 4 * hi].rearrange("p (c t) -> p c t", t=4),
                h_rows[g, s][:, :, lo:hi].rearrange("p t c -> p c t"), 1.0, 0.0, ALU.mult, ALU.add,
            )

        def quant_h(g, s):
            nc.vector.quantize_mx(h_codes[g, s][:].bitcast(FP8X4), h_sc[g, s][:], h_bf[g, s][:])

        def cast_early_w2(m, g):
            nc.scalar.copy(
                w2_bf[m][:, 4 * P * g : 4 * P * (g + 1)].rearrange("p (c i t) -> p c t i", i=4, t=4),
                w2_early[g][:, :, P * m : P * (m + 1)].rearrange("p t (c i) -> p c t i", i=4),
            )

        def cast_late_w2():
            nc.scalar.copy(
                w2_bf[2][:, 0 : 8 * P].rearrange("p (g c i t) -> p g c t i", g=2, i=4, t=4),
                w2_late[:].rearrange("p g t (c i) -> p g c t i", i=4),
            )

        def quant_w2(m):
            cols = slice(2 * P * m, 2 * P * (m + 1))
            nc.vector.quantize_mx(w2_codes[:, cols].bitcast(FP8X4), w2_sc[:, cols], w2_bf[m][:, 0 : 8 * P])

        def third_product(m, s, bank):
            for g in range(2):
                cols = slice(P * (2 * m + g), P * (2 * m + g + 1))
                nc.tensor.matmul_mx(
                    banks[bank][:], w2_codes[:, cols].bitcast(FP8X4), w2_sc[:, cols],
                    h_codes[g, s][:].bitcast(FP8X4), h_sc[g, s][:], start=(g == 0), stop=(g == 1),
                )

        def gather(m, s):
            nc.vector.tensor_copy(picked[m, s][:], page[m][:].indirect(half_list(s)))

        def cap(m, s, bank):
            nc.vector.scalar_tensor_tensor(
                capped[m, s][:], banks[bank][:], b2_col[:, m : m + 1], picked[m, s][:], ALU.add, ALU.min
            )

        def scatter(m, s):
            nc.vector.tensor_copy(page[m][:].indirect(half_list(s)), capped[m, s][:])

        def copy_ceiling(m, s, bank):
            nc.scalar.activation(ceiling[m, s][:], banks[bank][:], ACT.Identity, bias=b2_col[:, m : m + 1])

        def gather_excess(m, s):
            nc.vector.tensor_tensor(excess[m, s][:], page[m][:].indirect(half_list(s)), ceiling[m, s][:], ALU.subtract)

        def clip(m, s):
            nc.scalar.activation(room[m, s][:, 0:HALF], excess[m, s][:], ACT.Relu, scale=-1.0)
            nc.scalar.activation(excess[m, s][:], room[m, s][:, 0:HALF], ACT.Identity, scale=-1.0)

        def scatter_sum(m, s):
            nc.vector.tensor_tensor(page[m][:].indirect(half_list(s)), ceiling[m, s][:], excess[m, s][:], ALU.add)

        def store(m):
            nc.sync.dma_start(out[P * m : P * (m + 1), :], page[m][:])

        order_w4_words(0)
        order_w4_scales()
        order_w4_words(1)
        v_words[0, 1] = sb("v_words01", [P, HALF], U32, tag="w4_raw1")
        for a, s in ((0, 0), (1, 0), (1, 1), (0, 1)):
            gather_words(a, s)
        for a in range(2):
            for t in range(4):
                pass_b(0, 0, t, a, t)
        for t in range(4):
            copy_b(b_bf[0, 0][:, t, :], 0, t, t)
        for t in range(4):
            for a in (1, 0):
                pass_b(1, 0, t, a, 4 + t, first=1)
            copy_b(b_exact[t][:], 1, t, 4 + t)
        for t in range(2):
            rounded_b(0, 1, t, 4 + t)
        for a, g in ag_pairs[:3]:
            cast_w1(a, g)
            quant_w1(a, g)
        cast_last_w1(0, 0, 4)
        cast_last_w1(1, 0, 2)
        cast_last_w1(1, 2, 4)
        quant_w1(1, 1)
        for t in range(4):
            rounded_a(0, 0, t, t)
        for a in range(2):
            for t in range(4):
                pass_a(1, 0, t, a, 4 + t)
        h_rows[0, 0] = arena[:, 0 : 4 * HALF].rearrange("p (t c) -> p t c", t=4)
        rounded_max(0, 0)
        pool_weave(0, 0, 0, HALF)
        for t in range(4):
            bank_max(1, 0, t, 4 + t, b_exact[t][:])
        for m in range(2):
            cast_early_w2(m, 0)
        scalar_weave(1, 0, 0, SHARE)
        pool_weave(1, 0, SHARE, HALF)
        for t in range(2, 4):
            rounded_b(0, 1, t, t - 2)
        for t in range(3):
            rounded_a(0, 1, t, 4 + t)
        for a in range(2):
            pass_a(0, 1, 3, a, 7)
        for s in range(2):
            picked[0, s] = sb(f"picked0{s}", [P, HALF], F32, tag=f"b_exact{2 + s}")
            gather(0, s)
        for m in range(2):
            cast_early_w2(m, 1)
        cast_late_w2()
        h_codes[0, 0] = sb("h_codes00", [P, HALF], U32, tag="h_rows10")
        quant_h(0, 0)
        quant_h(1, 0)
        quant_w2(0)
        third_product(0, 0, 3)
        h_rows[0, 1] = sb("h_rows01", [P, 4, HALF], BF16, tag="w2_early1")
        rounded_max(0, 1, 3)
        bank_max(0, 1, 3, 7, b_bf[0, 1][:, 3, :])
        quant_w2(1)
        quant_w2(2)
        h_bf[0, 1] = sb("h_bf01", [P, 4 * HALF], BF16, tag="w2_bf2")
        pool_weave(0, 1, 0, HALF)
        capped[0, 0] = shared.tile([P, HALF], F32, name="capped00", offset=6 * HALF)
        cap(0, 0, 3)
        scatter(0, 0)
        b_bf[1, 1] = shared.tile([P, 4, HALF], BF16, name="b_bf11", offset=10 * HALF)
        for t, bank in enumerate((4, 5, 6, 7)):
            rounded_b(1, 1, t, bank)
        third_product(1, 0, 0)
        ceiling[1, 0] = shared.tile([P, HALF], F32, name="ceiling10", offset=2 * HALF)
        copy_ceiling(1, 0, 0)
        gather_excess(1, 0)
        a_bf[1, 1] = sb("a_bf11", [P, 4, HALF], BF16)
        for t, bank in enumerate((4, 5, 6, 3)):
            rounded_a(1, 1, t, bank)
        third_product(2, 0, 1)
        copy_ceiling(2, 0, 1)
        rounded_max(1, 1)
        gather_excess(2, 0)
        clip(1, 0)
        scatter_sum(1, 0)
        h_bf[1, 1] = sb("h_bf11", [P, 4 * HALF], BF16, tag="room10")
        scalar_weave(1, 1, 0, HALF)
        h_codes[0, 1] = shared.tile([P, HALF], U32, name="h_codes01", offset=FIRST, align_bytes=64)
        quant_h(0, 1)
        quant_h(1, 1)
        room[2, 0] = shared.tile([P, HALF], F32, name="room20", offset=FIRST + 4 * HALF)
        clip(2, 0)
        scatter_sum(2, 0)
        for m, bank in ((1, 0), (0, 2), (2, 7)):
            third_product(m, 1, bank)
        capped[0, 1] = shared.tile([P, HALF], F32, name="capped01", offset=FIRST + 4 * HALF)
        cap(0, 1, 2)
        copy_ceiling(1, 1, 0)
        gather_excess(1, 1)
        scatter(0, 1)
        store(0)
        copy_ceiling(2, 1, 7)
        gather_excess(2, 1)
        for m in (1, 2):
            clip(m, 1)
            scatter_sum(m, 1)
            store(m)
